import numpy as np, ml_dtypes
CORES = [242,247,114,119]
N = 4
BF = ml_dtypes.bfloat16
S, L, RO, WEAR = 2176, 256, 3, 8
def near(rng, home, h):
    q = S // 16
    return np.take_along_axis(np.broadcast_to(home, (N, 8, S)), h * q + rng.integers(0, q, h.shape), 2)
def parts(rng):
    home = np.argsort(rng.random((8, S)), axis=1); hab = np.zeros((8, S), np.int64)
    np.put_along_axis(hab, home, np.broadcast_to(np.arange(S) // (S // 16), (8, S)), 1)
    base = rng.integers(0, 256, (N, 8, 16, 16))
    x = np.clip(np.take_along_axis(base, hab[None, :, None, :], 3) + rng.integers(-60, 61, (N, 8, 16, S)), 0, 255)
    lab = np.argsort(rng.random((N, 8, L)), axis=2); inv = np.argsort(lab, axis=2)
    h = np.broadcast_to((lab % 16)[:, :, None, :], (N, 8, 16, L)).reshape(N, 8, 16 * L)
    m = np.where(rng.random(h.shape) < 0.75, near(rng, home, h), rng.integers(0, S, h.shape)).reshape(N, 8, 16, L)
    h = np.broadcast_to(hab[None, :, None, :], (N, 8, 16, S)).reshape(N, 8, 16 * S)
    nb = np.where(rng.random(h.shape) < 0.6, near(rng, home, h), rng.integers(0, S, h.shape)).reshape(N, 8, 16, S)
    v = hab[None] + 16 * rng.integers(0, L // 16, (N, 8, S))
    own = np.where(rng.random((N, 8, S)) < 0.6, np.take_along_axis(inv, v, 2), rng.integers(0, L, (N, 8, S)))
    return x, nb, m, own, rng.integers(600, 1100, (N, 8))
def pack(x, nb, m, own, th):
    return {"x0": x.reshape(N, 128, S).astype(np.float32).astype(BF), "nb": nb.reshape(N, 128, S).astype(np.int32), "m0": m.reshape(N, 128, L).astype(np.int32),
            "own0": own.reshape(N, 8, S).astype(np.int32), "th": th.reshape(N, 8, 1).astype(np.int32)}
def setup_inputs(rng):
    return pack(*parts(rng))
def setup_inputs_ties(rng):
    x, nb, m, own, th = parts(rng); step = rng.choice(np.array([1, 5, 40]), (N, 8, 1, 1))
    lo = ((256 - 3 * step) * rng.random((N, 8, 1, 1)) * (rng.random((N, 8, 1, 1)) < 0.7)).astype(np.int64)
    x = lo + step * rng.integers(0, 4, x.shape)
    pool = rng.integers(0, S, (N, 8, 3, L)); few = np.take_along_axis(pool, rng.integers(0, 3, m.shape), 2)
    m = np.where(rng.random((N, 8, 1, L)) < 0.7, few, rng.integers(0, S, m.shape))
    th = step[:, :, 0, 0] * rng.integers(14, 19, (N, 8))
    z = int(rng.integers(0, 8)); o = rng.permutation(S); cold, warm = o[:S // 2], o[S // 2:]; h = rng.integers(140, 250, N)
    is_cold = np.zeros(S, bool); is_cold[cold] = True
    x[:, z] = np.where(is_cold, 0, h[:, None, None]) + rng.integers(0, 2, (N, 16, S))
    three = cold[rng.integers(0, S // 2, (N, 3, L))]; m[:, z] = np.take_along_axis(three, rng.integers(0, 3, (N, 16, L)), 1)
    nb[:, z] = warm[rng.integers(0, S - S // 2, (N, 16, S))]; th[:, z] = 16 * h + rng.integers(3, 9, N)
    return pack(x, nb, m, own, th)
def setup_inputs_corners(rng):
    x, nb, m, own, th = parts(rng); K = S // L; ev = (K + 1) // 2; od = K // 2
    q = int(rng.integers(0, N)); p = (q - 1) % N; u = (q - 2) % N; la = np.arange(L); st = np.arange(S)
    turn = [rng.permutation(8) for r in range(N)]; turn[u] = turn[p]
    for r in range(N):
        for i, g in enumerate(turn[r]):
            if i == 0: own[r, g] = int(rng.choice(np.array([0, L - 1, L // 2])))
            if i == 1:
                own[r, g] = rng.permutation(L)[st % L]; m[r, g] = la + L * rng.integers(0, K, (16, L))
            if i == 2: m[r, g] = rng.choice(np.array([0, S - 1, int(rng.integers(0, S))]), (1, L))
            if i == 3: nb[r, g] = st[None, :]
            if i == 4: nb[r, g] = (S - 1) * rng.integers(0, 2, (1, S))
            if i == 5:
                th[r, g] = 0; x[r, g] = rng.integers(0, WEAR + 2, (16, S))
            if i == 6:
                th[r, g] = 4080; own[r, g] = (L - 1) * rng.integers(0, 2, S); m[r, g] = (S - 1) * rng.integers(0, 2, (16, L))
            if i == 7: x[r, g] = int(rng.choice(np.array([0, 7, 255])))
    x[q] = np.where((st // L) % 2 == 0, rng.integers(0, 9, (8, 16, S)), 255 - rng.integers(0, 9, (8, 16, S)))
    x[q] = np.where(st // L == 1, rng.integers(18, 21, (8, 16, S)), x[q])
    nb[q] = rng.integers(0, L, (8, 16, S)) + 2 * L * rng.integers(0, ev, (8, 16, S)); th[q] = 200
    own[q] = np.argsort(rng.random((8, L)), axis=1)[:, st % L]
    m[q] = la + L * (2 * rng.integers(1, od, (8, 16, L)) + 1); m[p] = la + 2 * L * rng.integers(0, ev, (8, 16, L))
    m[u, int(turn[u][0])] = L + la
    return pack(x, nb, m, own, th)
def setup_inputs_ends(rng):
    home = 1 + np.argsort(rng.random((8, S - 3)), axis=1)[:, :L]; homes = np.broadcast_to(home, (N, 8, L))
    c = rng.choice(np.array([0, 1, 8, 15, 16]), (N, 8)); c[0, 0] = 0; c[0, 1] = 16; c[N - 1] = rng.choice(np.array([1, 8, 15]), 8)
    x = 255 * rng.integers(0, 2, (N, 8, 16, S))
    x[..., 0] = 255 * (np.argsort(rng.random((N, 8, 16)), axis=2) < c[:, :, None]); x[..., S - 1] = 255 - x[..., 0]; x[..., S - 2] = 255
    np.put_along_axis(x, np.broadcast_to(home[None, :, None, :], (N, 8, 16, L)), 0, 3)
    nb = (S - 1) * rng.integers(0, 2, (N, 8, 16, S))
    nb = np.where(rng.random(nb.shape) < 0.15, np.take_along_axis(homes, rng.integers(0, L, (N, 8, 16 * S)), 2).reshape(nb.shape), nb)
    side = rng.integers(0, 2, (N, 8, S)); nb[:, :, 15] = (S - 1) * side; nb[:, :, 0] = (S - 1) * (1 - side)
    sig = np.argsort(rng.random((N, 8, L)), axis=2); own = (L - 1) * rng.integers(0, 2, (N, 8, S)); np.put_along_axis(own, homes, sig, 2)
    mix = (S - 1) * rng.integers(0, 2, (N, 8, 16, L)); kind = rng.choice(np.array([0, 1, 2, 3, 3, 3]), (N, 8, 1, L)); kind[N - 2] = 3; kind[N - 1] = rng.integers(0, 2, (8, 1, L))
    place = np.argsort(rng.random((N, 8, 16, L)), axis=2); place[:, :, :, L - 1] = np.array([2, 3, 4, 5, 6, 7, 8, 9, 10, 11, 12, 13, 14, 15, 0, 1])
    two = rng.random((N, 8, 1, L)) < 0.5; two[..., L - 1] = True
    far = np.where((place == 1) | ((place == 2) & two), S - 2, mix)
    keep = np.where((place == 0) | ((place == 3) & two), home[None, :, None, :], far)
    m = np.where(kind == 0, 0, np.where(kind == 1, S - 1, np.where(kind == 2, mix, keep)))
    th = 4080 * rng.integers(0, 2, (N, 8)); th[:, 2] = 0; th[:, 7] = 4080
    i = int(rng.integers(0, 7)); th[N - 1] = 4080; th[N - 1, i] = 0
    g = (i + 1 + int(rng.integers(0, 6))) % 7; a = int(rng.integers(0, L)); nb[N - 1, g, :, home[g, a]] = m[N - 1, g, 0, sig[N - 1, g, a]]
    return pack(x, nb, m, own, th)
def setup_inputs_spread(rng):
    x, nb, m, own, th = parts(rng)
    x = np.minimum(np.exp2(8 * rng.random((N, 8, 1, S))) * rng.random((N, 8, 16, S)) * 1.25, 255.0).astype(np.int64) * (rng.random((N, 8, 1, S)) > 0.0625)
    m = np.minimum((S * rng.random((N, 8, 16, L)) ** (1 + 3 * rng.random((N, 8, 1, L)))).astype(np.int64), S - 1)
    m = np.where(rng.random((N, 8, 1, L)) < 0.5, m, S - 1 - m)
    u = np.minimum((S * rng.random((N, 4, 16, S)) ** 2).astype(np.int64), S - 1); nb[:, 1::2] = u
    own = np.minimum((L * rng.random((N, 8, S)) ** 2).astype(np.int64), L - 1)
    return pack(x, nb, m, own, np.exp2(8 + 3 * rng.random((N, 8))).astype(np.int64))
def check_inputs(d):
    bad = []
    for k, lo, hi in (("x0", 0, 255), ("nb", 0, S - 1), ("m0", 0, S - 1), ("own0", 0, L - 1), ("th", 0, 4080)):
        try:
            v = np.asarray(d[k]).astype(np.float32).astype(np.float64)
            if not np.all((v >= lo) & (v <= hi)): bad.append("range of " + k)
            elif not np.all(v == np.floor(v)): bad.append("whole numbers of " + k)
        except Exception:
            bad.append("form of " + k)
    return bad
def centre(x, m):
    v = np.take_along_axis(x, m.reshape(8, 1, 16 * L), 2).reshape(8, 16, 16, L)
    c = (np.max(v, axis=2) + np.min(v, axis=2)) >> 1
    d = np.add.reduce(np.abs(v - c[:, :, None, :]), axis=1)
    return c, np.argmin(d, axis=1), np.argmax(d, axis=1)
def reference(x0, nb, m0, own0, th):
    X = x0.astype(np.float32).astype(np.int32).reshape(N, 8, 16, S); nbs = nb.astype(np.int64).reshape(N, 8, 16, S)
    M = m0.astype(np.int64).reshape(N, 8, 16, L); O = own0.astype(np.int64).reshape(N, 8, S); T = th.astype(np.int64).reshape(N, 8)
    wins = np.zeros(N, np.int64); lane = np.broadcast_to(np.arange(L), (8, L)); grp = np.broadcast_to(np.arange(8)[:, None], (8, L))
    for t in range(RO):
        res, back = [], []; now = np.zeros(N, np.int64)
        for q in range(N):
            p = (q - 1 - t % (N - 1)) % N
            ci, ki, fi = centre(X[q], M[p]); cr, kr, fr = centre(X[q], M[q])
            s = np.take_along_axis(M[p], ki[:, None, :], 1)[:, 0]
            b = np.take_along_axis(O[q], s, 1)
            low = np.full((8, L), L); np.minimum.at(low, (grp, b), lane)
            fight = np.take_along_axis(low, b, 1) == lane
            n = np.take_along_axis(nbs[q], s[:, None, :], 2)
            v = np.take_along_axis(X[q], n.reshape(8, 1, 16 * L), 2).reshape(8, 16, 16, L)
            ei = np.add.reduce(np.abs(v - ci[:, :, None, :]), axis=1)
            er = np.add.reduce(np.abs(v - np.take_along_axis(cr, b[:, None, :], 2)[:, :, None, :]), axis=1)
            lim = T[q][:, None, None] + (wins[q] & 63)
            won = np.count_nonzero(ei < lim, axis=1) > np.count_nonzero(er < lim, axis=1)
            e = np.where(won[:, None, :], ei, er)
            best = np.take_along_axis(n, np.argmin(e, axis=1)[:, None, :], 1)[:, 0]
            worst = np.take_along_axis(n, np.argmax(e, axis=1)[:, None, :], 1)[:, 0]
            g, a = np.nonzero(fight); w = won[g, a]; bb = b[g, a]; ss = s[g, a]
            res.append((q, g, fr[g, bb], bb, np.where(w, worst[g, a], best[g, a])))
            back.append((p, g, np.where(w, fi[g, a], ki[g, a]), a, np.where(w, best[g, a], worst[g, a])))
            O[q][g, ss] = np.where(w, np.where(bb + 1 == L, 0, bb + 1), bb)
            if t < RO - 1: X[q][g, :, ss] = np.maximum(X[q][g, :, ss] - WEAR, 0)
            now[q] = np.count_nonzero(w)
        for r, g, k, a, z in res + back: M[r][g, k, a] = z
        wins = now
    return {"ym": M.reshape(N, 128, L).astype(np.float32), "yown": O.astype(np.float32)}

@@ -1,0 +1,531 @@
+from concourse.mybir import dt, AluOpType, AxisListType, ActivationFunctionType
+
+S, L, RO = 2176, 256, 3
+OP = AluOpType
+AF = ActivationFunctionType
+
+SCRATCH = {}
+ALIAS = {}
+
+
+def _d(name, where, shape, dtype):
+    SCRATCH[name] = (where, shape, dtype)
+
+
+for _t, _l in (
+        ("bfloat16", "Xw:2560 OWw:2560 ob:136 vR:4096 vI:4096 vN:4096 mxA:2048 mnA:2048 mxB:2048 mnB:2048 CR:256 CI:256 CB:256 "
+                     "TR:256 TI:256 TB:256 mA:2048 mB:2048 mC:2048 mD:2048 rm:256 bG:256 dm:256 bs:256 EQ:4096 fG:256 fd:256 "
+                     "fs:256 vS:256 vT:256 fI:256 fR:256 mh:128 Nb:128 BA:16 E:2048 one:256 hf:2048 m0:1024 a0:1024 BK:256 "
+                     "BK1:256 BC:256 BM:16 BV:16 KR:256 Ib:128 W1:128 W2:128 W0:128 MIb:256"),
+        ("float32", "ZRw:640 Mo:256 kR:256 FR:256 thd:256 Fs:512 nw:512 np:512 RSI:512 NSI:512 NSR:512 MF:256 SIs:256 ex:256 nF:256 "
+                    "PC:272 mk2:256 DL:256 ez:256 zG:256 ov:256 ow:256 wf:256 TH:128 TH0:128 sF32:256 pf:8 AK:256 mkf:256 "
+                    "If:128 thr:256 pw:256 pv:256 CC:8 MI:256 ii:256 ks:32 o6:128 B8:128"),
+        ("int32", "NBw:2176 Mi:256 Tm:256 Tm2:256 oi:136 sI32:64 pi:4 bi:32 thi:1"),
+        ("uint16", "nU:256 sU16:64 BL:32")):
+    for _x in _l.split():
+        _d("c_" + _x.split(":")[0], "sbuf", [128, int(_x.split(":")[1])], _t)
+for _k, _n in enumerate(("sF", "w1", "w2", "dc", "won", "d1", "d2", "d3", "zi", "zr", "ch")):
+    ALIAS[_n] = ("c_sF32", 16 * _k, 16)
+for _k, _n in enumerate(("wc", "w16", "thf")):
+    ALIAS[_n] = ("c_sF32", 192 + 16 * _k, 1)
+for _k, (_n, _c) in enumerate((("pk", 16), ("si", 16), ("wi", 1), ("wj", 1))):
+    ALIAS[_n] = ("c_sI32", 16 * _k, _c)
+for _k, _n in enumerate(("sU", "bU", "sWU", "bWU")):
+    ALIAS[_n] = ("c_sU16", 16 * _k, 16)
+for _t in range(RO):
+    _d("Mu%d" % _t, "sbuf", [128, 256], "uint16")
+    _d("Lin%d" % _t, "sbuf", [128, 256], "uint16")
+    _d("Do%d" % _t, "sbuf", [128, 256], "float32")
+    _d("Din%d" % _t, "sbuf", [128, 256], "float32")
+for _n in ("BC0", "BC1", "BC2", "BC3", "KE0", "KE1", "SIT", "MS0"):
+    _d("p_" + _n, "psum", [128, 512], "float32")
+_d("ownd", "dram", [8, S], "bfloat16")
+
+SEMAPHORES = (["qV", "qS", "qP", "qG", "dx", "dm", "dn", "do", "dod", "dor", "dth", "dy", "dyo"]
+              + [n + "%d" % t for n in ("aL", "aD", "lL", "lD") for t in range(RO)])
+
+
+def rank_program(g, core, T, topo):
+    rank = T.rank_of(core)
+    if rank is None:
+        return
+    N = len(T.cores)
+    Q = {"V": g.vector, "S": g.scalar, "P": g.tensor, "G": g, "Y": g.sync}
+    cnt = {"V": 0, "S": 0, "P": 0, "G": 0}
+    known = {q: {} for q in Q}
+    snap = {}
+    acc = {}
+    total = {}
+
+    def R(name, c0=0, c1=None, st=1, p0=0, p1=128):
+        o = 0
+        if name in ALIAS:
+            name, o, w = ALIAS[name]
+        else:
+            if not (name in SCRATCH):
+                name = "c_" + name if "c_" + name in SCRATCH else "p_" + name
+            w = SCRATCH[name][1][1]
+        c1 = o + (w if c1 is None else c1)
+        c0 = o + c0
+        ap = T[name][p0:p1, c0:c1] if st == 1 else T[name][p0:p1, c0:c1:st]
+        return (ap, name, c0, c1)
+
+    def H(name, h, o=0):
+        return R(name, o + h * 128, o + h * 128 + 128)
+
+    def ind(win, off):
+        return win[0].indirect(off[0])
+
+    def need(queue, reads, writes):
+        out = {}
+        for regs, wr in ((reads, False), (writes, True)):
+            for r in regs:
+                ps = r[1].startswith("p_")
+                for (c0, c1, q, src, n, w) in acc.get(r[1], []):
+                    if ps:
+                        if q == queue == "P":
+                            continue
+                        if q == queue and (not w or wr or c0 >= r[3] or r[2] >= c1):
+                            continue
+                    else:
+                        if c0 >= r[3] or r[2] >= c1 or not (w or wr):
+                            continue
+                        if q == queue and q in cnt and not w:
+                            continue
+                    out[src] = max(out.get(src, 0), n)
+        return out
+
+    def learn(queue, src, n):
+        k = known[queue]
+        k[src] = max(k.get(src, 0), n)
+        for s2, n2 in snap.get((src, n), {}).items():
+            k[s2] = max(k.get(s2, 0), n2)
+
+    def waits(queue, nd):
+        for src in sorted(nd, key=lambda s: -nd[s]):
+            if known[queue].get(src, 0) < nd[src]:
+                Q[queue].wait_ge(T.sem[src], nd[src])
+                learn(queue, src, nd[src])
+
+    def note(queue, label, src, n, reads, writes):
+        snap[(src, n)] = dict(known[queue])
+        for regs, wr in ((reads, False), (writes, True)):
+            for r in regs:
+                lst = acc.get(r[1], [])
+                if wr:
+                    lst = [e for e in lst if not (e[0] >= r[2] and e[1] <= r[3])]
+                acc[r[1]] = lst + [(r[2], r[3], label, src, n, wr)]
+
+    def op(queue, fn, reads, writes):
+        waits(queue, need(queue, reads, writes))
+        inst = fn()
+        cnt[queue] += 1
+        inst.then_inc(T.sem["q" + queue], 1)
+        total["q" + queue] = cnt[queue]
+        note(queue, queue, "q" + queue, cnt[queue], reads, writes)
+
+    def act(out, in_, off=None, func=AF.Copy):
+        src = in_[0] if off is None else ind(in_, off)
+        op("S", lambda: g.scalar.activation(out[0], src, func), [in_] + ([off] if off else []), [out])
+
+    def cp(out, in_, off=None):
+        src = in_[0] if off is None else ind(in_, off)
+        op("V", lambda: g.vector.tensor_copy(out[0], src), [in_] + ([off] if off else []), [out])
+
+    def scat(win, off, in_):
+        op("V", lambda: g.vector.tensor_copy(ind(win, off), in_[0]), [in_, off], [win])
+
+    def tt(out, a, b, o, off=None):
+        src = a[0] if off is None else ind(a, off)
+        op("V", lambda: g.vector.tensor_tensor(out[0], src, b[0], o), [a, b] + ([off] if off else []), [out])
+
+    def ts(out, a, s1, o1, s2=None, o2=None):
+        rd = [a]
+        x1 = s1
+        if isinstance(s1, tuple):
+            rd.append(s1)
+            x1 = s1[0]
+        if o2 is None:
+            op("V", lambda: g.vector.tensor_scalar(out[0], a[0], x1, None, o1), rd, [out])
+        else:
+            op("V", lambda: g.vector.tensor_scalar(out[0], a[0], x1, s2, o1, o2), rd, [out])
+
+    def scan(out, a, b, o1, o2):
+        op("V", lambda: g.vector.tensor_tensor_scan(out[0], a[0], b[0], 0.0, o1, o2), [a, b], [out])
+
+    def fill(out, x):
+        op("V", lambda: g.vector.memset(out[0], x), [], [out])
+
+    def mm(out, l, r, start=True, stop=True):
+        op("P", lambda: g.tensor.matmul(out[0], l[0], r[0], start, stop), [l, r], [out])
+
+    def rsum(out, in_):
+        op("V", lambda: g.vector.tensor_reduce(out[0], in_[0], AxisListType.X, OP.add), [in_], [out])
+
+    def iota(out, pat, base, mult):
+        op("G", lambda: g.iota(out[0], pat, base, mult, allow_small_or_imprecise_dtypes=True), [], [out])
+
+    def asel(out, in_, pat, cmp_, base, mult):
+        op("G", lambda: g.affine_select(out[0], in_[0], pat, cmp_, 0.0, base, mult), [in_], [out])
+
+    def dma(sem, pairs, reads, writes, queue="Y"):
+        waits(queue, need(queue, reads, writes))
+        for o, i in pairs:
+            Q[queue].dma_start(o, i).then_inc(T.sem[sem], 16)
+        total[sem] = 16 * len(pairs)
+        note(queue, "D", sem, total[sem], reads, writes)
+
+    def send(buf, land, dst, asem, lsem):
+        eng = topo.engines(core, dst)[:8]
+        m = 0
+        for e in eng:
+            m |= 1 << e
+        waits("G", need("G", [buf], []))
+        rid, pid = topo.addr(dst, core)
+        g.remote_dma(T[land][:], buf[0], T.sem[asem], T.sem[lsem], pid, rid, m)
+        total[lsem] = len(eng)
+
+    def arrive(land, asem, src):
+        n = len(topo.engines(src, core)[:8])
+        total[asem] = n
+        acc[land] = [(0, 256, "X", asem, n, True)]
+
+    def weave(*gens):
+        gens = list(gens)
+        while gens:
+            for x in list(gens):
+                if next(x, 0) == 0:
+                    gens.remove(x)
+
+    dma("dm", [(T.c_Mi[:, :], T.m0[:, :])], [], [R("Mi")], "S")
+    dma("dx", [(T.c_Xw[:, 0:S], T.x0[:, :])], [], [R("Xw", 0, S)])
+    dma("do", [(T.c_oi[:, :], T.own0[:, :])], [], [R("oi")])
+    dma("dth", [(T.c_thi[0:8, :], T.th[:, :])], [], [R("thi", 0, 1)])
+    dma("dn", [(T.c_NBw[:, :], T.nb[:, :])], [], [R("NBw")])
+    fill(R("one"), 1.0)
+    fill(R("m0"), 1.0)
+    fill(R("a0"), 0.0)
+    fill(R("hf"), 0.5)
+    fill(R("m0", 0, 1024, 16), 0.0)
+    fill(R("a0", 0, 1024, 16), 512.0)
+    cp(R("Mu0"), R("Mi"))
+    for t in range(RO):
+        arrive("Lin%d" % t, "aL%d" % t, T.cores[(rank - 1 - t) % N])
+        arrive("Din%d" % t, "aD%d" % t, T.cores[(rank + 1 + t) % N])
+    iota(R("pi", 0, 1), [[0, 1]], 0, 1)
+    iota(R("bi", 0, 16), [[1, 16]], 0, 0)
+    iota(R("bi", 16, 32), [[16, 16]], 15, 0)
+    asel(R("Ib"), R("one", 0, 128), [[-1, 128]], OP.is_equal, 0, 1)
+    send(R("Mu0"), "Lin0", T.cores[(rank + 1) % N], "aL0", "lL0")
+    asel(R("E"), R("hf"), [[-1, 128], [0, 16]], OP.is_equal, 0, 1)
+    asel(R("BK1"), R("one", 0, 256), [[0, 2], [-16, 8], [0, 16]], OP.is_ge, 0, 1)
+    asel(R("BK"), R("BK1"), [[0, 2], [16, 8], [0, 16]], OP.is_ge, 15, -1)
+    iota(R("KR"), [[-15, 2], [0, 8], [1, 16]], 0, 0)
+    iota(R("ii"), [[0, 16], [1, 16]], 0, 0)
+    iota(R("ks", 0, 16), [[16, 16]], S, 1)
+    iota(R("ks", 16, 32), [[16, 16]], 256, 1)
+
+    def consts_early():
+        cp(R("ob"), R("oi"))
+        dma("dod", [(T.ownd[:, :], T.c_ob[:, :])], [R("ob")], [("", "ownd", 0, S)])
+        dma("dor", [(T.c_OWw[i::16, 0:S], T.ownd[:, :]) for i in range(16)], [("", "ownd", 0, S)], [R("OWw", 0, S)])
+        ts(R("pi", 1, 2), R("pi", 0, 1), 15, OP.bitwise_and)
+        cp(R("If"), R("Ib"))
+        cp(R("pf", 0, 1), R("pi", 1, 2))
+        ts(R("Nb"), R("Ib"), -1.0, OP.mult)
+        ts(R("pf", 1, 2), R("pf", 0, 1), 1.0, OP.add, 4096.0, OP.mult)
+        fill(R("mh"), -0.5)
+        cp(R("BL"), R("bi"))
+
+    def consts_mid():
+        ts(R("BM", 0, 8), R("BK", 0, 128, 16), 32.0, OP.mult)
+        ts(R("BM", 8, 16), R("BK", 0, 128, 16), -32.0, OP.mult)
+        ts(R("BV", 0, 8), R("BK", 0, 128, 16), -16.0, OP.mult)
+        ts(R("BV", 8, 16), R("BK", 0, 128, 16), 16.0, OP.mult)
+        ts(R("BC", 0, 128), R("BK", 0, 128), -8.0, OP.mult)
+        ts(R("BC", 128, 256), R("BK", 0, 128), 8.0, OP.mult)
+        ts(R("BA"), R("BV"), -1.0, OP.mult)
+        fill(R("AK"), 0.0)
+        fill(R("mkf"), 1.0)
+        ts(R("MI"), R("ii"), R("pf", 0, 1), OP.is_equal)
+        fill(R("AK", 0, 256, 16), 1000000.0)
+        fill(R("mkf", 0, 256, 16), 0.0)
+        cp(R("MIb"), R("MI"))
+        cp(R("CC"), R("BK", 0, 128, 16))
+
+    def consts_late():
+        fill(R("pw"), 0.0)
+        ts(R("pv"), R("mkf"), 0.5, OP.mult)
+        fill(R("pw", 0, 256, 16), 2.0)
+        scan(R("thr"), R("pv"), R("pw"), OP.mult, OP.add)
+        fill(R("W0"), 0.0)
+        tt(R("thd"), R("thr"), R("MI"), OP.mult)
+        fill(R("o6"), 0.0625)
+        rsum(R("pf", 2, 3), R("thd", 0, 16))
+        ts(R("W1"), R("BK", 0, 128), 64.0, OP.mult)
+        ts(R("W2"), R("BK", 0, 128), R("pf", 2, 3), OP.mult, 0.5, OP.mult)
+        fill(R("PC", 0, 16), 0.0)
+        cp(R("thf", 0, 1, 1, 0, 8), R("thi", 0, 1, 1, 0, 8))
+        ts(R("B8", 0, 128, 1, 0, 8), R("E", 0, 128, 1, 0, 8), R("thf", 0, 1, 1, 0, 8), OP.mult, 512.0, OP.mult)
+        mm(R("MS0", 0, 128), R("o6", 0, 128, 1, 0, 8), R("B8", 0, 128, 1, 0, 8))
+        cp(R("TH0"), R("MS0", 0, 128))
+
+    def gather(v, lst, h):
+        for c in range(2):
+            a = h * 128 + c * 64
+            act(R(v, a * 16, a * 16 + 1024), R("Xw", 0, S), R(lst, a, a + 64))
+
+    def scans(v, h, bufs, nat):
+        mx, mn = bufs
+        for c in range(2):
+            x = R(v, h * 2048 + c * 1024, h * 2048 + c * 1024 + 1024)
+            scan(R(mx, c * 1024, c * 1024 + 1024), R("m0"), x, OP.mult, OP.max)
+            scan(R(mn, c * 1024, c * 1024 + 1024), R("a0"), x, OP.add, OP.min)
+        a, b = R(mx, 15, 2048, 16), R(mn, 15, 2048, 16)
+        one, mh = R("one", 0, 128, 1, 0, 1), R("mh", 0, 128, 1, 0, 1)
+        mm(H("MS0", h), a, R("Ib"), True, False)
+        mm(H("MS0", h), b, R("Ib"), False, False)
+        mm(H("MS0", h), one, mh, False, True)
+        if nat:
+            mm(H("MS0", h, 256), R("Ib"), a, True, False)
+            mm(H("MS0", h, 256), R("Ib"), b, False, False)
+            mm(H("MS0", h, 256), one, mh, False, True)
+
+    def floor2(out, h, o=0):
+        ts(H(out, h), H("MS0", h, o), 16777216.0, OP.add, 16777216.0, OP.subtract)
+
+    bcn, ken, mbn, bank, kes, mbs = [0], [0], [0], {}, {}, {}
+
+    def bc(u, b):
+        k = "BC%d" % (bcn[0] % 4)
+        bcn[0] += 1
+        bank[(u, b)] = k
+        mm(R(k), H(u[2], u[4]), R("E", b * 512, b * 512 + 512), True, u[3] is not None)
+        if u[3] is None:
+            mm(R(k), R("Nb"), R(u[1], u[4] * 2048 + b * 512, u[4] * 2048 + b * 512 + 512), False, True)
+
+    def key(u):
+        ke = "KE%d" % (ken[0] % 2)
+        ken[0] += 1
+        h, mb = u[4], mbs[u]
+        mm(R(ke, 0, 256), R("one", 0, 128, 1, 0, 1), R("KR", 0, 256, 1, 0, 1), True, False)
+        if u[3] is not None:
+            mm(R(ke, 0, 256), H(u[3], h), R("BC"), False, False)
+            for k in range(16):
+                mm(R(ke, k, 256, 16), R(u[1], h * 2048 + k, h * 2048 + 2048, 16), R("BV"), False, False)
+        for k in range(16):
+            mm(R(ke, k, 256, 16), R(mb, k, 2048, 16), R("BM" if u[3] is not None else "BA"), False, k == 15)
+        kes[(u[0], h)] = ke
+
+    def run_units(units, hooks={}):
+        flat = [(u, b) for u in units for b in range(4)]
+        for u, b in flat[:4]:
+            bc(u, b)
+        if 0 in hooks:
+            hooks[0]()
+        for n, (u, b) in enumerate(flat):
+            if b == 0:
+                mbs[u] = "m" + "ABCD"[mbn[0] % 4]
+                mbn[0] += 1
+            o = R(mbs[u], b * 512, b * 512 + 512)
+            if u[3] is None:
+                act(o, R(bank[(u, b)]), None, AF.Abs)
+            else:
+                tt(o, R(u[1], u[4] * 2048 + b * 512, u[4] * 2048 + b * 512 + 512), R(bank[(u, b)]), OP.max)
+            if n + 4 < len(flat):
+                bc(*flat[n + 4])
+            if b == 3 and u in hooks:
+                hooks[u]()
+
+    def pick(jobs):
+        jobs = [(H(kes[(who, h)], x), H(res, 2 * x + h), h, n) for n, (who, res, h, x) in enumerate(jobs)]
+        for k, res, h, n in jobs:
+            yield scan(H("Fs", n), R("AK", 0, 128), k, OP.add, OP.min)
+        for k, res, h, n in jobs:
+            yield tt(H("nw", n), k, H("Fs", n), OP.is_equal)
+        for k, res, h, n in jobs:
+            yield tt(H("np", n), H("nw", n), H("SIT", h), OP.mult)
+        for k, res, h, n in jobs:
+            yield scan(res, R("mkf", 0, 128), H("np", n), OP.mult, OP.max)
+
+    def flip(src, ps, idn):
+        for h in range(2):
+            mm(H(ps, h), H(src, h), R(idn))
+
+    E16 = (15, 256, 16)
+    E16b = (271, 512, 16)
+    BL = R("BL", 0, 16)
+    for t in range(RO):
+        last = t == RO - 1
+        mu, li, do = "Mu%d" % t, "Lin%d" % t, "Do%d" % t
+        r0, r1 = ("R", "vR", "TR", None, 0), ("R", "vR", "TR", None, 1)
+        i0, i1 = ("I", "vI", "TI", None, 0), ("I", "vI", "TI", "CI", 1)
+        ni0, ni1 = ("NI", "vN", "TI", None, 0), ("NI", "vN", "TI", None, 1)
+        nr0, nr1 = ("NR", "vN", "TB", "CB", 0), ("NR", "vN", "TB", None, 1)
+        th = "TH" if t else "TH0"
+        gather("vR", mu, 0)
+        gather("vR", mu, 1)
+        if t == 0:
+            consts_early()
+        scans("vR", 0, ("mxA", "mnA"), True)
+        if t == 0:
+            consts_mid()
+        scans("vR", 1, ("mxB", "mnB"), True)
+        floor2("TR", 0)
+        floor2("CR", 0, 256)
+        gather("vI", li, 0)
+        gather("vI", li, 1)
+        floor2("TR", 1)
+        floor2("CR", 1, 256)
+        ts(R("MF"), R(li), R("pf", 1, 2), OP.add)
+        flip("MF", "SIT", "If")
+        scans("vI", 0, ("mxA", "mnA"), False)
+        floor2("TI", 0)
+        run_units([i0])
+        scans("vI", 1, ("mxB", "mnB"), True)
+        key(i0)
+        act(R("SIs"), R("SIT", 0, 256))
+        floor2("TI", 1)
+        floor2("CI", 1, 256)
+        run_units([i1])
+        key(i1)
+        run_units([r0])
+        weave(pick([("I", "RSI", 0, 0), ("I", "RSI", 1, 0)]))
+        cp(R("pk"), R("RSI", *E16))
+        ts(R("si"), R("pk"), 4095, OP.bitwise_and)
+        tt(R("ex"), R("si"), R("MI"), OP.mult, BL)
+        for h in range(2):
+            mm(R("MS0", h * 8, h * 8 + 8), H("ex", h), R("CC"))
+        cp(R("sU"), R("MS0", 0, 16))
+        run_units([r1])
+        cp(R("nU"), R("NBw"), R("sU"))
+        for h in range(2):
+            gather("vN", "nU", h)
+
+        def opponents():
+            yield tt(R("dm"), R("OWw", 0, S), R("MIb"), OP.mult, R("sU"))
+            yield cp(R("bG"), R("OWw", 0, S), R("sU"))
+            yield scan(R("bs"), R("m0", 0, 256), R("dm"), OP.mult, OP.add)
+            yield cp(R("sF"), R("sU"))
+            yield cp(R("bU"), R("bs", *E16))
+            yield ts(R("nF"), R("nU"), R("pf", 1, 2), OP.add)
+            yield cp(R("CB"), R("CR"), R("bU"))
+            flip("CB", "MS0", "Ib")
+
+        weave(opponents(), pick([("I", "RSI", 0, 1), ("I", "RSI", 1, 1)]))
+        key(r0)
+        for h in range(2):
+            cp(H("TB", h), H("MS0", h))
+        flip("nF", "SIT", "If")
+        if t == 0:
+            consts_late()
+        offs = [sum(256 - 16 * x for x in range(c)) for c in range(16)]
+        for c in range(16):
+            ts(R("EQ", offs[c], offs[c] + 256 - 16 * c), R("bG", 16 * c, 256), R("bs", 16 * c + 15, 16 * c + 16), OP.is_equal)
+
+        def fighters():
+            mm(R("MS0", 0, 256), R("W0"), R("EQ", 0, 256), True, False)
+            for c in range(16):
+                if c < 15:
+                    mm(R("MS0", 16 * c + 16, 256), R("W1"), R("EQ", offs[c] + 16, offs[c] + 256 - 16 * c), False, False)
+                mm(R("MS0", 16 * c, 16 * c + 16), R("W2"), R("EQ", offs[c], offs[c] + 16), False, c == 15)
+
+        def judge(who, h):
+            res = "NSI" if who == "NI" else "NSR"
+            yield tt(H("fI" if who == "NI" else "fR", h), H(kes[(who, h)], 0), R(th), OP.is_lt)
+            yield from pick([(who, res, h, 0), (who, res, h, 1)])
+
+        def lists():
+            yield tt(R("fd"), R("MS0", 0, 256), R("thd"), OP.is_lt)
+            yield tt(R("fG"), R("MS0", 0, 256), R("thr"), OP.is_lt)
+            yield scan(R("fs"), R("m0", 0, 256), R("fd"), OP.mult, OP.add)
+            yield tt(R("w1"), R("sF"), R("ks", 0, 16), OP.subtract)
+            yield tt(R("w2"), R("bs", *E16), R("ks", 16, 32), OP.subtract)
+            yield tt(R("w1"), R("w1"), R("fs", *E16), OP.mult)
+            yield tt(R("w2"), R("w2"), R("fs", *E16), OP.mult)
+            yield tt(R("w1"), R("w1"), R("ks", 0, 16), OP.add)
+            yield tt(R("w2"), R("w2"), R("ks", 16, 32), OP.add)
+            yield cp(R("sWU"), R("w1"))
+            yield cp(R("bWU"), R("w2"))
+            yield fill(R("ZRw", 0, 256), 0.0)
+            yield tt(R("d3"), R("RSI", *E16b), R("RSI", *E16), OP.subtract)
+            if not last:
+                yield cp(R("vS"), R("Xw", 0, S), R("sU"))
+                yield ts(R("vT"), R("vS"), -8.0, OP.add, 0.0, OP.max)
+
+        run_units([nr0], {0: fighters})
+        key(r1)
+        for h in range(2):
+            scan(H("FR", h), R("AK", 0, 128), H(kes[("R", h)], 1), OP.add, OP.min)
+            cp(H("kR", h), H(kes[("R", h)], 1))
+        key(nr0)
+        tt(R("rm"), R("FR"), R("kR"), OP.is_equal, R("BL", 16, 32))
+
+        def first():
+            weave(judge("NR", 0))
+            weave(lists())
+
+        def second():
+            key(ni1)
+            weave(judge("NI", 0))
+
+        run_units([ni0, ni1, nr1], {0: first, ni0: lambda: key(ni0), ni1: second})
+        key(nr1)
+        weave(judge("NI", 1))
+        weave(judge("NR", 1))
+        flip("rm", "SIT", "Ib")
+        scan(R("PC", 16, 272), R("fI"), R("fR"), OP.add, OP.subtract)
+        tt(R("d1"), R("NSI", *E16), R("NSR", *E16b), OP.subtract)
+        tt(R("dc"), R("PC", 31, 272, 16), R("PC", *E16), OP.subtract)
+        tt(R("d2"), R("NSI", *E16b), R("NSR", *E16), OP.subtract)
+        ts(R("won"), R("dc"), 0.0, OP.is_gt)
+        ts(R("d2"), R("d2"), 262144.0, OP.add)
+        tt(R("d3"), R("d3"), R("won"), OP.mult)
+        tt(R("d1"), R("d1"), R("won"), OP.mult)
+        tt(R("ch"), R("d3"), R("RSI", *E16), OP.add)
+        tt(R("zi"), R("d1"), R("NSR", *E16b), OP.add)
+        tt(R("mk2"), R("ch"), R("SIs"), OP.is_equal, BL)
+        tt(R("DL"), R("zi"), R("mk2"), OP.mult, BL)
+        flip("DL", "MS0", "If")
+        tt(R("d2"), R("d2"), R("won"), OP.mult)
+        tt(R("zr"), R("d2"), R("NSR", *E16), OP.add)
+        act(R("ez"), R("zr"), BL)
+        flip("ez", "BC0", "If")
+        tt(R(do), R("MS0", 0, 256), R("fG"), OP.mult)
+        send(R(do), "Din%d" % t, T.cores[(rank - 1 - t) % N], "aD%d" % t, "lD%d" % t)
+        act(R("zG"), R("BC0", 0, 256))
+        if not last:
+            scat(R("Xw"), R("sWU"), R("vT"))
+        scat(R("ZRw"), R("bWU"), R("zG"))
+        tt(R("SIT", 256, 512), R("ZRw", 0, 256), R("SIT", 0, 256), OP.mult)
+        tt(R("Tm"), R("Mi"), R("SIT", 256, 512), OP.max)
+        ts(R("Tm2"), R("Tm"), 4095, OP.bitwise_and)
+        cp(R("SIT", 0, 256), R("Tm2"))
+        ts(R("BC1", 0, 256), R("zG"), 262144.0, OP.is_ge)
+        tt(R("ov"), R("bG"), R("BC1", 0, 256), OP.add)
+        ts(R("BC1", 256, 512), R("ov"), 256.0, OP.is_ge, -256.0, OP.mult)
+        tt(R("ow"), R("ov"), R("BC1", 256, 512), OP.add)
+        if last:
+            scat(R("OWw"), R("sWU"), R("ow"))
+            waits("G", need("G", [R("OWw", 0, S)], []))
+            g.dma_start(T.yown[:, :], T.c_OWw[0::16, 0:S]).then_inc(T.sem.dyo, 16)
+            total["dyo"] = 16
+        tt(R("Tm"), R("Din%d" % t), R("SIT", 0, 256), OP.max)
+        ts(R("Mi"), R("Tm"), 4095, OP.bitwise_and)
+        if last:
+            cp(R("Mo"), R("Mi"))
+            dma("dy", [(T.ym[:, :], T.c_Mo[:, :])], [R("Mo")], [])
+        else:
+            cp(R("Mu%d" % (t + 1)), R("Mi"))
+            send(R("Mu%d" % (t + 1)), "Lin%d" % (t + 1), T.cores[(rank + 2 + t) % N], "aL%d" % (t + 1), "lL%d" % (t + 1))
+            scat(R("OWw"), R("sWU"), R("ow"))
+            tt(R("wf"), R("BC1", 0, 256), R("fG"), OP.mult)
+            rsum(R("wc"), R("wf"))
+            mm(R("MS0", 0, 1), R("o6"), R("wc"))
+            cp(R("wi"), R("MS0", 0, 1))
+            ts(R("wj"), R("wi"), 63, OP.bitwise_and)
+            ts(R("w16"), R("wj"), 16.0, OP.mult)
+            ts(R("TH"), R("TH0"), R("w16"), OP.add)
+    for s in sorted(total):
+        if known["G"].get(s, 0) < total[s]:
+            g.wait_ge(T.sem[s], total[s])

@@ -3,6 +3,16 @@ from concourse.mybir import dt, AluOpType, AxisListType, ActivationFunctionType
 S, L, RO = 2176, 256, 3
 OP = AluOpType
 AF = ActivationFunctionType
+MID = 1088.0
+BIG = 16384.0
+R1, R16, R4096 = 1.5 * 2 ** 23, 1.5 * 2 ** 27, 1.5 * 2 ** 35
+
+ON_V = {"I": (8, 8), "NI": (0, 0), "NR": (16, 16), "R": (0, 0)}
+GATHER_V = {"vR": (1,), "vI": (1,), "vN": ()}
+SYNC, HOP, LOAD = 0.2, 2.3, 1.6
+LOOK = 5.0
+TURNS = 6
+ORDER = []
 
 SCRATCH = {}
 ALIAS = {}
@@ -13,36 +23,36 @@ def _d(name, where, shape, dtype):
 
 
 for _t, _l in (
-        ("bfloat16", "Xw:2560 OWw:2560 ob:136 vR:4096 vI:4096 vN:4096 mxA:2048 mnA:2048 mxB:2048 mnB:2048 CR:256 CI:256 CB:256 "
-                     "TR:256 TI:256 TB:256 mA:2048 mB:2048 mC:2048 mD:2048 rm:256 bG:256 dm:256 bs:256 EQ:4096 fG:256 fd:256 "
-                     "fs:256 vS:256 vT:256 fI:256 fR:256 mh:128 Nb:128 BA:16 E:2048 one:256 hf:2048 m0:1024 a0:1024 BK:256 "
-                     "BK1:256 BC:256 BM:16 BV:16 KR:256 Ib:128 W1:128 W2:128 W0:128 MIb:256"),
-        ("float32", "ZRw:640 Mo:256 kR:256 FR:256 thd:256 Fs:512 nw:512 np:512 RSI:512 NSI:512 NSR:512 MF:256 SIs:256 ex:256 nF:256 "
-                    "PC:272 mk2:256 DL:256 ez:256 zG:256 ov:256 ow:256 wf:256 TH:128 TH0:128 sF32:256 pf:8 AK:256 mkf:256 "
-                    "If:128 thr:256 pw:256 pv:256 CC:8 MI:256 ii:256 ks:32 o6:128 B8:128"),
-        ("int32", "NBw:2176 Mi:256 Tm:256 Tm2:256 oi:136 sI32:64 pi:4 bi:32 thi:1"),
-        ("uint16", "nU:256 sU16:64 BL:32")):
+        ("bfloat16", "Xw:2432 OWw:2432 ob:136 vR:4096 vI:4096 vN:4096 mxA:2048 mnA:2048 mxB:2048 mnB:2048 CR:256 CI:256 CB:256 "
+                     "mA:2048 mB:2048 mC:2048 mD:2048 bG:256 EQ:2176 nfG:256 vT:256 fI:256 fR:256 PC:272 ow:256 NE:1024 wf:16 "
+                     "one:256 m0:1024 a0:1024 AK:512 Ib:128 Nb:128 H1:128 H2:128 BK:256 BK1:256 BC:256 BC4:256 BC8:256 BC12:256 "
+                     "BM:16 BV:16 BA:16 KR:512 TG:128 MI:256 DB:256 D1:256 W1:128 W2:128 Sel:16 kw:256 WY:256 WZ:256 WO:256 "
+                     "cq:128 cq1:128 cc:256"),
+        ("float16", "SF:256 SN:256 ex:256 bs:256 fs:256 TP:128 TR:128 TY:128 KK:32"),
+        ("float32", "ZR0:2432 ZR1:2432 ZR2:2432 Mo:256 FI:512 FR:256 FN:1024 RS:256 NS:1024 x1:256 zG:256 TH:128 TH0:128 ZK:128 "
+                    "Df:64 Pr:64 sF32:256 pf:8 If:128 thr:256 pw:256 pv:256 ii:256 ks:16 o6:128 B8:128"),
+        ("int32", "NBw:2176 Mi:256 Tm:256 oi:136 pi:8 bi:16 thi:1 wI:16"),
+        ("uint16", "nU:256 sU16:64 BL:8 WL:4")):
     for _x in _l.split():
         _d("c_" + _x.split(":")[0], "sbuf", [128, int(_x.split(":")[1])], _t)
-for _k, _n in enumerate(("sF", "w1", "w2", "dc", "won", "d1", "d2", "d3", "zi", "zr", "ch")):
-    ALIAS[_n] = ("c_sF32", 16 * _k, 16)
-for _k, _n in enumerate(("wc", "w16", "thf")):
-    ALIAS[_n] = ("c_sF32", 192 + 16 * _k, 1)
-for _k, (_n, _c) in enumerate((("pk", 16), ("si", 16), ("wi", 1), ("wj", 1))):
-    ALIAS[_n] = ("c_sI32", 16 * _k, _c)
-for _k, _n in enumerate(("sU", "bU", "sWU", "bWU")):
-    ALIAS[_n] = ("c_sU16", 16 * _k, 16)
+for _k, (_n, _c) in enumerate((("sl", 16), ("r1", 16), ("sF", 16), ("bL", 16), ("won", 16), ("dl", 16), ("f1", 16), ("w16", 1),
+                               ("r2", 32), ("thf", 1), ("sb", 32), ("-", 1), ("r3", 64))):
+    ALIAS[_n] = ("c_sF32", 16 * _k, _c)
+ALIAS["thf"] = ("c_pf", 7, 1)
+for _k, (_n, _c) in enumerate((("sU", 16), ("bU", 16), ("WU", 32))):
+    ALIAS[_n] = ("c_sU16", 16 * _k, _c)
 for _t in range(RO):
     _d("Mu%d" % _t, "sbuf", [128, 256], "uint16")
     _d("Lin%d" % _t, "sbuf", [128, 256], "uint16")
-    _d("Do%d" % _t, "sbuf", [128, 256], "float32")
-    _d("Din%d" % _t, "sbuf", [128, 256], "float32")
-for _n in ("BC0", "BC1", "BC2", "BC3", "KE0", "KE1", "SIT", "MS0"):
+    _d("Do%d" % _t, "sbuf", [128, 80], "float16")
+    _d("Din%d" % _t, "sbuf", [128, 48], "float16")
+for _n in ("D0", "D1", "D2", "K0", "K1", "H0", "H1", "MS"):
     _d("p_" + _n, "psum", [128, 512], "float32")
 _d("ownd", "dram", [8, S], "bfloat16")
 
 SEMAPHORES = (["qV", "qS", "qP", "qG", "dx", "dm", "dn", "do", "dod", "dor", "dth", "dy", "dyo"]
               + [n + "%d" % t for n in ("aL", "aD", "lL", "lD") for t in range(RO)])
+WIDE = {"float32": 4, "int32": 4, "bfloat16": 2, "float16": 2, "uint16": 2}
 
 
 def rank_program(g, core, T, topo):
@@ -51,481 +61,483 @@ def rank_program(g, core, T, topo):
         return
     N = len(T.cores)
     Q = {"V": g.vector, "S": g.scalar, "P": g.tensor, "G": g, "Y": g.sync}
-    cnt = {"V": 0, "S": 0, "P": 0, "G": 0}
-    known = {q: {} for q in Q}
-    snap = {}
+    ops = []
     acc = {}
-    total = {}
+    turn = {}
 
-    def R(name, c0=0, c1=None, st=1, p0=0, p1=128):
+    def R(name, c0=0, c1=None, st=1, p1=128):
         o = 0
         if name in ALIAS:
             name, o, w = ALIAS[name]
         else:
             if not (name in SCRATCH):
-                name = "c_" + name if "c_" + name in SCRATCH else "p_" + name
+                name = "c_" + name
             w = SCRATCH[name][1][1]
         c1 = o + (w if c1 is None else c1)
         c0 = o + c0
-        ap = T[name][p0:p1, c0:c1] if st == 1 else T[name][p0:p1, c0:c1:st]
-        return (ap, name, c0, c1)
+        ap = T[name][0:p1, c0:c1] if st == 1 else T[name][0:p1, c0:c1:st]
+        return (ap, name, c0, c1, len(range(c0, c1, st)))
 
-    def H(name, h, o=0):
-        return R(name, o + h * 128, o + h * 128 + 128)
+    def H(name, h, o=0, p1=128):
+        return R(name, o + h * 128, o + h * 128 + 128, 1, p1)
 
-    def ind(win, off):
-        return win[0].indirect(off[0])
+    def E(name, c0=0, c1=None):
+        return R(name, c0 + 15, c1, 16)
 
-    def need(queue, reads, writes):
-        out = {}
+    def op(queue, fn, reads, writes, us, sem=None, late=0.0, after=()):
+        me = len(ops)
+        dep = {a: True for a in after}
         for regs, wr in ((reads, False), (writes, True)):
             for r in regs:
                 ps = r[1].startswith("p_")
-                for (c0, c1, q, src, n, w) in acc.get(r[1], []):
-                    if ps:
-                        if q == queue == "P":
-                            continue
-                        if q == queue and (not w or wr or c0 >= r[3] or r[2] >= c1):
-                            continue
+                if ps:
+                    q, cur, prev = turn.get(r[1], (queue, [], []))
+                    if q != queue:
+                        cur, prev = [], cur
+                    for a in prev:
+                        dep[a] = True
+                    if queue == "P" and cur and cur[-1] != me:
+                        dep.setdefault(cur[-1], False)
+                    turn[r[1]] = (queue, cur + [me] if me not in cur else cur, prev)
+                for (c0, c1, a, w) in acc.get(r[1], []):
+                    if c0 >= r[3] or r[2] >= c1 or not (w or wr) or a == me:
+                        continue
+                    own = ops[a]["q"] == queue and ops[a]["sem"] is None and sem is None
+                    if own and (not w or queue == "P" or (ps and wr)):
+                        dep.setdefault(a, False)
                     else:
-                        if c0 >= r[3] or r[2] >= c1 or not (w or wr):
-                            continue
-                        if q == queue and q in cnt and not w:
-                            continue
-                    out[src] = max(out.get(src, 0), n)
-        return out
-
-    def learn(queue, src, n):
-        k = known[queue]
-        k[src] = max(k.get(src, 0), n)
-        for s2, n2 in snap.get((src, n), {}).items():
-            k[s2] = max(k.get(s2, 0), n2)
-
-    def waits(queue, nd):
-        for src in sorted(nd, key=lambda s: -nd[s]):
-            if known[queue].get(src, 0) < nd[src]:
-                Q[queue].wait_ge(T.sem[src], nd[src])
-                learn(queue, src, nd[src])
-
-    def note(queue, label, src, n, reads, writes):
-        snap[(src, n)] = dict(known[queue])
+                        dep[a] = True
+        ops.append({"q": queue, "fn": fn, "us": us, "sem": sem, "late": late, "dep": dep})
         for regs, wr in ((reads, False), (writes, True)):
             for r in regs:
                 lst = acc.get(r[1], [])
-                if wr:
+                if wr and r[4] == r[3] - r[2]:
                     lst = [e for e in lst if not (e[0] >= r[2] and e[1] <= r[3])]
-                acc[r[1]] = lst + [(r[2], r[3], label, src, n, wr)]
+                acc[r[1]] = lst + [(r[2], r[3], me, wr)]
+        return me
 
-    def op(queue, fn, reads, writes):
-        waits(queue, need(queue, reads, writes))
-        inst = fn()
-        cnt[queue] += 1
-        inst.then_inc(T.sem["q" + queue], 1)
-        total["q" + queue] = cnt[queue]
-        note(queue, queue, "q" + queue, cnt[queue], reads, writes)
+    CY = 0.00083
 
-    def act(out, in_, off=None, func=AF.Copy):
-        src = in_[0] if off is None else ind(in_, off)
-        op("S", lambda: g.scalar.activation(out[0], src, func), [in_] + ([off] if off else []), [out])
+    def narrow(*rs):
+        return 0.5 if all(WIDE[SCRATCH[r[1]][2]] == 2 for r in rs) else 1
+
+    def cyc(n):
+        return max(64, n) * CY
+
+    def src(a, off):
+        return a[0] if off is None else a[0].indirect(off[0])
+
+    def gat(out):
+        return 0.06 + 1.56 * CY * out[4]
+
+    def act(out, in_, off=None, func=AF.Copy, bias=None):
+        x = src(in_, off)
+        fn = (lambda: g.scalar.activation(out[0], x, func)) if bias is None else (lambda: g.scalar.activation(out[0], x, func, bias))
+        op("S", fn, [in_] + ([off] if off else []), [out], gat(out) if off else cyc(out[4]))
 
     def cp(out, in_, off=None):
-        src = in_[0] if off is None else ind(in_, off)
-        op("V", lambda: g.vector.tensor_copy(out[0], src), [in_] + ([off] if off else []), [out])
+        x = src(in_, off)
+        op("V", lambda: g.vector.tensor_copy(out[0], x), [in_] + ([off] if off else []), [out],
+           gat(out) if off else cyc(out[4] * narrow(out, in_)))
 
     def scat(win, off, in_):
-        op("V", lambda: g.vector.tensor_copy(ind(win, off), in_[0]), [in_, off], [win])
+        op("V", lambda: g.vector.tensor_copy(win[0].indirect(off[0]), in_[0]), [in_, off], [win], 0.05 + 3.8 * CY * in_[4])
 
     def tt(out, a, b, o, off=None):
-        src = a[0] if off is None else ind(a, off)
-        op("V", lambda: g.vector.tensor_tensor(out[0], src, b[0], o), [a, b] + ([off] if off else []), [out])
+        x = src(a, off)
+        op("V", lambda: g.vector.tensor_tensor(out[0], x, b[0], o), [a, b] + ([off] if off else []), [out],
+           gat(out) if off else cyc(out[4] * (1 if "p_" in (a[1][:2], b[1][:2]) else 2)))
 
-    def ts(out, a, s1, o1, s2=None, o2=None):
-        rd = [a]
-        x1 = s1
+    def ts(out, a, s1, o1, s2=None, o2=None, off=None):
+        rd = [a] + ([off] if off else [])
+        x, x1 = src(a, off), s1
         if isinstance(s1, tuple):
             rd.append(s1)
             x1 = s1[0]
+        us = gat(out) if off else cyc(out[4] * narrow(out, a))
         if o2 is None:
-            op("V", lambda: g.vector.tensor_scalar(out[0], a[0], x1, None, o1), rd, [out])
+            op("V", lambda: g.vector.tensor_scalar(out[0], x, x1, None, o1), rd, [out], us)
         else:
-            op("V", lambda: g.vector.tensor_scalar(out[0], a[0], x1, s2, o1, o2), rd, [out])
+            op("V", lambda: g.vector.tensor_scalar(out[0], x, x1, s2, o1, o2), rd, [out], us)
 
     def scan(out, a, b, o1, o2):
-        op("V", lambda: g.vector.tensor_tensor_scan(out[0], a[0], b[0], 0.0, o1, o2), [a, b], [out])
+        op("V", lambda: g.vector.tensor_tensor_scan(out[0], a[0], b[0], 0.0, o1, o2), [a, b], [out], cyc(out[4] * narrow(out, a, b)))
 
     def fill(out, x):
-        op("V", lambda: g.vector.memset(out[0], x), [], [out])
+        op("V", lambda: g.vector.memset(out[0], x), [], [out], cyc(out[4] * narrow(out)))
 
     def mm(out, l, r, start=True, stop=True):
-        op("P", lambda: g.tensor.matmul(out[0], l[0], r[0], start, stop), [l, r], [out])
+        op("P", lambda: g.tensor.matmul(out[0], l[0], r[0], start, stop), [l, r], [out],
+           max(min(64, l[4]), r[4]) * CY / 2 * (4 if SCRATCH[l[1]][2] == "float32" else 1))
 
     def rsum(out, in_):
-        op("V", lambda: g.vector.tensor_reduce(out[0], in_[0], AxisListType.X, OP.add), [in_], [out])
+        op("V", lambda: g.vector.tensor_reduce(out[0], in_[0], AxisListType.X, OP.add), [in_], [out], cyc(in_[4]))
 
-    def iota(out, pat, base, mult):
-        op("G", lambda: g.iota(out[0], pat, base, mult, allow_small_or_imprecise_dtypes=True), [], [out])
+    def iota(out, pat, base, mult=0):
+        op("G", lambda: g.iota(out[0], pat, base, mult, allow_small_or_imprecise_dtypes=True), [], [out], 0.13 + 2 * CY * out[4])
 
-    def asel(out, in_, pat, cmp_, base, mult):
-        op("G", lambda: g.affine_select(out[0], in_[0], pat, cmp_, 0.0, base, mult), [in_], [out])
+    def asel(out, in_, pat, cmp_, base, mult=1, other=0.0):
+        op("G", lambda: g.affine_select(out[0], in_[0], pat, cmp_, other, base, mult), [in_], [out], 0.17 + 2 * CY * out[4])
 
-    def dma(sem, pairs, reads, writes, queue="Y"):
-        waits(queue, need(queue, reads, writes))
-        for o, i in pairs:
-            Q[queue].dma_start(o, i).then_inc(T.sem[sem], 16)
-        total[sem] = 16 * len(pairs)
-        note(queue, "D", sem, total[sem], reads, writes)
+    def dma(sem, pairs, reads, writes, late, queue="Y", after=()):
+        def fn():
+            for o, i in pairs:
+                Q[queue].dma_start(o, i).then_inc(T.sem[sem], 16)
+        return op(queue, fn, reads, writes, 0.05 * len(pairs), (sem, 16 * len(pairs)), late, after)
 
-    def send(buf, land, dst, asem, lsem):
+    def send(buf, land, step, asem, lsem):
+        dst, frm = T.cores[(rank + step) % N], T.cores[(rank - step) % N]
         eng = topo.engines(core, dst)[:8]
-        m = 0
-        for e in eng:
-            m |= 1 << e
-        waits("G", need("G", [buf], []))
         rid, pid = topo.addr(dst, core)
-        g.remote_dma(T[land][:], buf[0], T.sem[asem], T.sem[lsem], pid, rid, m)
-        total[lsem] = len(eng)
+        s = op("G", lambda: g.remote_dma(T[land][:], buf[0], T.sem[asem], T.sem[lsem], pid, rid, sum(1 << e for e in eng)),
+               [buf], [], 0.3, (lsem, len(eng)), HOP)
+        op("X", None, [], [R(land)], 0.0, (asem, len(topo.engines(frm, core)[:8])), 0.0, [s])
 
-    def arrive(land, asem, src):
-        n = len(topo.engines(src, core)[:8])
-        total[asem] = n
-        acc[land] = [(0, 256, "X", asem, n, True)]
-
-    def weave(*gens):
-        gens = list(gens)
-        while gens:
-            for x in list(gens):
-                if next(x, 0) == 0:
-                    gens.remove(x)
-
-    dma("dm", [(T.c_Mi[:, :], T.m0[:, :])], [], [R("Mi")], "S")
-    dma("dx", [(T.c_Xw[:, 0:S], T.x0[:, :])], [], [R("Xw", 0, S)])
-    dma("do", [(T.c_oi[:, :], T.own0[:, :])], [], [R("oi")])
-    dma("dth", [(T.c_thi[0:8, :], T.th[:, :])], [], [R("thi", 0, 1)])
-    dma("dn", [(T.c_NBw[:, :], T.nb[:, :])], [], [R("NBw")])
-    fill(R("one"), 1.0)
-    fill(R("m0"), 1.0)
-    fill(R("a0"), 0.0)
-    fill(R("hf"), 0.5)
-    fill(R("m0", 0, 1024, 16), 0.0)
-    fill(R("a0", 0, 1024, 16), 512.0)
+    a = dma("dm", [(T.c_Mi[:, :], T.m0[:, :])], [], [R("Mi")], LOAD, "S")
+    a = dma("dx", [(T.c_Xw[:, 0:S], T.x0[:, :])], [], [R("Xw", 0, S)], LOAD + 2.5)
+    dma("do", [(T.c_oi[:, :], T.own0[:, :])], [], [R("oi")], LOAD + 3)
+    dma("dth", [(T.c_thi[0:8, :], T.th[:, :])], [], [R("thi")], LOAD + 3)
+    dma("dn", [(T.c_NBw[:, :], T.nb[:, :])], [], [R("NBw")], LOAD + 8)
     cp(R("Mu0"), R("Mi"))
-    for t in range(RO):
-        arrive("Lin%d" % t, "aL%d" % t, T.cores[(rank - 1 - t) % N])
-        arrive("Din%d" % t, "aD%d" % t, T.cores[(rank + 1 + t) % N])
-    iota(R("pi", 0, 1), [[0, 1]], 0, 1)
-    iota(R("bi", 0, 16), [[1, 16]], 0, 0)
-    iota(R("bi", 16, 32), [[16, 16]], 15, 0)
-    asel(R("Ib"), R("one", 0, 128), [[-1, 128]], OP.is_equal, 0, 1)
-    send(R("Mu0"), "Lin0", T.cores[(rank + 1) % N], "aL0", "lL0")
-    asel(R("E"), R("hf"), [[-1, 128], [0, 16]], OP.is_equal, 0, 1)
-    asel(R("BK1"), R("one", 0, 256), [[0, 2], [-16, 8], [0, 16]], OP.is_ge, 0, 1)
+    send(R("Mu0"), "Lin0", 1, "aL0", "lL0")
+    cp(R("ob"), R("oi"))
+    dram = ("", "ownd", 0, S, S)
+    dma("dod", [(T.ownd[:, :], T.c_ob[:, :])], [R("ob")], [dram], LOAD + 5)
+    dma("dor", [(T.c_OWw[i::16, 0:S], T.ownd[:, :]) for i in range(16)], [dram], [R("OWw", 0, S)], LOAD + 3)
+    one = R("one", 0, 128, 1, 1)
+    fill(R("one"), 1.0)
+    for name, x, first in (("m0", 1.0, 0.0), ("a0", 0.0, 512.0), ("AK", 0.0, 1e7), ("pv", 0.5, 0.0), ("pw", 0.0, 2.0)):
+        fill(R(name), x)
+        fill(R(name, 0, None, 16), first)
+    asel(R("Ib"), R("one", 0, 128), [[-1, 128]], OP.is_equal, 0)
+    for name, x in (("Nb", -1.0), ("H1", 255 / 512), ("H2", 0.5), ("If", 1.0)):
+        ts(R(name), R("Ib"), x, OP.mult)
+    asel(R("BK1"), R("one"), [[0, 2], [-16, 8], [0, 16]], OP.is_ge, 0)
     asel(R("BK"), R("BK1"), [[0, 2], [16, 8], [0, 16]], OP.is_ge, 15, -1)
-    iota(R("KR"), [[-15, 2], [0, 8], [1, 16]], 0, 0)
-    iota(R("ii"), [[0, 16], [1, 16]], 0, 0)
-    iota(R("ks", 0, 16), [[16, 16]], S, 1)
-    iota(R("ks", 16, 32), [[16, 16]], 256, 1)
-
-    def consts_early():
-        cp(R("ob"), R("oi"))
-        dma("dod", [(T.ownd[:, :], T.c_ob[:, :])], [R("ob")], [("", "ownd", 0, S)])
-        dma("dor", [(T.c_OWw[i::16, 0:S], T.ownd[:, :]) for i in range(16)], [("", "ownd", 0, S)], [R("OWw", 0, S)])
-        ts(R("pi", 1, 2), R("pi", 0, 1), 15, OP.bitwise_and)
-        cp(R("If"), R("Ib"))
-        cp(R("pf", 0, 1), R("pi", 1, 2))
-        ts(R("Nb"), R("Ib"), -1.0, OP.mult)
-        ts(R("pf", 1, 2), R("pf", 0, 1), 1.0, OP.add, 4096.0, OP.mult)
-        fill(R("mh"), -0.5)
-        cp(R("BL"), R("bi"))
-
-    def consts_mid():
-        ts(R("BM", 0, 8), R("BK", 0, 128, 16), 32.0, OP.mult)
-        ts(R("BM", 8, 16), R("BK", 0, 128, 16), -32.0, OP.mult)
-        ts(R("BV", 0, 8), R("BK", 0, 128, 16), -16.0, OP.mult)
-        ts(R("BV", 8, 16), R("BK", 0, 128, 16), 16.0, OP.mult)
-        ts(R("BC", 0, 128), R("BK", 0, 128), -8.0, OP.mult)
-        ts(R("BC", 128, 256), R("BK", 0, 128), 8.0, OP.mult)
-        ts(R("BA"), R("BV"), -1.0, OP.mult)
-        fill(R("AK"), 0.0)
-        fill(R("mkf"), 1.0)
-        ts(R("MI"), R("ii"), R("pf", 0, 1), OP.is_equal)
-        fill(R("AK", 0, 256, 16), 1000000.0)
-        fill(R("mkf", 0, 256, 16), 0.0)
-        cp(R("MIb"), R("MI"))
-        cp(R("CC"), R("BK", 0, 128, 16))
-
-    def consts_late():
-        fill(R("pw"), 0.0)
-        ts(R("pv"), R("mkf"), 0.5, OP.mult)
-        fill(R("pw", 0, 256, 16), 2.0)
-        scan(R("thr"), R("pv"), R("pw"), OP.mult, OP.add)
-        fill(R("W0"), 0.0)
-        tt(R("thd"), R("thr"), R("MI"), OP.mult)
-        fill(R("o6"), 0.0625)
-        rsum(R("pf", 2, 3), R("thd", 0, 16))
-        ts(R("W1"), R("BK", 0, 128), 64.0, OP.mult)
-        ts(R("W2"), R("BK", 0, 128), R("pf", 2, 3), OP.mult, 0.5, OP.mult)
-        fill(R("PC", 0, 16), 0.0)
-        cp(R("thf", 0, 1, 1, 0, 8), R("thi", 0, 1, 1, 0, 8))
-        ts(R("B8", 0, 128, 1, 0, 8), R("E", 0, 128, 1, 0, 8), R("thf", 0, 1, 1, 0, 8), OP.mult, 512.0, OP.mult)
-        mm(R("MS0", 0, 128), R("o6", 0, 128, 1, 0, 8), R("B8", 0, 128, 1, 0, 8))
-        cp(R("TH0"), R("MS0", 0, 128))
+    CC = R("BK", 0, 128, 16)
+    for name, x in (("BM", 32.0), ("BV", -16.0), ("BA", 16.0)):
+        ts(R(name, 0, 8), CC, x, OP.mult)
+        ts(R(name, 8, 16), CC, -x, OP.mult)
+    ts(H("BC", 0), H("BK", 0), -16.0, OP.mult)
+    ts(H("BC", 1), H("BK", 0), 16.0, OP.mult)
+    for n in sorted(set(sum(ON_V.values(), ())) - {0, 16}):
+        asel(R("BC%d" % n), R("BC"), [[0, 16], [-1, 16]], OP.is_ge, n - 1, 0)
+    iota(R("ii"), [[0, 16], [1, 16]], 0)
+    for u in range(2):
+        ts(R("KR", 256 * u, 256 * u + 256, 1, 1), R("ii", 0, 256, 1, 1), -7.5, OP.add)
+    ts(R("TG", 0, 128, 1, 1), R("ii", 0, 128, 1, 1), -16.0, OP.add, 4096.0, OP.mult)
+    iota(R("pi", 0, 1), [[0, 1]], 0, 1)
+    ts(R("pi", 1, 2), R("pi", 0, 1), 15, OP.bitwise_and)
+    cp(R("pf", 0, 1), R("pi", 1, 2))
+    ts(R("pf", 1, 2), R("pf", 0, 1), 1.0, OP.add)
+    ts(R("pf", 3, 4), R("pf", 0, 1), 15.0, OP.is_lt, 256.0, OP.mult)
+    off = R("pf", 3, 4)
+    ts(R("MI"), R("ii"), R("pf", 0, 1), OP.is_equal)
+    ts(R("DB"), R("ii"), R("pf", 0, 1), OP.is_equal, -1024.0, OP.mult)
+    ts(R("D1"), R("ii"), R("pf", 1, 2), OP.is_equal, 256.0, OP.mult)
+    tt(R("DB"), R("DB"), R("D1"), OP.add)
+    iota(R("bi", 0, 8), [[1, 8]], 0)
+    cp(R("BL"), R("bi", 0, 8))
+    ts(R("pi", 2, 3), R("pi", 1, 2), 1, OP.arith_shift_right)
+    cp(R("WL", 0, 1), R("pi", 2, 3))
+    ts(R("WL", 1, 2), R("pi", 2, 3), 8.0, OP.add)
+    cp(R("WL", 2, 3), R("pi", 1, 2))
+    cp(R("WL", 3, 4), R("pi", 1, 2))
+    iota(R("ks"), [[16, 16]], S, 0)
+    ts(R("ks"), R("ks"), R("pf", 0, 1), OP.add)
+    scan(R("thr"), R("pv"), R("pw"), OP.mult, OP.add)
+    tt(R("pw", 0, 16), R("thr", 0, 16), R("MI", 0, 16), OP.mult)
+    rsum(R("pf", 2, 3), R("pw", 0, 16))
+    ts(R("W1"), H("BK", 0), 64.0, OP.mult)
+    ts(R("W2"), H("BK", 0), R("pf", 2, 3), OP.mult, 0.5, OP.mult)
+    cp(R("Sel", 0, 8), R("Ib", 0, 128, 16))
+    ts(R("Sel", 8, 16), R("Ib", 0, 128, 16), -256.0, OP.mult)
+    fill(R("PC", 0, 16), 0.0)
+    fill(R("o6"), 1.0)
+    ts(R("kw"), R("ii"), -7.5, OP.add, 2 * BIG, OP.mult)
+    asel(R("WY"), R("kw"), [[-16, 2], [-2, 8], [0, 16]], OP.is_equal, 0)
+    asel(R("WY"), R("WY"), [[-16, 2], [-2, 8], [0, 16]], OP.not_equal, -1, 1, -BIG)
+    asel(R("WY"), R("WY"), [[-8, 2], [-1, 8], [0, 16]], OP.not_equal, -32, 1, 1.0)
+    asel(R("WZ"), R("one"), [[-8, 2], [-1, 8], [0, 16]], OP.is_equal, 0)
+    asel(R("WO"), R("one"), [[-8, 2], [-1, 8], [0, 16]], OP.is_equal, -16)
+    ts(R("cq1", 0, 128, 1, 1), R("KR", 0, 128, 1, 1), -BIG, OP.mult)
+    tt(R("cq", 0, 128, 1, 1), R("cq1", 0, 128, 1, 1), R("KR", 0, 128, 1, 1), OP.mult)
+    fill(R("cc", 0, 256, 1, 1), MID + 8192)
+    for t in range(RO):
+        iota(R("ZR%d" % t, 0, 256), [[0, 256]], -30000)
+    cp(R("thf", 0, 1, 1, 8), R("thi", 0, 1, 1, 8))
+    ts(R("thf", 0, 1, 1, 8), R("thf", 0, 1, 1, 8), 16.0, OP.mult, -8.0, OP.add)
+    asel(R("B8", 0, 128, 1, 8), R("o6", 0, 128, 1, 8), [[-1, 8], [0, 16]], OP.is_equal, 0)
+    ts(R("B8", 0, 128, 1, 8), R("B8", 0, 128, 1, 8), R("thf", 0, 1, 1, 8), OP.mult)
+    mm(R("p_MS", 0, 128), R("o6", 0, 128, 1, 8), R("B8", 0, 128, 1, 8))
+    cp(R("TH0"), R("p_MS", 0, 128))
 
     def gather(v, lst, h):
-        for c in range(2):
-            a = h * 128 + c * 64
-            act(R(v, a * 16, a * 16 + 1024), R("Xw", 0, S), R(lst, a, a + 64))
+        for c in range(2 * h, 2 * h + 2):
+            (cp if c in GATHER_V[v] else act)(R(v, c * 1024, c * 1024 + 1024), R("Xw", 0, S), R(lst, c * 64, c * 64 + 64))
 
-    def scans(v, h, bufs, nat):
-        mx, mn = bufs
+    def centre(v, C, h):
+        mx, mn = ("mxA", "mnA") if h == 0 else ("mxB", "mnB")
         for c in range(2):
             x = R(v, h * 2048 + c * 1024, h * 2048 + c * 1024 + 1024)
             scan(R(mx, c * 1024, c * 1024 + 1024), R("m0"), x, OP.mult, OP.max)
             scan(R(mn, c * 1024, c * 1024 + 1024), R("a0"), x, OP.add, OP.min)
-        a, b = R(mx, 15, 2048, 16), R(mn, 15, 2048, 16)
-        one, mh = R("one", 0, 128, 1, 0, 1), R("mh", 0, 128, 1, 0, 1)
-        mm(H("MS0", h), a, R("Ib"), True, False)
-        mm(H("MS0", h), b, R("Ib"), False, False)
-        mm(H("MS0", h), one, mh, False, True)
-        if nat:
-            mm(H("MS0", h, 256), R("Ib"), a, True, False)
-            mm(H("MS0", h, 256), R("Ib"), b, False, False)
-            mm(H("MS0", h, 256), one, mh, False, True)
+        out = H("p_H%d" % h, 3)
+        mm(out, R("H1"), E(mx), True, False)
+        mm(out, R("H2"), E(mn), False, True)
+        ts(H(C, h), out, R1, OP.add, R1, OP.subtract)
 
-    def floor2(out, h, o=0):
-        ts(H(out, h), H("MS0", h, o), 16777216.0, OP.add, 16777216.0, OP.subtract)
+    def sites(sf, h):
+        out = H("p_H%d" % h, 2)
+        mm(out, one, R("TG", 0, 128, 1, 1), True, False)
+        mm(out, H(sf, h), R("Ib"), False, True)
 
-    bcn, ken, mbn, bank, kes, mbs = [0], [0], [0], {}, {}, {}
+    cnt = {"D": 0, "m": 0}
 
-    def bc(u, b):
-        k = "BC%d" % (bcn[0] % 4)
-        bcn[0] += 1
-        bank[(u, b)] = k
-        mm(R(k), H(u[2], u[4]), R("E", b * 512, b * 512 + 512), True, u[3] is not None)
-        if u[3] is None:
-            mm(R(k), R("Nb"), R(u[1], u[4] * 2048 + b * 512, u[4] * 2048 + b * 512 + 512), False, True)
-
-    def key(u):
-        ke = "KE%d" % (ken[0] % 2)
-        ken[0] += 1
-        h, mb = u[4], mbs[u]
-        mm(R(ke, 0, 256), R("one", 0, 128, 1, 0, 1), R("KR", 0, 256, 1, 0, 1), True, False)
-        if u[3] is not None:
-            mm(R(ke, 0, 256), H(u[3], h), R("BC"), False, False)
-            for k in range(16):
-                mm(R(ke, k, 256, 16), R(u[1], h * 2048 + k, h * 2048 + 2048, 16), R("BV"), False, False)
-        for k in range(16):
-            mm(R(ke, k, 256, 16), R(mb, k, 2048, 16), R("BM" if u[3] is not None else "BA"), False, k == 15)
-        kes[(u[0], h)] = ke
-
-    def run_units(units, hooks={}):
-        flat = [(u, b) for u in units for b in range(4)]
-        for u, b in flat[:4]:
-            bc(u, b)
-        if 0 in hooks:
-            hooks[0]()
-        for n, (u, b) in enumerate(flat):
-            if b == 0:
-                mbs[u] = "m" + "ABCD"[mbn[0] % 4]
-                mbn[0] += 1
-            o = R(mbs[u], b * 512, b * 512 + 512)
-            if u[3] is None:
-                act(o, R(bank[(u, b)]), None, AF.Abs)
+    def keys(v, h, units):
+        kb = "p_K%d" % h
+        w = 256 * len(units)
+        col = lambda k: R(v, h * 2048 + k, h * 2048 + 2048, 16)
+        ms = []
+        for u, (name, C) in enumerate(units):
+            ms.append("m" + "ABCD"[cnt["m"] % 4])
+            cnt["m"] += 1
+            if ON_V[name][h]:
+                mm(H("p_H%d" % h, u), R("Ib"), H(C, h))
+        mm(R(kb, 0, w), one, R("KR", 0, w, 1, 1), True, False)
+        for u, (name, C) in enumerate(units):
+            n = ON_V[name][h]
+            if n:
+                mm(R(kb, 256 * u, 256 * u + 256), H(C, h), R("BC" if n == 16 else "BC%d" % n), False, False)
+            for k in range(n):
+                mm(R(kb, 256 * u + k, 256 * u + 256, 16), col(k), R("BV"), False, False)
+        todo = [(b, u) for b in range(4) for u in range(len(units))]
+        todo.sort(key=lambda x: x[0] - (ON_V[units[x[1]][0]][h] // 4 if 4 * x[0] >= ON_V[units[x[1]][0]][h] else 0))
+        for b, u in todo:
+            name, C = units[u]
+            vec = 4 * b < ON_V[name][h]
+            if vec:
+                for k in range(4 * b, 4 * b + 4):
+                    tt(H(ms[u], k), col(k), H("p_H%d" % h, u), OP.max)
             else:
-                tt(o, R(u[1], u[4] * 2048 + b * 512, u[4] * 2048 + b * 512 + 512), R(bank[(u, b)]), OP.max)
-            if n + 4 < len(flat):
-                bc(*flat[n + 4])
-            if b == 3 and u in hooks:
-                hooks[u]()
+                d = "p_D%d" % (cnt["D"] % 3)
+                cnt["D"] += 1
+                for k in range(4):
+                    mm(H(d, k), R("Ib"), H(C, h), True, False)
+                    mm(H(d, k), R("Nb"), col(4 * b + k), False, True)
+                act(R(ms[u], b * 512, b * 512 + 512), R(d), None, AF.Abs)
+            for k in range(4 * b, 4 * b + 4):
+                mm(R(kb, 256 * u + k, 256 * u + 256, 16), H(ms[u], k), R("BM" if vec else "BA"), False,
+                   (b, u) == todo[-1] and k == 4 * b + 3)
 
-    def pick(jobs):
-        jobs = [(H(kes[(who, h)], x), H(res, 2 * x + h), h, n) for n, (who, res, h, x) in enumerate(jobs)]
-        for k, res, h, n in jobs:
-            yield scan(H("Fs", n), R("AK", 0, 128), k, OP.add, OP.min)
-        for k, res, h, n in jobs:
-            yield tt(H("nw", n), k, H("Fs", n), OP.is_equal)
-        for k, res, h, n in jobs:
-            yield tt(H("np", n), H("nw", n), H("SIT", h), OP.mult)
-        for k, res, h, n in jobs:
-            yield scan(res, R("mkf", 0, 128), H("np", n), OP.mult, OP.max)
+    def places(out, ends, n):
+        ts(R("r2", 0, n), ends, R16, OP.add, R16, OP.subtract)
+        tt(R(out, 0, 2 * n, 2), ends, R("r2", 0, n), OP.subtract)
+        tt(R(out, 1, 2 * n, 2), R(out, 0, 2 * n, 2), R(out, 0, 2 * n, 2), OP.mult)
 
-    def flip(src, ps, idn):
-        for h in range(2):
-            mm(H(ps, h), H(src, h), R(idn))
+    def turned(out, in_, c0):
+        mm(R("p_MS", c0, c0 + 128, 1, in_[4]), in_, R("Ib"))
+        cp(R(out, 0, 128, 1, in_[4]), R("p_MS", c0, c0 + 128, 1, in_[4]))
 
-    E16 = (15, 256, 16)
-    E16b = (271, 512, 16)
-    BL = R("BL", 0, 16)
     for t in range(RO):
         last = t == RO - 1
-        mu, li, do = "Mu%d" % t, "Lin%d" % t, "Do%d" % t
-        r0, r1 = ("R", "vR", "TR", None, 0), ("R", "vR", "TR", None, 1)
-        i0, i1 = ("I", "vI", "TI", None, 0), ("I", "vI", "TI", "CI", 1)
-        ni0, ni1 = ("NI", "vN", "TI", None, 0), ("NI", "vN", "TI", None, 1)
-        nr0, nr1 = ("NR", "vN", "TB", "CB", 0), ("NR", "vN", "TB", None, 1)
+        mu, li, do, zr = "Mu%d" % t, "Lin%d" % t, "Do%d" % t, "ZR%d" % t
         th = "TH" if t else "TH0"
-        gather("vR", mu, 0)
-        gather("vR", mu, 1)
-        if t == 0:
-            consts_early()
-        scans("vR", 0, ("mxA", "mnA"), True)
-        if t == 0:
-            consts_mid()
-        scans("vR", 1, ("mxB", "mnB"), True)
-        floor2("TR", 0)
-        floor2("CR", 0, 256)
-        gather("vI", li, 0)
-        gather("vI", li, 1)
-        floor2("TR", 1)
-        floor2("CR", 1, 256)
-        ts(R("MF"), R(li), R("pf", 1, 2), OP.add)
-        flip("MF", "SIT", "If")
-        scans("vI", 0, ("mxA", "mnA"), False)
-        floor2("TI", 0)
-        run_units([i0])
-        scans("vI", 1, ("mxB", "mnB"), True)
-        key(i0)
-        act(R("SIs"), R("SIT", 0, 256))
-        floor2("TI", 1)
-        floor2("CI", 1, 256)
-        run_units([i1])
-        key(i1)
-        run_units([r0])
-        weave(pick([("I", "RSI", 0, 0), ("I", "RSI", 1, 0)]))
-        cp(R("pk"), R("RSI", *E16))
-        ts(R("si"), R("pk"), 4095, OP.bitwise_and)
-        tt(R("ex"), R("si"), R("MI"), OP.mult, BL)
         for h in range(2):
-            mm(R("MS0", h * 8, h * 8 + 8), H("ex", h), R("CC"))
-        cp(R("sU"), R("MS0", 0, 16))
-        run_units([r1])
-        cp(R("nU"), R("NBw"), R("sU"))
+            gather("vR", mu, h)
+            centre("vR", "CR", h)
+        ts(R("SF"), R(li), -MID, OP.add)
         for h in range(2):
+            gather("vI", li, h)
+            sites("SF", h)
+            centre("vI", "CI", h)
+        for h in range(2):
+            kb, hb = "p_K%d" % h, "p_H%d" % h
+            keys("vI", h, [("I", "CI")])
+            scan(H("FI", 2 + h), R("AK", 0, 128), H(kb, 0), OP.add, OP.min)
+            tt(H("NE", h), H(kb, 0), H("FI", 2 + h), OP.not_equal)
+            scan(H("FI", h), R("AK", 0, 128), H(kb, 1), OP.add, OP.min)
+            scan(H("RS", h), H("NE", h), H(hb, 2), OP.mult, OP.min)
+            c = (8 * h, 8 * h + 8)
+            ends = E("RS", 128 * h, 128 * h + 128)
+            ts(R("r1", *c), ends, R4096, OP.add, R4096, OP.subtract)
+            tt(R("sl", *c), ends, R("r1", *c), OP.subtract)
+            tt(H("ex", h), R("sl", *c), H("MI", 0), OP.mult, R("BL"))
+            mm(R(hb, 384, 392), H("ex", h), CC)
+            ts(R("sU", *c), R(hb, 384, 392), MID, OP.add)
+            cp(H("nU", h), R("NBw"), R("sU", *c))
+            act(H("bG", h), R("OWw", 0, S), R("sU", *c))
             gather("vN", "nU", h)
-
-        def opponents():
-            yield tt(R("dm"), R("OWw", 0, S), R("MIb"), OP.mult, R("sU"))
-            yield cp(R("bG"), R("OWw", 0, S), R("sU"))
-            yield scan(R("bs"), R("m0", 0, 256), R("dm"), OP.mult, OP.add)
-            yield cp(R("sF"), R("sU"))
-            yield cp(R("bU"), R("bs", *E16))
-            yield ts(R("nF"), R("nU"), R("pf", 1, 2), OP.add)
-            yield cp(R("CB"), R("CR"), R("bU"))
-            flip("CB", "MS0", "Ib")
-
-        weave(opponents(), pick([("I", "RSI", 0, 1), ("I", "RSI", 1, 1)]))
-        key(r0)
-        for h in range(2):
-            cp(H("TB", h), H("MS0", h))
-        flip("nF", "SIT", "If")
-        if t == 0:
-            consts_late()
+            ts(H("SN", h), H("nU", h), -MID, OP.add)
+            sites("SN", h)
+            scan(H("bs", h), H("DB", h), H("bG", h), OP.add, OP.max)
+            ends = E("bs", 128 * h, 128 * h + 128)
+            ts(R("bU", *c), ends, off, OP.subtract)
+            act(H("CB", h), R("CR"), R("bU", *c))
+        ts(R("bL"), E("bs"), off, OP.subtract)
+        places("ZK", E("FI"), 32)
         offs = [sum(256 - 16 * x for x in range(c)) for c in range(16)]
         for c in range(16):
-            ts(R("EQ", offs[c], offs[c] + 256 - 16 * c), R("bG", 16 * c, 256), R("bs", 16 * c + 15, 16 * c + 16), OP.is_equal)
-
-        def fighters():
-            mm(R("MS0", 0, 256), R("W0"), R("EQ", 0, 256), True, False)
-            for c in range(16):
-                if c < 15:
-                    mm(R("MS0", 16 * c + 16, 256), R("W1"), R("EQ", offs[c] + 16, offs[c] + 256 - 16 * c), False, False)
-                mm(R("MS0", 16 * c, 16 * c + 16), R("W2"), R("EQ", offs[c], offs[c] + 16), False, c == 15)
-
-        def judge(who, h):
-            res = "NSI" if who == "NI" else "NSR"
-            yield tt(H("fI" if who == "NI" else "fR", h), H(kes[(who, h)], 0), R(th), OP.is_lt)
-            yield from pick([(who, res, h, 0), (who, res, h, 1)])
-
-        def lists():
-            yield tt(R("fd"), R("MS0", 0, 256), R("thd"), OP.is_lt)
-            yield tt(R("fG"), R("MS0", 0, 256), R("thr"), OP.is_lt)
-            yield scan(R("fs"), R("m0", 0, 256), R("fd"), OP.mult, OP.add)
-            yield tt(R("w1"), R("sF"), R("ks", 0, 16), OP.subtract)
-            yield tt(R("w2"), R("bs", *E16), R("ks", 16, 32), OP.subtract)
-            yield tt(R("w1"), R("w1"), R("fs", *E16), OP.mult)
-            yield tt(R("w2"), R("w2"), R("fs", *E16), OP.mult)
-            yield tt(R("w1"), R("w1"), R("ks", 0, 16), OP.add)
-            yield tt(R("w2"), R("w2"), R("ks", 16, 32), OP.add)
-            yield cp(R("sWU"), R("w1"))
-            yield cp(R("bWU"), R("w2"))
-            yield fill(R("ZRw", 0, 256), 0.0)
-            yield tt(R("d3"), R("RSI", *E16b), R("RSI", *E16), OP.subtract)
-            if not last:
-                yield cp(R("vS"), R("Xw", 0, S), R("sU"))
-                yield ts(R("vT"), R("vS"), -8.0, OP.add, 0.0, OP.max)
-
-        run_units([nr0], {0: fighters})
-        key(r1)
+            ts(R("EQ", offs[c], offs[c] + 256 - 16 * c), R("bG", 16 * c, 256), R("bL", c, c + 1), OP.is_equal)
+        for c in range(16):
+            mm(R("p_MS", 16 * c, 16 * c + 16), R("W2"), R("EQ", offs[c], offs[c] + 16), c == 0, c in (0, 15))
+            if c < 15:
+                mm(R("p_MS", 16 * c + 16, 256), R("W1"), R("EQ", offs[c] + 16, offs[c] + 256 - 16 * c), c == 0, False)
+        tt(R("nfG"), R("p_MS", 0, 256), R("thr"), OP.is_ge)
+        for x in range(2):
+            for h in range(2):
+                mm(R("p_MS", 256 + 16 * x + 8 * h, 264 + 16 * x + 8 * h), H("nfG", h), R("Sel", 0, 8))
         for h in range(2):
-            scan(H("FR", h), R("AK", 0, 128), H(kes[("R", h)], 1), OP.add, OP.min)
-            cp(H("kR", h), H(kes[("R", h)], 1))
-        key(nr0)
-        tt(R("rm"), R("FR"), R("kR"), OP.is_equal, R("BL", 16, 32))
-
-        def first():
-            weave(judge("NR", 0))
-            weave(lists())
-
-        def second():
-            key(ni1)
-            weave(judge("NI", 0))
-
-        run_units([ni0, ni1, nr1], {0: first, ni0: lambda: key(ni0), ni1: second})
-        key(nr1)
-        weave(judge("NI", 1))
-        weave(judge("NR", 1))
-        flip("rm", "SIT", "Ib")
-        scan(R("PC", 16, 272), R("fI"), R("fR"), OP.add, OP.subtract)
-        tt(R("d1"), R("NSI", *E16), R("NSR", *E16b), OP.subtract)
-        tt(R("dc"), R("PC", 31, 272, 16), R("PC", *E16), OP.subtract)
-        tt(R("d2"), R("NSI", *E16b), R("NSR", *E16), OP.subtract)
-        ts(R("won"), R("dc"), 0.0, OP.is_gt)
-        ts(R("d2"), R("d2"), 262144.0, OP.add)
-        tt(R("d3"), R("d3"), R("won"), OP.mult)
-        tt(R("d1"), R("d1"), R("won"), OP.mult)
-        tt(R("ch"), R("d3"), R("RSI", *E16), OP.add)
-        tt(R("zi"), R("d1"), R("NSR", *E16b), OP.add)
-        tt(R("mk2"), R("ch"), R("SIs"), OP.is_equal, BL)
-        tt(R("DL"), R("zi"), R("mk2"), OP.mult, BL)
-        flip("DL", "MS0", "If")
-        tt(R("d2"), R("d2"), R("won"), OP.mult)
-        tt(R("zr"), R("d2"), R("NSR", *E16), OP.add)
-        act(R("ez"), R("zr"), BL)
-        flip("ez", "BC0", "If")
-        tt(R(do), R("MS0", 0, 256), R("fG"), OP.mult)
-        send(R(do), "Din%d" % t, T.cores[(rank - 1 - t) % N], "aD%d" % t, "lD%d" % t)
-        act(R("zG"), R("BC0", 0, 256))
+            mm(R("p_MS", 288 + 8 * h, 296 + 8 * h), H("bG", h), R("Sel", 8, 16))
+        tt(R("ZK", 1, 64, 2), R("ZK", 1, 64, 2), R("p_MS", 256, 288), OP.add)
+        ts(R("dl"), R("p_MS", 288, 304), 65025.0, OP.add, 1.0, OP.min)
+        tt(R("Df", 0, 32), R("ZK", 0, 32), R("ZK", 32, 64), OP.subtract)
+        scan(R("fs"), R("DB"), R("nfG"), OP.add, OP.max)
+        cp(R("sF"), R("sU"))
+        ts(R("f1"), E("fs"), off, OP.subtract)
+        tt(R("f1"), R("f1"), R("ks"), OP.mult)
+        tt(R("sb", 0, 16), R("f1"), R("sF"), OP.max)
+        tt(R("sb", 16, 32), R("f1"), R("bL"), OP.max)
+        cp(R("WU"), R("sb"))
         if not last:
-            scat(R("Xw"), R("sWU"), R("vT"))
-        scat(R("ZRw"), R("bWU"), R("zG"))
-        tt(R("SIT", 256, 512), R("ZRw", 0, 256), R("SIT", 0, 256), OP.mult)
-        tt(R("Tm"), R("Mi"), R("SIT", 256, 512), OP.max)
-        ts(R("Tm2"), R("Tm"), 4095, OP.bitwise_and)
-        cp(R("SIT", 0, 256), R("Tm2"))
-        ts(R("BC1", 0, 256), R("zG"), 262144.0, OP.is_ge)
-        tt(R("ov"), R("bG"), R("BC1", 0, 256), OP.add)
-        ts(R("BC1", 256, 512), R("ov"), 256.0, OP.is_ge, -256.0, OP.mult)
-        tt(R("ow"), R("ov"), R("BC1", 256, 512), OP.add)
+            ts(R("vT"), R("Xw", 0, S), -8.0, OP.add, 0.0, OP.max, R("sU"))
+        for h in range(2):
+            kb, hb = "p_K%d" % h, "p_H%d" % h
+            keys("vN", h, [("NI", "CI"), ("NR", "CB")])
+            c = (512 * h, 512 * h + 512)
+            scan(R("FN", *c), R("AK"), R(kb), OP.add, OP.min)
+            tt(H("fI", h), H(kb, 0), R(th), OP.is_lt)
+            tt(H("fR", h), H(kb, 2), R(th), OP.is_lt)
+            tt(R("NE", *c), R(kb), R("FN", *c), OP.not_equal)
+            for x, slot in enumerate((2, 3, 1, 0)):
+                scan(H("NS", 2 * slot + h), H("NE", 4 * h + x), H(hb, 2), OP.mult, OP.min)
+        if not last:
+            scat(R("Xw"), R("WU", 0, 16), R("vT"))
+        scan(R("PC", 16, 272), R("fI"), R("fR"), OP.add, OP.subtract)
+        tt(R("won"), E("PC", 16), E("PC", 0, 256), OP.is_gt)
+        ts(R("r3"), E("NS"), R4096, OP.add, R4096, OP.subtract)
+        tt(R("ZK", 64, 128), E("NS"), R("r3"), OP.subtract)
+        tt(R("Df", 32, 64), R("ZK", 96, 128), R("ZK", 64, 96), OP.subtract)
+        tt(R("Pr"), R("won"), R("Df"), OP.mult, R("WL"))
+        tt(R(do, 0, 64), R("Pr"), R("ZK", 32, 96), OP.add)
+        send(R(do, 0, 48), "Din%d" % t, -1 - t, "aD%d" % t, "lD%d" % t)
+        tt(R(do, 64, 80), R("won"), R("dl"), OP.mult)
+        if not last:
+            tt(R("wf"), R("won"), R("p_MS", 256, 272), OP.is_gt)
+        turned("TP", R(do, 48, 80), 304)
+        for h in range(2):
+            mm(H("p_H1", h), H("WZ", h, 0, 32), R("TP", 0, 128, 1, 32))
+        for h in range(2):
+            mm(H("p_H1", 2 + h), R("Ib"), H("bG", h), True, False)
+            mm(H("p_H1", 2 + h), H("WO", h, 0, 32), R("TP", 0, 128, 1, 32), False, True)
+        act(R("zG"), R("p_H1", 0, 256), None, AF.Identity, MID + 4096)
+        act(R("ow"), R("p_H1", 256, 512))
+        scat(R(zr), R("WU", 16, 32), R("zG"))
+        scat(R("OWw"), R("WU", 0, 16), R("ow"))
         if last:
-            scat(R("OWw"), R("sWU"), R("ow"))
-            waits("G", need("G", [R("OWw", 0, S)], []))
-            g.dma_start(T.yown[:, :], T.c_OWw[0::16, 0:S]).then_inc(T.sem.dyo, 16)
-            total["dyo"] = 16
-        tt(R("Tm"), R("Din%d" % t), R("SIT", 0, 256), OP.max)
+            dma("dyo", [(T.yown[:, :], T.c_OWw[0::16, 0:S])], [R("OWw", 0, S)], [], LOAD + 1.5, "G")
+        for h in range(2):
+            keys("vR", h, [("R", "CR")])
+            scan(H("FR", h), R("AK", 0, 128), H("p_K%d" % h, 1), OP.add, OP.min)
+        places("KK", E("FR"), 16)
+        turned("TR", R("KK"), 0)
+        row = R("one", 0, 256, 1, 1)
+        mm(R("p_H0", 0, 256), R("cq", 0, 128, 1, 1), row, True, False)
+        mm(R("p_H0", 0, 256), R("If"), R(zr, 0, 256), False, False)
+        for h in range(2):
+            mm(H("p_H0", h), H("WY", h, 0, 32), R("TR", 0, 128, 1, 32), False, h == 1)
+        tt(R("x1"), R("Mi"), R("p_H0", 0, 256), OP.max)
+        turned("TY", R("Din%d" % t), 128)
+        mm(R("p_H1", 0, 256), R("cq", 0, 128, 1, 1), row, True, False)
+        mm(R("p_H1", 0, 256), one, R("cc", 0, 256, 1, 1), False, False)
+        for h in range(2):
+            mm(H("p_H1", h), H("WY", h, 0, 48), R("TY", 0, 128, 1, 48), False, h == 1)
+        tt(R("Tm"), R("x1"), R("p_H1", 0, 256), OP.max)
         ts(R("Mi"), R("Tm"), 4095, OP.bitwise_and)
         if last:
             cp(R("Mo"), R("Mi"))
-            dma("dy", [(T.ym[:, :], T.c_Mo[:, :])], [R("Mo")], [])
+            dma("dy", [(T.ym[:, :], T.c_Mo[:, :])], [R("Mo")], [], LOAD)
         else:
             cp(R("Mu%d" % (t + 1)), R("Mi"))
-            send(R("Mu%d" % (t + 1)), "Lin%d" % (t + 1), T.cores[(rank + 2 + t) % N], "aL%d" % (t + 1), "lL%d" % (t + 1))
-            scat(R("OWw"), R("sWU"), R("ow"))
-            tt(R("wf"), R("BC1", 0, 256), R("fG"), OP.mult)
-            rsum(R("wc"), R("wf"))
-            mm(R("MS0", 0, 1), R("o6"), R("wc"))
-            cp(R("wi"), R("MS0", 0, 1))
-            ts(R("wj"), R("wi"), 63, OP.bitwise_and)
-            ts(R("w16"), R("wj"), 16.0, OP.mult)
+            send(R("Mu%d" % (t + 1)), "Lin%d" % (t + 1), 2 + t, "aL%d" % (t + 1), "lL%d" % (t + 1))
+            for c in range(16):
+                mm(R("p_MS", 440, 441), R("one", 0, 128), R("wf", c, c + 1), c == 0, c == 15)
+            cp(R("wI", 0, 1), R("p_MS", 440, 441))
+            ts(R("wI", 8, 9), R("wI", 0, 1), 63, OP.bitwise_and)
+            ts(R("w16"), R("wI", 8, 9), 16.0, OP.mult)
             ts(R("TH"), R("TH0"), R("w16"), OP.add)
+
+    op("X", None, [], [], 0.0, ("dy", 16), 0.0, [i for i, o in enumerate(ops) if o["sem"]])
+    n = len(ops)
+    before = [{a: ops[a]["late"] + (SYNC if s else 0.0) for a, s in o["dep"].items()} for o in ops]
+    behind = [{} for _ in range(n)]
+    for i in range(n):
+        for a, x in before[i].items():
+            behind[a][i] = x
+
+    def lay(first, then, way):
+        left = [len(x) for x in first]
+        can, end, order = [0.0] * n, [0.0] * n, []
+        free = {q: 0.0 for q in "VSPGYX"}
+        ready = {q: [i for i in range(n) if ops[i]["q"] == q and not left[i]] for q in free}
+        while len(order) < n:
+            best = None
+            for q in free:
+                if ready[q]:
+                    i = max(ready[q], key=lambda j: (way[j] - LOOK * max(0.0, can[j] - free[q]), -j))
+                    st = max(free[q], can[i])
+                    if best is None or st < best[0]:
+                        best = (st, q, i)
+            st, q, i = best
+            ready[q].remove(i)
+            order.append(i)
+            end[i] = free[q] = st + ops[i]["us"]
+            for j, x in then[i].items():
+                can[j] = max(can[j], end[i] + x)
+                left[j] -= 1
+                if not left[j]:
+                    ready[ops[j]["q"]].append(j)
+        return order, end
+
+    if not ORDER:
+        way = [0.0] * n
+        for i in range(n - 1, -1, -1):
+            way[i] = ops[i]["us"] + max([x + way[j] for j, x in behind[i].items()] + [0.0])
+        tries = []
+        for _ in range(TURNS):
+            order, end = lay(before, behind, way)
+            tries.append((max(end), order))
+            way = lay(behind, before, end)[1]
+        ORDER.extend(min(tries)[1])
+
+    done = {}
+    count = {q: 0 for q in "VSPG"}
+    known = {q: {} for q in "VSPGYX"}
+    snap = {}
+    total = {}
+    for i in ORDER:
+        o = ops[i]
+        q = o["q"]
+        if q != "X":
+            nd = {}
+            for a, s in o["dep"].items():
+                if s and done[a][1] > nd.get(done[a][0], (0, 0))[0]:
+                    nd[done[a][0]] = (done[a][1], a)
+            for s in sorted(nd, key=lambda s: -nd[s][1]):
+                if known[q].get(s, 0) < nd[s][0]:
+                    Q[q].wait_ge(T.sem[s], nd[s][0])
+                    known[q][s] = nd[s][0]
+                    for s2, n2 in snap[nd[s][1]].items():
+                        known[q][s2] = max(known[q].get(s2, 0), n2)
+            inst = o["fn"]()
+        snap[i] = dict(known[q]) if q != "X" else {}
+        if o["sem"] is None:
+            count[q] += 1
+            inst.then_inc(T.sem["q" + q], 1)
+            done[i] = ("q" + q, count[q])
+        else:
+            done[i] = o["sem"]
+        total[done[i][0]] = done[i][1]
     for s in sorted(total):
         if known["G"].get(s, 0) < total[s]:
             g.wait_ge(T.sem[s], total[s])

@@ -7,11 +7,15 @@ MID = 1088.0
 BIG = 16384.0
 R1, R16, R4096 = 1.5 * 2 ** 23, 1.5 * 2 ** 27, 1.5 * 2 ** 35
 
-ON_V = {"I": (8, 8), "NI": (0, 0), "NR": (16, 16), "R": (0, 0)}
-GATHER_V = {"vR": (1,), "vI": (1,), "vN": ()}
+ON_V = {"I": (8, 8), "NI": (8, 8), "NR": (8, 8), "R": (0, 0)}
+GATHER_V = "R2 I1"
+PLAN = "set I0 I1 sI0 sI1 I2 I3 sI2 sI3 dI0 pI0 dI1 pI1 R0 R1 sR0 sR1 R2 R3 sR2 sR3 b0 N0 N1 b1 N2 N3 oI dN0 EQ dN1 pN0 pN1 fin loc back dR0 dR1 pR lists X own w"
 SYNC, HOP, LOAD = 0.2, 2.3, 1.6
-LOOK = 5.0
-TURNS = 6
+TURNS = 2
+EARLY = {}
+SWAP = 0
+FIRST = 1.5
+CUT = {"vR": 64, "vI": 64, "vN": 64}
 ORDER = []
 
 SCRATCH = {}
@@ -23,10 +27,10 @@ def _d(name, where, shape, dtype):
 
 
 for _t, _l in (
-        ("bfloat16", "Xw:2432 OWw:2432 ob:136 vR:4096 vI:4096 vN:4096 mxA:2048 mnA:2048 mxB:2048 mnB:2048 CR:256 CI:256 CB:256 "
-                     "mA:2048 mB:2048 mC:2048 mD:2048 bG:256 EQ:2176 nfG:256 vT:256 fI:256 fR:256 PC:272 ow:256 NE:1024 wf:16 "
+        ("bfloat16", "Xw:2432 OWw:2432 ob:136 vR:4096 vI:4096 vN:4096 mxR:4096 mnR:4096 CR:256 CI:256 CB:256 "
+                     "mxI:4096 mnI:4096 mI:4096 mR:4096 mNI:4096 mNR:4096 bG:256 EQ:2176 nfG:256 vT:256 fI:256 fR:256 PC:272 ow:256 NE:1024 wf:16 "
                      "one:256 m0:1024 a0:1024 AK:512 Ib:128 Nb:128 H1:128 H2:128 BK:256 BK1:256 BC:256 BC4:256 BC8:256 BC12:256 "
-                     "BM:16 BV:16 BA:16 KR:512 TG:128 MI:256 DB:256 D1:256 W1:128 W2:128 Sel:16 kw:256 WY:256 WZ:256 WO:256 "
+                     "BM:16 BV:32 BA:16 KR:512 TG:128 MI:256 DB:256 D1:256 W1:128 W2:128 Sel:16 kw:256 WY:256 WZ:256 WO:256 "
                      "cq:128 cq1:128 cc:256"),
         ("float16", "SF:256 SN:256 ex:256 bs:256 fs:256 TP:128 TR:128 TY:128 KK:32"),
         ("float32", "ZR0:2432 ZR1:2432 ZR2:2432 Mo:256 FI:512 FR:256 FN:1024 RS:256 NS:1024 x1:256 zG:256 TH:128 TH0:128 ZK:128 "
@@ -84,7 +88,9 @@ def rank_program(g, core, T, topo):
     def E(name, c0=0, c1=None):
         return R(name, c0 + 15, c1, 16)
 
-    def op(queue, fn, reads, writes, us, sem=None, late=0.0, after=()):
+    opened, todo = {}, {}
+
+    def op(queue, fn, reads, writes, us, sem=None, late=0.0, after=(), sum_=None):
         me = len(ops)
         dep = {a: True for a in after}
         for regs, wr in ((reads, False), (writes, True)):
@@ -96,18 +102,19 @@ def rank_program(g, core, T, topo):
                         cur, prev = [], cur
                     for a in prev:
                         dep[a] = True
-                    if queue == "P" and cur and cur[-1] != me:
-                        dep.setdefault(cur[-1], False)
+                    if queue == "P":
+                        for a in (cur if sum_ == me else [sum_]):
+                            dep.setdefault(a, False)
                     turn[r[1]] = (queue, cur + [me] if me not in cur else cur, prev)
                 for (c0, c1, a, w) in acc.get(r[1], []):
-                    if c0 >= r[3] or r[2] >= c1 or not (w or wr) or a == me:
+                    if c0 >= r[3] or r[2] >= c1 or not (w or wr) or a == me or (ps and ops[a]["q"] == queue == "P"):
                         continue
                     own = ops[a]["q"] == queue and ops[a]["sem"] is None and sem is None
                     if own and (not w or queue == "P" or (ps and wr)):
                         dep.setdefault(a, False)
                     else:
                         dep[a] = True
-        ops.append({"q": queue, "fn": fn, "us": us, "sem": sem, "late": late, "dep": dep})
+        ops.append({"q": queue, "fn": fn, "us": us, "sem": sem, "late": late, "dep": dep, "part": tuple(now)})
         for regs, wr in ((reads, False), (writes, True)):
             for r in regs:
                 lst = acc.get(r[1], [])
@@ -117,6 +124,10 @@ def rank_program(g, core, T, topo):
         return me
 
     CY = 0.00083
+    now = [0, "set"]
+
+    def part(name):
+        now[1] = name
 
     def narrow(*rs):
         return 0.5 if all(WIDE[SCRATCH[r[1]][2]] == 2 for r in rs) else 1
@@ -131,6 +142,8 @@ def rank_program(g, core, T, topo):
         return 0.06 + 1.56 * CY * out[4]
 
     def act(out, in_, off=None, func=AF.Copy, bias=None):
+        if off and now[1] in GATHER_V.split():
+            return cp(out, in_, off)
         x = src(in_, off)
         fn = (lambda: g.scalar.activation(out[0], x, func)) if bias is None else (lambda: g.scalar.activation(out[0], x, func, bias))
         op("S", fn, [in_] + ([off] if off else []), [out], gat(out) if off else cyc(out[4]))
@@ -166,9 +179,16 @@ def rank_program(g, core, T, topo):
     def fill(out, x):
         op("V", lambda: g.vector.memset(out[0], x), [], [out], cyc(out[4] * narrow(out)))
 
-    def mm(out, l, r, start=True, stop=True):
-        op("P", lambda: g.tensor.matmul(out[0], l[0], r[0], start, stop), [l, r], [out],
-           max(min(64, l[4]), r[4]) * CY / 2 * (4 if SCRATCH[l[1]][2] == "float32" else 1))
+    def mm(out, l, r, start=True, _=None):
+        if start:
+            opened[out[1]] = len(ops)
+        a = opened[out[1]]
+        todo[a] = todo.get(a, 0) + 1
+
+        def fn():
+            todo[a] -= 1
+            return g.tensor.matmul(out[0], l[0], r[0], start, not todo[a])
+        op("P", fn, [l, r], [out], max(min(64, l[4]), r[4]) * CY / 2 * (4 if SCRATCH[l[1]][2] == "float32" else 1), sum_=a)
 
     def rsum(out, in_):
         op("V", lambda: g.vector.tensor_reduce(out[0], in_[0], AxisListType.X, OP.add), [in_], [out], cyc(in_[4]))
@@ -190,7 +210,7 @@ def rank_program(g, core, T, topo):
         eng = topo.engines(core, dst)[:8]
         rid, pid = topo.addr(dst, core)
         s = op("G", lambda: g.remote_dma(T[land][:], buf[0], T.sem[asem], T.sem[lsem], pid, rid, sum(1 << e for e in eng)),
-               [buf], [], 0.3, (lsem, len(eng)), HOP)
+               [buf], [], 0.3, (lsem, len(eng)), HOP + (FIRST if land == "Lin0" else 0))
         op("X", None, [], [R(land)], 0.0, (asem, len(topo.engines(frm, core)[:8])), 0.0, [s])
 
     a = dma("dm", [(T.c_Mi[:, :], T.m0[:, :])], [], [R("Mi")], LOAD, "S")
@@ -218,6 +238,7 @@ def rank_program(g, core, T, topo):
     for name, x in (("BM", 32.0), ("BV", -16.0), ("BA", 16.0)):
         ts(R(name, 0, 8), CC, x, OP.mult)
         ts(R(name, 8, 16), CC, -x, OP.mult)
+    cp(R("BV", 16, 32), R("BV", 0, 16))
     ts(H("BC", 0), H("BK", 0), -16.0, OP.mult)
     ts(H("BC", 1), H("BK", 0), 16.0, OP.mult)
     for n in sorted(set(sum(ON_V.values(), ())) - {0, 16}):
@@ -274,17 +295,21 @@ def rank_program(g, core, T, topo):
 
     def gather(v, lst, h):
         for c in range(2 * h, 2 * h + 2):
-            (cp if c in GATHER_V[v] else act)(R(v, c * 1024, c * 1024 + 1024), R("Xw", 0, S), R(lst, c * 64, c * 64 + 64))
+            part(v[1] + str(c))
+            for a in range(c * 64, c * 64 + 64, CUT[v]):
+                act(R(v, a * 16, (a + CUT[v]) * 16), R("Xw", 0, S), R(lst, a, a + CUT[v]))
 
     def centre(v, C, h):
-        mx, mn = ("mxA", "mnA") if h == 0 else ("mxB", "mnB")
-        for c in range(2):
-            x = R(v, h * 2048 + c * 1024, h * 2048 + c * 1024 + 1024)
-            scan(R(mx, c * 1024, c * 1024 + 1024), R("m0"), x, OP.mult, OP.max)
-            scan(R(mn, c * 1024, c * 1024 + 1024), R("a0"), x, OP.add, OP.min)
-        out = H("p_H%d" % h, 3)
-        mm(out, R("H1"), E(mx), True, False)
-        mm(out, R("H2"), E(mn), False, True)
+        mx, mn = "mx" + v[1], "mn" + v[1]
+        for c in range(2 * h, 2 * h + 2):
+            part("s%s%d" % (v[1], c))
+            n = 16 * CUT[v]
+            for a in range(c * 1024, c * 1024 + 1024, n):
+                scan(R(mx, a, a + n), R("m0", 0, n), R(v, a, a + n), OP.mult, OP.max)
+                scan(R(mn, a, a + n), R("a0", 0, n), R(v, a, a + n), OP.add, OP.min)
+        out = H("p_MS", h) if v == "vR" else H("p_H%d" % h, 3)
+        mm(out, R("H1"), E(mx, 2048 * h, 2048 * h + 2048))
+        mm(out, R("H2"), E(mn, 2048 * h, 2048 * h + 2048), False)
         ts(H(C, h), out, R1, OP.add, R1, OP.subtract)
 
     def sites(sf, h):
@@ -294,23 +319,27 @@ def rank_program(g, core, T, topo):
 
     cnt = {"D": 0, "m": 0}
 
-    def keys(v, h, units):
-        kb = "p_K%d" % h
+    def outermost(h):
+        kb, o = ("p_MS", 256) if h in EARLY else ("p_K%d" % h, 0)
+        keys("vR", h, [("R", "CR")], kb, o)
+        scan(H("FR", h), R("AK", 0, 128), H(kb, 1, o), OP.add, OP.min)
+
+    def keys(v, h, units, kb, o=0):
         w = 256 * len(units)
         col = lambda k: R(v, h * 2048 + k, h * 2048 + 2048, 16)
-        ms = []
+        part("d%s%d" % (v[1], h))
         for u, (name, C) in enumerate(units):
-            ms.append("m" + "ABCD"[cnt["m"] % 4])
-            cnt["m"] += 1
             if ON_V[name][h]:
                 mm(H("p_H%d" % h, u), R("Ib"), H(C, h))
-        mm(R(kb, 0, w), one, R("KR", 0, w, 1, 1), True, False)
+        mm(R(kb, o, o + w), one, R("KR", 0, w, 1, 1))
         for u, (name, C) in enumerate(units):
             n = ON_V[name][h]
             if n:
-                mm(R(kb, 256 * u, 256 * u + 256), H(C, h), R("BC" if n == 16 else "BC%d" % n), False, False)
-            for k in range(n):
-                mm(R(kb, 256 * u + k, 256 * u + 256, 16), col(k), R("BV"), False, False)
+                mm(R(kb, o + 256 * u, o + 256 * u + 256), H(C, h), R("BC" if n == 16 else "BC%d" % n), False)
+        for k in range(16):
+            us = [u for u, (name, C) in enumerate(units) if k < ON_V[name][h]]
+            if us:
+                mm(R(kb, o + 256 * us[0] + k, o + 256 * us[-1] + 256, 16), col(k), R("BV", 0, 16 * len(us)), False)
         todo = [(b, u) for b in range(4) for u in range(len(units))]
         todo.sort(key=lambda x: x[0] - (ON_V[units[x[1]][0]][h] // 4 if 4 * x[0] >= ON_V[units[x[1]][0]][h] else 0))
         for b, u in todo:
@@ -318,45 +347,52 @@ def rank_program(g, core, T, topo):
             vec = 4 * b < ON_V[name][h]
             if vec:
                 for k in range(4 * b, 4 * b + 4):
-                    tt(H(ms[u], k), col(k), H("p_H%d" % h, u), OP.max)
+                    tt(H("m" + name, 16 * h + k), col(k), H("p_H%d" % h, u), OP.max)
             else:
                 d = "p_D%d" % (cnt["D"] % 3)
                 cnt["D"] += 1
                 for k in range(4):
-                    mm(H(d, k), R("Ib"), H(C, h), True, False)
-                    mm(H(d, k), R("Nb"), col(4 * b + k), False, True)
-                act(R(ms[u], b * 512, b * 512 + 512), R(d), None, AF.Abs)
+                    mm(H(d, k), R("Ib"), H(C, h))
+                    mm(H(d, k), R("Nb"), col(4 * b + k), False)
+                act(R("m" + name, h * 2048 + b * 512, h * 2048 + b * 512 + 512), R(d), None, AF.Abs)
             for k in range(4 * b, 4 * b + 4):
-                mm(R(kb, 256 * u + k, 256 * u + 256, 16), H(ms[u], k), R("BM" if vec else "BA"), False,
-                   (b, u) == todo[-1] and k == 4 * b + 3)
+                mm(R(kb, o + 256 * u + k, o + 256 * u + 256, 16), H("m" + name, 16 * h + k), R("BM" if vec else "BA"), False)
 
     def places(out, ends, n):
         ts(R("r2", 0, n), ends, R16, OP.add, R16, OP.subtract)
         tt(R(out, 0, 2 * n, 2), ends, R("r2", 0, n), OP.subtract)
         tt(R(out, 1, 2 * n, 2), R(out, 0, 2 * n, 2), R(out, 0, 2 * n, 2), OP.mult)
 
-    def turned(out, in_, c0):
-        mm(R("p_MS", c0, c0 + 128, 1, in_[4]), in_, R("Ib"))
-        cp(R(out, 0, 128, 1, in_[4]), R("p_MS", c0, c0 + 128, 1, in_[4]))
+    def turned(out, in_, bank, c0):
+        mm(R(bank, c0, c0 + 128, 1, in_[4]), in_, R("Ib"))
+        cp(R(out, 0, 128, 1, in_[4]), R(bank, c0, c0 + 128, 1, in_[4]))
 
     for t in range(RO):
         last = t == RO - 1
+        now[0] = t
         mu, li, do, zr = "Mu%d" % t, "Lin%d" % t, "Do%d" % t, "ZR%d" % t
         th = "TH" if t else "TH0"
         for h in range(2):
             gather("vR", mu, h)
             centre("vR", "CR", h)
+        part("sI0")
         ts(R("SF"), R(li), -MID, OP.add)
         for h in range(2):
-            gather("vI", li, h)
             sites("SF", h)
+        for h in range(2):
+            gather("vI", li, h)
             centre("vI", "CI", h)
         for h in range(2):
             kb, hb = "p_K%d" % h, "p_H%d" % h
-            keys("vI", h, [("I", "CI")])
+            for x in EARLY:
+                if EARLY[x] == h:
+                    outermost(x)
+            keys("vI", h, [("I", "CI")], kb)
+            part("oI")
+            scan(H("FI", h), R("AK", 0, 128), H(kb, 1), OP.add, OP.min)
+            part("pI%d" % h)
             scan(H("FI", 2 + h), R("AK", 0, 128), H(kb, 0), OP.add, OP.min)
             tt(H("NE", h), H(kb, 0), H("FI", 2 + h), OP.not_equal)
-            scan(H("FI", h), R("AK", 0, 128), H(kb, 1), OP.add, OP.min)
             scan(H("RS", h), H("NE", h), H(hb, 2), OP.mult, OP.min)
             c = (8 * h, 8 * h + 8)
             ends = E("RS", 128 * h, 128 * h + 128)
@@ -366,16 +402,19 @@ def rank_program(g, core, T, topo):
             mm(R(hb, 384, 392), H("ex", h), CC)
             ts(R("sU", *c), R(hb, 384, 392), MID, OP.add)
             cp(H("nU", h), R("NBw"), R("sU", *c))
-            act(H("bG", h), R("OWw", 0, S), R("sU", *c))
             gather("vN", "nU", h)
+            part("b%d" % h)
+            act(H("bG", h), R("OWw", 0, S), R("sU", *c))
             ts(H("SN", h), H("nU", h), -MID, OP.add)
             sites("SN", h)
             scan(H("bs", h), H("DB", h), H("bG", h), OP.add, OP.max)
             ends = E("bs", 128 * h, 128 * h + 128)
             ts(R("bU", *c), ends, off, OP.subtract)
             act(H("CB", h), R("CR"), R("bU", *c))
-        ts(R("bL"), E("bs"), off, OP.subtract)
+        part("oI")
         places("ZK", E("FI"), 32)
+        part("EQ")
+        ts(R("bL"), E("bs"), off, OP.subtract)
         offs = [sum(256 - 16 * x for x in range(c)) for c in range(16)]
         for c in range(16):
             ts(R("EQ", offs[c], offs[c] + 256 - 16 * c), R("bG", 16 * c, 256), R("bL", c, c + 1), OP.is_equal)
@@ -392,6 +431,7 @@ def rank_program(g, core, T, topo):
         tt(R("ZK", 1, 64, 2), R("ZK", 1, 64, 2), R("p_MS", 256, 288), OP.add)
         ts(R("dl"), R("p_MS", 288, 304), 65025.0, OP.add, 1.0, OP.min)
         tt(R("Df", 0, 32), R("ZK", 0, 32), R("ZK", 32, 64), OP.subtract)
+        part("lists")
         scan(R("fs"), R("DB"), R("nfG"), OP.add, OP.max)
         cp(R("sF"), R("sU"))
         ts(R("f1"), E("fs"), off, OP.subtract)
@@ -403,7 +443,11 @@ def rank_program(g, core, T, topo):
             ts(R("vT"), R("Xw", 0, S), -8.0, OP.add, 0.0, OP.max, R("sU"))
         for h in range(2):
             kb, hb = "p_K%d" % h, "p_H%d" % h
-            keys("vN", h, [("NI", "CI"), ("NR", "CB")])
+            for x in EARLY:
+                if EARLY[x] == 2 + h:
+                    outermost(x)
+            keys("vN", h, [("NI", "CI"), ("NR", "CB")], kb)
+            part("pN%d" % h)
             c = (512 * h, 512 * h + 512)
             scan(R("FN", *c), R("AK"), R(kb), OP.add, OP.min)
             tt(H("fI", h), H(kb, 0), R(th), OP.is_lt)
@@ -412,7 +456,9 @@ def rank_program(g, core, T, topo):
             for x, slot in enumerate((2, 3, 1, 0)):
                 scan(H("NS", 2 * slot + h), H("NE", 4 * h + x), H(hb, 2), OP.mult, OP.min)
         if not last:
+            part("X")
             scat(R("Xw"), R("WU", 0, 16), R("vT"))
+        part("fin")
         scan(R("PC", 16, 272), R("fI"), R("fR"), OP.add, OP.subtract)
         tt(R("won"), E("PC", 16), E("PC", 0, 256), OP.is_gt)
         ts(R("r3"), E("NS"), R4096, OP.add, R4096, OP.subtract)
@@ -421,10 +467,12 @@ def rank_program(g, core, T, topo):
         tt(R("Pr"), R("won"), R("Df"), OP.mult, R("WL"))
         tt(R(do, 0, 64), R("Pr"), R("ZK", 32, 96), OP.add)
         send(R(do, 0, 48), "Din%d" % t, -1 - t, "aD%d" % t, "lD%d" % t)
-        tt(R(do, 64, 80), R("won"), R("dl"), OP.mult)
         if not last:
+            part("w")
             tt(R("wf"), R("won"), R("p_MS", 256, 272), OP.is_gt)
-        turned("TP", R(do, 48, 80), 304)
+        part("loc")
+        tt(R(do, 64, 80), R("won"), R("dl"), OP.mult)
+        turned("TP", R(do, 48, 80), "p_H0", 0)
         for h in range(2):
             mm(H("p_H1", h), H("WZ", h, 0, 32), R("TP", 0, 128, 1, 32))
         for h in range(2):
@@ -433,26 +481,29 @@ def rank_program(g, core, T, topo):
         act(R("zG"), R("p_H1", 0, 256), None, AF.Identity, MID + 4096)
         act(R("ow"), R("p_H1", 256, 512))
         scat(R(zr), R("WU", 16, 32), R("zG"))
+        part("own")
         scat(R("OWw"), R("WU", 0, 16), R("ow"))
         if last:
             dma("dyo", [(T.yown[:, :], T.c_OWw[0::16, 0:S])], [R("OWw", 0, S)], [], LOAD + 1.5, "G")
         for h in range(2):
-            keys("vR", h, [("R", "CR")])
-            scan(H("FR", h), R("AK", 0, 128), H("p_K%d" % h, 1), OP.add, OP.min)
+            if h not in EARLY:
+                outermost(h)
+        part("pR")
         places("KK", E("FR"), 16)
-        turned("TR", R("KK"), 0)
+        turned("TR", R("KK"), "p_MS", 0)
         row = R("one", 0, 256, 1, 1)
         mm(R("p_H0", 0, 256), R("cq", 0, 128, 1, 1), row, True, False)
         mm(R("p_H0", 0, 256), R("If"), R(zr, 0, 256), False, False)
         for h in range(2):
             mm(H("p_H0", h), H("WY", h, 0, 32), R("TR", 0, 128, 1, 32), False, h == 1)
-        tt(R("x1"), R("Mi"), R("p_H0", 0, 256), OP.max)
-        turned("TY", R("Din%d" % t), 128)
-        mm(R("p_H1", 0, 256), R("cq", 0, 128, 1, 1), row, True, False)
-        mm(R("p_H1", 0, 256), one, R("cc", 0, 256, 1, 1), False, False)
+        part("back")
+        turned("TY", R("Din%d" % t), "p_K0", 256)
+        mm(R("p_K0", 0, 256), R("cq", 0, 128, 1, 1), row)
+        mm(R("p_K0", 0, 256), one, R("cc", 0, 256, 1, 1), False)
         for h in range(2):
-            mm(H("p_H1", h), H("WY", h, 0, 48), R("TY", 0, 128, 1, 48), False, h == 1)
-        tt(R("Tm"), R("x1"), R("p_H1", 0, 256), OP.max)
+            mm(H("p_K0", h), H("WY", h, 0, 48), R("TY", 0, 128, 1, 48), False)
+        tt(R("x1"), R("Mi"), R("p_K0" if SWAP else "p_H0", 0, 256), OP.max)
+        tt(R("Tm"), R("x1"), R("p_H0" if SWAP else "p_K0", 0, 256), OP.max)
         ts(R("Mi"), R("Tm"), 4095, OP.bitwise_and)
         if last:
             cp(R("Mo"), R("Mi"))
@@ -460,6 +511,7 @@ def rank_program(g, core, T, topo):
         else:
             cp(R("Mu%d" % (t + 1)), R("Mi"))
             send(R("Mu%d" % (t + 1)), "Lin%d" % (t + 1), 2 + t, "aL%d" % (t + 1), "lL%d" % (t + 1))
+            part("w")
             for c in range(16):
                 mm(R("p_MS", 440, 441), R("one", 0, 128), R("wf", c, c + 1), c == 0, c == 15)
             cp(R("wI", 0, 1), R("p_MS", 440, 441))
@@ -475,40 +527,36 @@ def rank_program(g, core, T, topo):
         for a, x in before[i].items():
             behind[a][i] = x
 
-    def lay(first, then, way):
+    def lay(first, then, rank_):
         left = [len(x) for x in first]
-        can, end, order = [0.0] * n, [0.0] * n, []
-        free = {q: 0.0 for q in "VSPGYX"}
-        ready = {q: [i for i in range(n) if ops[i]["q"] == q and not left[i]] for q in free}
-        while len(order) < n:
-            best = None
-            for q in free:
-                if ready[q]:
-                    i = max(ready[q], key=lambda j: (way[j] - LOOK * max(0.0, can[j] - free[q]), -j))
-                    st = max(free[q], can[i])
-                    if best is None or st < best[0]:
-                        best = (st, q, i)
-            st, q, i = best
-            ready[q].remove(i)
-            order.append(i)
-            end[i] = free[q] = st + ops[i]["us"]
+        can, end = [0.0] * n, [0.0] * n
+        busy = {q: [] for q in "VSPGYX"}
+        ready = [i for i in range(n) if not left[i]]
+        while ready:
+            i = min(ready, key=lambda j: rank_[j])
+            ready.remove(i)
+            lst, st, us = busy[ops[i]["q"]], can[i], ops[i]["us"]
+            k = len(lst)
+            while k and lst[k - 1][1] > st:
+                k -= 1
+            while k < len(lst) and lst[k][0] < st + us - 1e-9:
+                st = max(st, lst[k][1])
+                k += 1
+            lst.insert(k, (st, st + us))
+            end[i] = st + us
             for j, x in then[i].items():
                 can[j] = max(can[j], end[i] + x)
                 left[j] -= 1
                 if not left[j]:
-                    ready[ops[j]["q"]].append(j)
-        return order, end
+                    ready.append(j)
+        return end
 
     if not ORDER:
-        way = [0.0] * n
-        for i in range(n - 1, -1, -1):
-            way[i] = ops[i]["us"] + max([x + way[j] for j, x in behind[i].items()] + [0.0])
-        tries = []
+        plan = PLAN.split()
+        end = lay(before, behind, [(o["part"][0], plan.index(o["part"][1]), i) for i, o in enumerate(ops)])
         for _ in range(TURNS):
-            order, end = lay(before, behind, way)
-            tries.append((max(end), order))
-            way = lay(behind, before, end)[1]
-        ORDER.extend(min(tries)[1])
+            end = lay(before, behind, [-x for x in lay(behind, before, [-x for x in end])])
+        ORDER.extend(sorted(range(n), key=lambda i: (end[i] - ops[i]["us"], end[i], i)))
 
     done = {}
     count = {q: 0 for q in "VSPG"}

@@ -4,18 +4,27 @@ S, L, RO = 2176, 256, 3
 OP = AluOpType
 AF = ActivationFunctionType
 MID = 1088.0
-BIG = 16384.0
-R1, R16, R4096 = 1.5 * 2 ** 23, 1.5 * 2 ** 27, 1.5 * 2 ** 35
+BIG = 4096
+KEY = 32.0
+R1, RKEY, R4096 = 1.5 * 2 ** 23, 1.5 * 2 ** 28, 1.5 * 2 ** 35
 
-ON_V = {"I": (8, 8), "NI": (8, 8), "NR": (8, 8), "R": (0, 0)}
+ON_V = {"I": (4, 4), "NI": (8, 8), "NR": (8, 12), "R": (8, 8)}
 GATHER_V = "R2 I1"
-PLAN = "set I0 I1 sI0 sI1 I2 I3 sI2 sI3 dI0 pI0 dI1 pI1 R0 R1 sR0 sR1 R2 R3 sR2 sR3 b0 N0 N1 b1 N2 N3 oI dN0 EQ dN1 pN0 pN1 fin loc back dR0 dR1 pR lists X own w"
-SYNC, HOP, LOAD = 0.2, 2.3, 1.6
-TURNS = 2
-EARLY = {}
-SWAP = 0
+PLAN = "R3 dR0 vT sR0 dI0 I3 own0 sI1 c0 EQ back b1 pI1 I1 dN0 R2 N0 R0 loc b0 pI0 dN1 I2 dI1 pN0 c1 N2 N1 sR2 sI2 R1 w set sR1 sI3 pN1 dR1 fin I0 oI N3 X sI0 pR own lists sR3"
+SCALAR = "own0 R0 R1 I0 I2 I3 dI0 R3 dI1 b0 N0 c0 b1 N2 c1 dN0 dN1 vT dR0 dR1"
+CUT = {"vR": 64, "vI": 64, "vN": 128}
+RUN = 512
+SYNC = {"V": 0.22, "S": 0.22, "P": 0.22}
+OWN = 0.22
+HOP = 2.6
 FIRST = 1.5
-CUT = {"vR": 64, "vI": 64, "vN": 64}
+LOAD = 1.9
+ISSUE = 0.3
+CY = 0.00083
+PE = 0.5
+GAT = 1.56
+ADDS = 0.0
+PADD = 0.0
 ORDER = []
 
 SCRATCH = {}
@@ -27,35 +36,35 @@ def _d(name, where, shape, dtype):
 
 
 for _t, _l in (
-        ("bfloat16", "Xw:2432 OWw:2432 ob:136 vR:4096 vI:4096 vN:4096 mxR:4096 mnR:4096 CR:256 CI:256 CB:256 "
-                     "mxI:4096 mnI:4096 mI:4096 mR:4096 mNI:4096 mNR:4096 bG:256 EQ:2176 nfG:256 vT:256 fI:256 fR:256 PC:272 ow:256 NE:1024 wf:16 "
-                     "one:256 m0:1024 a0:1024 AK:512 Ib:128 Nb:128 H1:128 H2:128 BK:256 BK1:256 BC:256 BC4:256 BC8:256 BC12:256 "
-                     "BM:16 BV:32 BA:16 KR:512 TG:128 MI:256 DB:256 D1:256 W1:128 W2:128 Sel:16 kw:256 WY:256 WZ:256 WO:256 "
-                     "cq:128 cq1:128 cc:256"),
-        ("float16", "SF:256 SN:256 ex:256 bs:256 fs:256 TP:128 TR:128 TY:128 KK:32"),
+        ("bfloat16", "Xw:2432 OWw:2432 ob:136 vR:4096 vI:4096 vN:4096 mxR:4096 mnR:4096 mxI:4096 mnI:4096 CR:256 CI:256 CB:256 "
+                     "mI:4096 mR:4096 mNI:4096 mNR:4096 bG:256 EQ:2176 nfG:256 vT:256 fI:256 fR:256 PC:272 ow:256 NE:1024 wf:16 "
+                     "one:256 m0:%d a0:%d " % (RUN, RUN) + "AK:128 Ib:128 Nb:128 H1:128 H2:128 BK:128 BK1:128 BC:256 BC4:256 "
+                     "BC8:256 BC12:256 sB:80 KR:512 TG:128 DB:128 D1:128 W1:128 W2:128 kw:256 WY:256 WX:256 WZ:256 WO:256 "
+                     "cq:128 cq1:128 cc:128 KK:32 TR:128"),
+        ("float16", "SF:256 SN:256 ex:256 bs:256 fs:256 TP:128 TY:128"),
         ("float32", "ZR0:2432 ZR1:2432 ZR2:2432 Mo:256 FI:512 FR:256 FN:1024 RS:256 NS:1024 x1:256 zG:256 TH:128 TH0:128 ZK:128 "
-                    "Df:64 Pr:64 sF32:256 pf:8 If:128 thr:256 pw:256 pv:256 ii:256 ks:16 o6:128 B8:128"),
-        ("int32", "NBw:2176 Mi:256 Tm:256 oi:136 pi:8 bi:16 thi:1 wI:16"),
-        ("uint16", "nU:256 sU16:64 BL:8 WL:4")):
+                    "sF32:288 wl:8 pf:8 If:128 thr:128 pw:128 pv:128 ii:128 MI:128 ks:16 o6:128 B8:128"),
+        ("int32", "NBw:2176 Mi:256 Tm:256 oi:136 pi:8 bi:8 thi:1 wI:16"),
+        ("uint16", "nU:256 sU16:64 BL:8 WL:8")):
     for _x in _l.split():
         _d("c_" + _x.split(":")[0], "sbuf", [128, int(_x.split(":")[1])], _t)
-for _k, (_n, _c) in enumerate((("sl", 16), ("r1", 16), ("sF", 16), ("bL", 16), ("won", 16), ("dl", 16), ("f1", 16), ("w16", 1),
-                               ("r2", 32), ("thf", 1), ("sb", 32), ("-", 1), ("r3", 64))):
-    ALIAS[_n] = ("c_sF32", 16 * _k, _c)
+for _b, _l in (("c_sF32", "sl:16 sF:16 bL:16 won:32 dl:16 f1:16 w16:16 rR:16 rI:32 rS:16 sb:32 rN:64"),
+               ("c_sB", "BM:16 BV:32 BA:16 Sel:16"), ("c_sU16", "sU:16 bU:16 WU:32")):
+    _o = 0
+    for _x in _l.split():
+        ALIAS[_x.split(":")[0]] = (_b, _o, int(_x.split(":")[1]))
+        _o += int(_x.split(":")[1])
 ALIAS["thf"] = ("c_pf", 7, 1)
-for _k, (_n, _c) in enumerate((("sU", 16), ("bU", 16), ("WU", 32))):
-    ALIAS[_n] = ("c_sU16", 16 * _k, _c)
 for _t in range(RO):
     _d("Mu%d" % _t, "sbuf", [128, 256], "uint16")
     _d("Lin%d" % _t, "sbuf", [128, 256], "uint16")
-    _d("Do%d" % _t, "sbuf", [128, 80], "float16")
-    _d("Din%d" % _t, "sbuf", [128, 48], "float16")
+    _d("Do%d" % _t, "sbuf", [128, 144], "float16")
+    _d("Din%d" % _t, "sbuf", [128, 96], "float16")
 for _n in ("D0", "D1", "D2", "K0", "K1", "H0", "H1", "MS"):
     _d("p_" + _n, "psum", [128, 512], "float32")
-_d("ownd", "dram", [8, S], "bfloat16")
 
-SEMAPHORES = (["qV", "qS", "qP", "qG", "dx", "dm", "dn", "do", "dod", "dor", "dth", "dy", "dyo"]
-              + [n + "%d" % t for n in ("aL", "aD", "lL", "lD") for t in range(RO)])
+SEMAPHORES = (["qV", "qS", "qP", "qG", "dx", "dm", "dn", "do", "dth", "dy0", "dy1", "dyo"]
+              + [n + "%d" % t for n in ("aL0", "aL1", "aD", "lL0", "lL1", "lD") for t in range(RO)])
 WIDE = {"float32": 4, "int32": 4, "bfloat16": 2, "float16": 2, "uint16": 2}
 
 
@@ -68,6 +77,8 @@ def rank_program(g, core, T, topo):
     ops = []
     acc = {}
     turn = {}
+    opened, todo = {}, {}
+    now = [0, "set"]
 
     def R(name, c0=0, c1=None, st=1, p1=128):
         o = 0
@@ -82,13 +93,11 @@ def rank_program(g, core, T, topo):
         ap = T[name][0:p1, c0:c1] if st == 1 else T[name][0:p1, c0:c1:st]
         return (ap, name, c0, c1, len(range(c0, c1, st)))
 
-    def H(name, h, o=0, p1=128):
-        return R(name, o + h * 128, o + h * 128 + 128, 1, p1)
+    def H(name, h, p1=128):
+        return R(name, h * 128, h * 128 + 128, 1, p1)
 
     def E(name, c0=0, c1=None):
         return R(name, c0 + 15, c1, 16)
-
-    opened, todo = {}, {}
 
     def op(queue, fn, reads, writes, us, sem=None, late=0.0, after=(), sum_=None):
         me = len(ops)
@@ -123,9 +132,6 @@ def rank_program(g, core, T, topo):
                 acc[r[1]] = lst + [(r[2], r[3], me, wr)]
         return me
 
-    CY = 0.00083
-    now = [0, "set"]
-
     def part(name):
         now[1] = name
 
@@ -139,14 +145,14 @@ def rank_program(g, core, T, topo):
         return a[0] if off is None else a[0].indirect(off[0])
 
     def gat(out):
-        return 0.06 + 1.56 * CY * out[4]
+        return 0.06 + GAT * CY * out[4]
 
     def act(out, in_, off=None, func=AF.Copy, bias=None):
         if off and now[1] in GATHER_V.split():
             return cp(out, in_, off)
         x = src(in_, off)
         fn = (lambda: g.scalar.activation(out[0], x, func)) if bias is None else (lambda: g.scalar.activation(out[0], x, func, bias))
-        op("S", fn, [in_] + ([off] if off else []), [out], gat(out) if off else cyc(out[4]))
+        op("S", fn, [in_] + ([off] if off else []), [out], gat(out) if off else cyc(out[4]) + ADDS)
 
     def cp(out, in_, off=None):
         x = src(in_, off)
@@ -161,17 +167,16 @@ def rank_program(g, core, T, topo):
         op("V", lambda: g.vector.tensor_tensor(out[0], x, b[0], o), [a, b] + ([off] if off else []), [out],
            gat(out) if off else cyc(out[4] * (1 if "p_" in (a[1][:2], b[1][:2]) else 2)))
 
-    def ts(out, a, s1, o1, s2=None, o2=None, off=None):
-        rd = [a] + ([off] if off else [])
-        x, x1 = src(a, off), s1
-        if isinstance(s1, tuple):
-            rd.append(s1)
-            x1 = s1[0]
-        us = gat(out) if off else cyc(out[4] * narrow(out, a))
+    def ts(out, a, s1, o1, s2=None, o2=None):
+        rd, x1 = ([a, s1], s1[0]) if isinstance(s1, tuple) else ([a], s1)
+        us = cyc(out[4] * narrow(out, a))
         if o2 is None:
-            op("V", lambda: g.vector.tensor_scalar(out[0], x, x1, None, o1), rd, [out], us)
+            op("V", lambda: g.vector.tensor_scalar(out[0], a[0], x1, None, o1), rd, [out], us)
         else:
-            op("V", lambda: g.vector.tensor_scalar(out[0], x, x1, s2, o1, o2), rd, [out], us)
+            op("V", lambda: g.vector.tensor_scalar(out[0], a[0], x1, s2, o1, o2), rd, [out], us)
+
+    def rnd(out, a, r):
+        ts(out, a, r, OP.add, r, OP.subtract)
 
     def scan(out, a, b, o1, o2):
         op("V", lambda: g.vector.tensor_tensor_scan(out[0], a[0], b[0], 0.0, o1, o2), [a, b], [out], cyc(out[4] * narrow(out, a, b)))
@@ -179,7 +184,7 @@ def rank_program(g, core, T, topo):
     def fill(out, x):
         op("V", lambda: g.vector.memset(out[0], x), [], [out], cyc(out[4] * narrow(out)))
 
-    def mm(out, l, r, start=True, _=None):
+    def mm(out, l, r, start=True):
         if start:
             opened[out[1]] = len(ops)
         a = opened[out[1]]
@@ -188,7 +193,7 @@ def rank_program(g, core, T, topo):
         def fn():
             todo[a] -= 1
             return g.tensor.matmul(out[0], l[0], r[0], start, not todo[a])
-        op("P", fn, [l, r], [out], max(min(64, l[4]), r[4]) * CY / 2 * (4 if SCRATCH[l[1]][2] == "float32" else 1), sum_=a)
+        op("P", fn, [l, r], [out], max(64, r[4] * (4 if SCRATCH[l[1]][2] == "float32" else 1)) * CY * PE + PADD, sum_=a)
 
     def rsum(out, in_):
         op("V", lambda: g.vector.tensor_reduce(out[0], in_[0], AxisListType.X, OP.add), [in_], [out], cyc(in_[4]))
@@ -199,173 +204,176 @@ def rank_program(g, core, T, topo):
     def asel(out, in_, pat, cmp_, base, mult=1, other=0.0):
         op("G", lambda: g.affine_select(out[0], in_[0], pat, cmp_, other, base, mult), [in_], [out], 0.17 + 2 * CY * out[4])
 
-    def dma(sem, pairs, reads, writes, late, queue="Y", after=()):
-        def fn():
-            for o, i in pairs:
-                Q[queue].dma_start(o, i).then_inc(T.sem[sem], 16)
-        return op(queue, fn, reads, writes, 0.05 * len(pairs), (sem, 16 * len(pairs)), late, after)
+    def dma(sem, out, in_, reads, writes, late, queue="Y", behind=None):
+        a = op(queue, lambda: Q[queue].dma_start(out, in_).then_inc(T.sem[sem], 16), reads, writes, ISSUE, (sem, 16), late)
+        if behind is not None:
+            ops[a]["first"] = behind
+        return a
 
-    def send(buf, land, step, asem, lsem):
+    def send(buf, land, step, asem, lsem, late=HOP):
         dst, frm = T.cores[(rank + step) % N], T.cores[(rank - step) % N]
         eng = topo.engines(core, dst)[:8]
         rid, pid = topo.addr(dst, core)
-        s = op("G", lambda: g.remote_dma(T[land][:], buf[0], T.sem[asem], T.sem[lsem], pid, rid, sum(1 << e for e in eng)),
-               [buf], [], 0.3, (lsem, len(eng)), HOP + (FIRST if land == "Lin0" else 0))
-        op("X", None, [], [R(land)], 0.0, (asem, len(topo.engines(frm, core)[:8])), 0.0, [s])
+        s = op("G", lambda: g.remote_dma(land[0], buf[0], T.sem[asem], T.sem[lsem], pid, rid, sum(1 << e for e in eng)),
+               [buf], [], 0.3, (lsem, len(eng)), late)
+        op("X", None, [], [land], 0.0, (asem, len(topo.engines(frm, core)[:8])), 0.0, [s])
 
-    a = dma("dm", [(T.c_Mi[:, :], T.m0[:, :])], [], [R("Mi")], LOAD, "S")
-    a = dma("dx", [(T.c_Xw[:, 0:S], T.x0[:, :])], [], [R("Xw", 0, S)], LOAD + 2.5)
-    dma("do", [(T.c_oi[:, :], T.own0[:, :])], [], [R("oi")], LOAD + 3)
-    dma("dth", [(T.c_thi[0:8, :], T.th[:, :])], [], [R("thi")], LOAD + 3)
-    dma("dn", [(T.c_NBw[:, :], T.nb[:, :])], [], [R("NBw")], LOAD + 8)
+    dma("dm", T.c_Mi[:, :], T.m0[:, :], [], [R("Mi")], LOAD + 0.5, "S")
+    a = dma("do", T.c_oi[:, :], T.own0[:, :], [], [R("oi")], LOAD + 0.8)
+    a = dma("dx", T.c_Xw[:, 0:S], T.x0[:, :], [], [R("Xw", 0, S)], LOAD + 3.3, "Y", a)
+    a = dma("dn", T.c_NBw[:, :], T.nb[:, :], [], [R("NBw")], LOAD + 7, "Y", a)
+    a = dma("dth", T.c_thi[0:8, :], T.th[:, :], [], [R("thi")], LOAD + 7, "Y", a)
     cp(R("Mu0"), R("Mi"))
-    send(R("Mu0"), "Lin0", 1, "aL0", "lL0")
-    cp(R("ob"), R("oi"))
-    dram = ("", "ownd", 0, S, S)
-    dma("dod", [(T.ownd[:, :], T.c_ob[:, :])], [R("ob")], [dram], LOAD + 5)
-    dma("dor", [(T.c_OWw[i::16, 0:S], T.ownd[:, :]) for i in range(16)], [dram], [R("OWw", 0, S)], LOAD + 3)
-    one = R("one", 0, 128, 1, 1)
+    send(R("Mu0"), R("Lin0"), 1, "aL00", "lL00", HOP + FIRST)
+    one, row = R("one", 0, 128, 1, 1), R("one", 0, 256, 1, 1)
     fill(R("one"), 1.0)
-    for name, x, first in (("m0", 1.0, 0.0), ("a0", 0.0, 512.0), ("AK", 0.0, 1e7), ("pv", 0.5, 0.0), ("pw", 0.0, 2.0)):
+    asel(R("BK1"), R("one", 0, 128), [[-16, 8], [0, 16]], OP.is_ge, 0)
+    asel(R("BK"), R("BK1"), [[16, 8], [0, 16]], OP.is_ge, 15, -1)
+    iota(R("ii"), [[0, 8], [1, 16]], 0)
+    iota(R("pi", 0, 1), [[0, 1]], 0, 1)
+    ts(R("pi", 1, 2), R("pi", 0, 1), 15, OP.bitwise_and)
+    cp(R("pf", 0, 1), R("pi", 1, 2))
+    ts(R("MI"), R("ii"), R("pf", 0, 1), OP.is_equal)
+    part("own0")
+    cp(R("ob"), R("oi"))
+    for j in range(16):
+        ts(H("EQ", j), R("BK"), R("MI", j, j + 1), OP.mult)
+    for b in range(6):
+        bank = "p_" + ("D0", "D1", "D2", "K0", "K1", "H0")[b]
+        n = min(3, 16 - 3 * b)
+        for j in range(n):
+            mm(R(bank, 136 * j, 136 * j + 136), H("EQ", 3 * b + j), R("ob"))
+        (cp if b % 2 else act)(R("OWw", 408 * b, 408 * b + 136 * n), R(bank, 0, 136 * n))
+    part("set")
+    iota(R("m0"), [[0, RUN // 16], [256, 16]], 0)
+    iota(R("a0"), [[0, RUN // 16], [-256, 16]], 256)
+    for name, x, first in (("AK", 0.0, 1e7), ("pv", 0.5, 0.0), ("pw", 0.0, 2.0)):
         fill(R(name), x)
         fill(R(name, 0, None, 16), first)
     asel(R("Ib"), R("one", 0, 128), [[-1, 128]], OP.is_equal, 0)
     for name, x in (("Nb", -1.0), ("H1", 255 / 512), ("H2", 0.5), ("If", 1.0)):
         ts(R(name), R("Ib"), x, OP.mult)
-    asel(R("BK1"), R("one"), [[0, 2], [-16, 8], [0, 16]], OP.is_ge, 0)
-    asel(R("BK"), R("BK1"), [[0, 2], [16, 8], [0, 16]], OP.is_ge, 15, -1)
     CC = R("BK", 0, 128, 16)
-    for name, x in (("BM", 32.0), ("BV", -16.0), ("BA", 16.0)):
+    for name, x in (("BM", 2 * KEY), ("BV", -KEY), ("BA", KEY)):
         ts(R(name, 0, 8), CC, x, OP.mult)
         ts(R(name, 8, 16), CC, -x, OP.mult)
     cp(R("BV", 16, 32), R("BV", 0, 16))
-    ts(H("BC", 0), H("BK", 0), -16.0, OP.mult)
-    ts(H("BC", 1), H("BK", 0), 16.0, OP.mult)
+    ts(H("BC", 0), R("BK"), -KEY, OP.mult)
+    ts(H("BC", 1), R("BK"), KEY, OP.mult)
     for n in sorted(set(sum(ON_V.values(), ())) - {0, 16}):
         asel(R("BC%d" % n), R("BC"), [[0, 16], [-1, 16]], OP.is_ge, n - 1, 0)
-    iota(R("ii"), [[0, 16], [1, 16]], 0)
-    for u in range(2):
-        ts(R("KR", 256 * u, 256 * u + 256, 1, 1), R("ii", 0, 256, 1, 1), -7.5, OP.add)
-    ts(R("TG", 0, 128, 1, 1), R("ii", 0, 128, 1, 1), -16.0, OP.add, 4096.0, OP.mult)
-    iota(R("pi", 0, 1), [[0, 1]], 0, 1)
-    ts(R("pi", 1, 2), R("pi", 0, 1), 15, OP.bitwise_and)
-    cp(R("pf", 0, 1), R("pi", 1, 2))
+    iota(R("KR", 0, 512, 1, 1), [[0, 32], [2, 16]], -15)
+    iota(R("TG", 0, 128, 1, 1), [[0, 8], [4096, 16]], -65536)
     ts(R("pf", 1, 2), R("pf", 0, 1), 1.0, OP.add)
     ts(R("pf", 3, 4), R("pf", 0, 1), 15.0, OP.is_lt, 256.0, OP.mult)
     off = R("pf", 3, 4)
-    ts(R("MI"), R("ii"), R("pf", 0, 1), OP.is_equal)
-    ts(R("DB"), R("ii"), R("pf", 0, 1), OP.is_equal, -1024.0, OP.mult)
+    ts(R("DB"), R("MI"), -1024.0, OP.mult)
     ts(R("D1"), R("ii"), R("pf", 1, 2), OP.is_equal, 256.0, OP.mult)
     tt(R("DB"), R("DB"), R("D1"), OP.add)
-    iota(R("bi", 0, 8), [[1, 8]], 0)
-    cp(R("BL"), R("bi", 0, 8))
+    iota(R("bi"), [[1, 8]], 0)
+    cp(R("BL"), R("bi"))
     ts(R("pi", 2, 3), R("pi", 1, 2), 1, OP.arith_shift_right)
-    cp(R("WL", 0, 1), R("pi", 2, 3))
-    ts(R("WL", 1, 2), R("pi", 2, 3), 8.0, OP.add)
-    cp(R("WL", 2, 3), R("pi", 1, 2))
-    cp(R("WL", 3, 4), R("pi", 1, 2))
+    cp(R("pf", 4, 5), R("pi", 2, 3))
+    iota(R("wl", 0, 4), [[8, 4]], 0)
+    iota(R("wl", 4, 8), [[0, 2], [-16, 2]], 16)
+    ts(R("WL", 0, 4), R("wl", 0, 4), R("pf", 4, 5), OP.add)
+    ts(R("WL", 4, 8), R("wl", 4, 8), R("pf", 0, 1), OP.add)
     iota(R("ks"), [[16, 16]], S, 0)
     ts(R("ks"), R("ks"), R("pf", 0, 1), OP.add)
     scan(R("thr"), R("pv"), R("pw"), OP.mult, OP.add)
     tt(R("pw", 0, 16), R("thr", 0, 16), R("MI", 0, 16), OP.mult)
     rsum(R("pf", 2, 3), R("pw", 0, 16))
-    ts(R("W1"), H("BK", 0), 64.0, OP.mult)
-    ts(R("W2"), H("BK", 0), R("pf", 2, 3), OP.mult, 0.5, OP.mult)
-    cp(R("Sel", 0, 8), R("Ib", 0, 128, 16))
+    ts(R("W1"), R("BK"), 64.0, OP.mult)
+    ts(R("W2"), R("BK"), R("pf", 2, 3), OP.mult, 0.5, OP.mult)
+    ts(R("Sel", 0, 8), R("Ib", 0, 128, 16), 4.0, OP.mult)
     ts(R("Sel", 8, 16), R("Ib", 0, 128, 16), -256.0, OP.mult)
     fill(R("PC", 0, 16), 0.0)
     fill(R("o6"), 1.0)
-    ts(R("kw"), R("ii"), -7.5, OP.add, 2 * BIG, OP.mult)
-    asel(R("WY"), R("kw"), [[-16, 2], [-2, 8], [0, 16]], OP.is_equal, 0)
-    asel(R("WY"), R("WY"), [[-16, 2], [-2, 8], [0, 16]], OP.not_equal, -1, 1, -BIG)
-    asel(R("WY"), R("WY"), [[-8, 2], [-1, 8], [0, 16]], OP.not_equal, -32, 1, 1.0)
-    asel(R("WZ"), R("one"), [[-8, 2], [-1, 8], [0, 16]], OP.is_equal, 0)
-    asel(R("WO"), R("one"), [[-8, 2], [-1, 8], [0, 16]], OP.is_equal, -16)
-    ts(R("cq1", 0, 128, 1, 1), R("KR", 0, 128, 1, 1), -BIG, OP.mult)
+    two, single = [[-16, 2], [-2, 8], [0, 16]], [[-8, 2], [-1, 8], [0, 16]]
+    iota(R("kw"), [[0, 16], [4 * BIG, 16]], -30 * BIG)
+    for name, o in (("WY", 0), ("WX", 1)):
+        asel(R(name), R("kw"), two, OP.is_equal, -32 * o)
+        asel(R(name), R(name), two, OP.not_equal, -32 * o - 1, 1, -float(BIG))
+        asel(R(name), R(name), single, OP.not_equal, -64 - 16 * o, 1, 1.0)
+    asel(R("WZ"), R("one"), single, OP.is_equal, 0)
+    asel(R("WZ"), R("WZ"), single, OP.not_equal, -16, 1, 1.0)
+    asel(R("WO"), R("one"), single, OP.is_equal, -32)
+    ts(R("cq1", 0, 128, 1, 1), R("KR", 0, 128, 1, 1), -float(BIG), OP.mult)
     tt(R("cq", 0, 128, 1, 1), R("cq1", 0, 128, 1, 1), R("KR", 0, 128, 1, 1), OP.mult)
-    fill(R("cc", 0, 256, 1, 1), MID + 8192)
+    iota(R("cc", 0, 128, 1, 1), [[0, 128]], int(MID) + 8192)
     for t in range(RO):
-        iota(R("ZR%d" % t, 0, 256), [[0, 256]], -30000)
+        iota(R("ZR%d" % t, 0, 256), [[0, 256]], 0)
     cp(R("thf", 0, 1, 1, 8), R("thi", 0, 1, 1, 8))
-    ts(R("thf", 0, 1, 1, 8), R("thf", 0, 1, 1, 8), 16.0, OP.mult, -8.0, OP.add)
+    ts(R("thf", 0, 1, 1, 8), R("thf", 0, 1, 1, 8), KEY, OP.mult, -KEY / 2, OP.add)
     asel(R("B8", 0, 128, 1, 8), R("o6", 0, 128, 1, 8), [[-1, 8], [0, 16]], OP.is_equal, 0)
     ts(R("B8", 0, 128, 1, 8), R("B8", 0, 128, 1, 8), R("thf", 0, 1, 1, 8), OP.mult)
     mm(R("p_MS", 0, 128), R("o6", 0, 128, 1, 8), R("B8", 0, 128, 1, 8))
     cp(R("TH0"), R("p_MS", 0, 128))
 
     def gather(v, lst, h):
-        for c in range(2 * h, 2 * h + 2):
-            part(v[1] + str(c))
-            for a in range(c * 64, c * 64 + 64, CUT[v]):
-                act(R(v, a * 16, (a + CUT[v]) * 16), R("Xw", 0, S), R(lst, a, a + CUT[v]))
+        for a in range(128 * h, 128 * h + 128, CUT[v]):
+            part(v[1] + str(a // 64))
+            act(R(v, a * 16, (a + CUT[v]) * 16), R("Xw", 0, S), R(lst, a, a + CUT[v]))
 
     def centre(v, C, h):
         mx, mn = "mx" + v[1], "mn" + v[1]
         for c in range(2 * h, 2 * h + 2):
             part("s%s%d" % (v[1], c))
-            n = 16 * CUT[v]
-            for a in range(c * 1024, c * 1024 + 1024, n):
-                scan(R(mx, a, a + n), R("m0", 0, n), R(v, a, a + n), OP.mult, OP.max)
-                scan(R(mn, a, a + n), R("a0", 0, n), R(v, a, a + n), OP.add, OP.min)
+            for a in range(c * 1024, c * 1024 + 1024, RUN):
+                scan(R(mx, a, a + RUN), R("m0"), R(v, a, a + RUN), OP.min, OP.max)
+                scan(R(mn, a, a + RUN), R("a0"), R(v, a, a + RUN), OP.max, OP.min)
         out = H("p_MS", h) if v == "vR" else H("p_H%d" % h, 3)
         mm(out, R("H1"), E(mx, 2048 * h, 2048 * h + 2048))
         mm(out, R("H2"), E(mn, 2048 * h, 2048 * h + 2048), False)
-        ts(H(C, h), out, R1, OP.add, R1, OP.subtract)
+        rnd(H(C, h), out, R1)
 
     def sites(sf, h):
         out = H("p_H%d" % h, 2)
-        mm(out, one, R("TG", 0, 128, 1, 1), True, False)
-        mm(out, H(sf, h), R("Ib"), False, True)
+        mm(out, one, R("TG", 0, 128, 1, 1))
+        mm(out, H(sf, h), R("Ib"), False)
 
-    cnt = {"D": 0, "m": 0}
+    banks = [0]
 
-    def outermost(h):
-        kb, o = ("p_MS", 256) if h in EARLY else ("p_K%d" % h, 0)
-        keys("vR", h, [("R", "CR")], kb, o)
-        scan(H("FR", h), R("AK", 0, 128), H(kb, 1, o), OP.add, OP.min)
+    def sizes(name, v, C, h, b):
+        d = "p_D%d" % (banks[0] % 3)
+        banks[0] += 1
+        for k in range(4):
+            mm(H(d, k), R("Ib"), H(C, h))
+            mm(H(d, k), R("Nb"), R(v, h * 2048 + 4 * b + k, h * 2048 + 2048, 16), False)
+        act(R("m" + name, h * 2048 + b * 512, h * 2048 + b * 512 + 512), R(d), None, AF.Abs)
 
-    def keys(v, h, units, kb, o=0):
-        w = 256 * len(units)
+    def keys(v, h, units):
+        kb, w = "p_K%d" % h, 256 * len(units)
         col = lambda k: R(v, h * 2048 + k, h * 2048 + 2048, 16)
         part("d%s%d" % (v[1], h))
-        for u, (name, C) in enumerate(units):
-            if ON_V[name][h]:
-                mm(H("p_H%d" % h, u), R("Ib"), H(C, h))
-        mm(R(kb, o, o + w), one, R("KR", 0, w, 1, 1))
+        mm(R(kb, 0, w), one, R("KR", 0, w, 1, 1))
         for u, (name, C) in enumerate(units):
             n = ON_V[name][h]
+            if n and (name != "NI" or not ON_V["I"][h]):
+                mm(H("p_H%d" % h, u), R("Ib"), H(C, h))
             if n:
-                mm(R(kb, o + 256 * u, o + 256 * u + 256), H(C, h), R("BC" if n == 16 else "BC%d" % n), False)
+                mm(R(kb, 256 * u, 256 * u + 256), H(C, h), R("BC" if n == 16 else "BC%d" % n), False)
         for k in range(16):
             us = [u for u, (name, C) in enumerate(units) if k < ON_V[name][h]]
             if us:
-                mm(R(kb, o + 256 * us[0] + k, o + 256 * us[-1] + 256, 16), col(k), R("BV", 0, 16 * len(us)), False)
-        todo = [(b, u) for b in range(4) for u in range(len(units))]
-        todo.sort(key=lambda x: x[0] - (ON_V[units[x[1]][0]][h] // 4 if 4 * x[0] >= ON_V[units[x[1]][0]][h] else 0))
-        for b, u in todo:
-            name, C = units[u]
-            vec = 4 * b < ON_V[name][h]
-            if vec:
+                mm(R(kb, 256 * us[0] + k, 256 * us[-1] + 256, 16), col(k), R("BV", 0, 16 * len(us)), False)
+        for b in range(4):
+            for u, (name, C) in enumerate(units):
+                vec = 4 * b < ON_V[name][h]
+                if vec:
+                    for k in range(4 * b, 4 * b + 4):
+                        tt(H("m" + name, 16 * h + k), col(k), H("p_H%d" % h, u), OP.max)
+                else:
+                    sizes(name, v, C, h, b)
                 for k in range(4 * b, 4 * b + 4):
-                    tt(H("m" + name, 16 * h + k), col(k), H("p_H%d" % h, u), OP.max)
-            else:
-                d = "p_D%d" % (cnt["D"] % 3)
-                cnt["D"] += 1
-                for k in range(4):
-                    mm(H(d, k), R("Ib"), H(C, h))
-                    mm(H(d, k), R("Nb"), col(4 * b + k), False)
-                act(R("m" + name, h * 2048 + b * 512, h * 2048 + b * 512 + 512), R(d), None, AF.Abs)
-            for k in range(4 * b, 4 * b + 4):
-                mm(R(kb, o + 256 * u + k, o + 256 * u + 256, 16), H("m" + name, 16 * h + k), R("BM" if vec else "BA"), False)
+                    mm(R(kb, 256 * u + k, 256 * u + 256, 16), H("m" + name, 16 * h + k), R("BM" if vec else "BA"), False)
 
-    def places(out, ends, n):
-        ts(R("r2", 0, n), ends, R16, OP.add, R16, OP.subtract)
-        tt(R(out, 0, 2 * n, 2), ends, R("r2", 0, n), OP.subtract)
-        tt(R(out, 1, 2 * n, 2), R(out, 0, 2 * n, 2), R(out, 0, 2 * n, 2), OP.mult)
+    def least(out, kb, x):
+        scan(out, R("AK"), H(kb, x), OP.add, OP.min)
 
-    def turned(out, in_, bank, c0):
+    def turned(out, in_, bank, c0, copy):
         mm(R(bank, c0, c0 + 128, 1, in_[4]), in_, R("Ib"))
-        cp(R(out, 0, 128, 1, in_[4]), R(bank, c0, c0 + 128, 1, in_[4]))
+        copy(R(out, 0, 128, 1, in_[4]), R(bank, c0, c0 + 128, 1, in_[4]))
 
     for t in range(RO):
         last = t == RO - 1
@@ -375,30 +383,27 @@ def rank_program(g, core, T, topo):
         for h in range(2):
             gather("vR", mu, h)
             centre("vR", "CR", h)
-        part("sI0")
-        ts(R("SF"), R(li), -MID, OP.add)
         for h in range(2):
+            part("sI%d" % (2 * h))
+            ts(H("SF", h), H(li, h), -MID, OP.add)
             sites("SF", h)
         for h in range(2):
             gather("vI", li, h)
             centre("vI", "CI", h)
         for h in range(2):
             kb, hb = "p_K%d" % h, "p_H%d" % h
-            for x in EARLY:
-                if EARLY[x] == h:
-                    outermost(x)
-            keys("vI", h, [("I", "CI")], kb)
+            keys("vI", h, [("I", "CI")])
             part("oI")
-            scan(H("FI", h), R("AK", 0, 128), H(kb, 1), OP.add, OP.min)
+            least(H("FI", h), kb, 1)
             part("pI%d" % h)
-            scan(H("FI", 2 + h), R("AK", 0, 128), H(kb, 0), OP.add, OP.min)
+            least(H("FI", 2 + h), kb, 0)
             tt(H("NE", h), H(kb, 0), H("FI", 2 + h), OP.not_equal)
             scan(H("RS", h), H("NE", h), H(hb, 2), OP.mult, OP.min)
             c = (8 * h, 8 * h + 8)
             ends = E("RS", 128 * h, 128 * h + 128)
-            ts(R("r1", *c), ends, R4096, OP.add, R4096, OP.subtract)
-            tt(R("sl", *c), ends, R("r1", *c), OP.subtract)
-            tt(H("ex", h), R("sl", *c), H("MI", 0), OP.mult, R("BL"))
+            rnd(R("rS", *c), ends, R4096)
+            tt(R("sl", *c), ends, R("rS", *c), OP.subtract)
+            tt(H("ex", h), R("sl", *c), R("MI"), OP.mult, R("BL"))
             mm(R(hb, 384, 392), H("ex", h), CC)
             ts(R("sU", *c), R(hb, 384, 392), MID, OP.add)
             cp(H("nU", h), R("NBw"), R("sU", *c))
@@ -407,22 +412,25 @@ def rank_program(g, core, T, topo):
             act(H("bG", h), R("OWw", 0, S), R("sU", *c))
             ts(H("SN", h), H("nU", h), -MID, OP.add)
             sites("SN", h)
-            scan(H("bs", h), H("DB", h), H("bG", h), OP.add, OP.max)
-            ends = E("bs", 128 * h, 128 * h + 128)
-            ts(R("bU", *c), ends, off, OP.subtract)
+            scan(H("bs", h), R("DB"), H("bG", h), OP.add, OP.max)
+            ts(R("bU", *c), E("bs", 128 * h, 128 * h + 128), off, OP.subtract)
+            part("c%d" % h)
             act(H("CB", h), R("CR"), R("bU", *c))
         part("oI")
-        places("ZK", E("FI"), 32)
+        rnd(R("rI"), E("FI"), RKEY)
+        tt(R("ZK", 0, 64, 2), E("FI"), R("rI"), OP.subtract)
+        tt(R("ZK", 1, 64, 2), R("ZK", 0, 64, 2), R("ZK", 0, 64, 2), OP.mult)
         part("EQ")
         ts(R("bL"), E("bs"), off, OP.subtract)
         offs = [sum(256 - 16 * x for x in range(c)) for c in range(16)]
         for c in range(16):
             ts(R("EQ", offs[c], offs[c] + 256 - 16 * c), R("bG", 16 * c, 256), R("bL", c, c + 1), OP.is_equal)
         for c in range(16):
-            mm(R("p_MS", 16 * c, 16 * c + 16), R("W2"), R("EQ", offs[c], offs[c] + 16), c == 0, c in (0, 15))
+            mm(R("p_MS", 16 * c, 16 * c + 16), R("W2"), R("EQ", offs[c], offs[c] + 16), c == 0)
             if c < 15:
-                mm(R("p_MS", 16 * c + 16, 256), R("W1"), R("EQ", offs[c] + 16, offs[c] + 256 - 16 * c), c == 0, False)
-        tt(R("nfG"), R("p_MS", 0, 256), R("thr"), OP.is_ge)
+                mm(R("p_MS", 16 * c + 16, 256), R("W1"), R("EQ", offs[c] + 16, offs[c] + 256 - 16 * c), c == 0)
+        for h in range(2):
+            tt(H("nfG", h), H("p_MS", h), R("thr"), OP.is_ge)
         for x in range(2):
             for h in range(2):
                 mm(R("p_MS", 256 + 16 * x + 8 * h, 264 + 16 * x + 8 * h), H("nfG", h), R("Sel", 0, 8))
@@ -430,9 +438,9 @@ def rank_program(g, core, T, topo):
             mm(R("p_MS", 288 + 8 * h, 296 + 8 * h), H("bG", h), R("Sel", 8, 16))
         tt(R("ZK", 1, 64, 2), R("ZK", 1, 64, 2), R("p_MS", 256, 288), OP.add)
         ts(R("dl"), R("p_MS", 288, 304), 65025.0, OP.add, 1.0, OP.min)
-        tt(R("Df", 0, 32), R("ZK", 0, 32), R("ZK", 32, 64), OP.subtract)
         part("lists")
-        scan(R("fs"), R("DB"), R("nfG"), OP.add, OP.max)
+        for h in range(2):
+            scan(H("fs", h), R("DB"), H("nfG", h), OP.add, OP.max)
         cp(R("sF"), R("sU"))
         ts(R("f1"), E("fs"), off, OP.subtract)
         tt(R("f1"), R("f1"), R("ks"), OP.mult)
@@ -440,88 +448,112 @@ def rank_program(g, core, T, topo):
         tt(R("sb", 16, 32), R("f1"), R("bL"), OP.max)
         cp(R("WU"), R("sb"))
         if not last:
-            ts(R("vT"), R("Xw", 0, S), -8.0, OP.add, 0.0, OP.max, R("sU"))
+            part("vT")
+            act(R("vT"), R("Xw", 0, S), R("sU"), AF.Relu, -8.0)
         for h in range(2):
             kb, hb = "p_K%d" % h, "p_H%d" % h
-            for x in EARLY:
-                if EARLY[x] == 2 + h:
-                    outermost(x)
-            keys("vN", h, [("NI", "CI"), ("NR", "CB")], kb)
+            keys("vN", h, [("NI", "CI"), ("NR", "CB")])
             part("pN%d" % h)
-            c = (512 * h, 512 * h + 512)
-            scan(R("FN", *c), R("AK"), R(kb), OP.add, OP.min)
+            slots = [2 * s + h for s in (1, 3, 2, 0)]
+            for x in range(4):
+                least(H("FN", slots[x]), kb, x)
             tt(H("fI", h), H(kb, 0), R(th), OP.is_lt)
             tt(H("fR", h), H(kb, 2), R(th), OP.is_lt)
-            tt(R("NE", *c), R(kb), R("FN", *c), OP.not_equal)
-            for x, slot in enumerate((2, 3, 1, 0)):
-                scan(H("NS", 2 * slot + h), H("NE", 4 * h + x), H(hb, 2), OP.mult, OP.min)
+            for x in range(4):
+                tt(H("NE", slots[x]), H(kb, x), H("FN", slots[x]), OP.not_equal)
+            for x in range(4):
+                scan(H("NS", slots[x]), H("NE", slots[x]), H(hb, 2), OP.mult, OP.min)
         if not last:
             part("X")
             scat(R("Xw"), R("WU", 0, 16), R("vT"))
         part("fin")
         scan(R("PC", 16, 272), R("fI"), R("fR"), OP.add, OP.subtract)
-        tt(R("won"), E("PC", 16), E("PC", 0, 256), OP.is_gt)
-        ts(R("r3"), E("NS"), R4096, OP.add, R4096, OP.subtract)
-        tt(R("ZK", 64, 128), E("NS"), R("r3"), OP.subtract)
-        tt(R("Df", 32, 64), R("ZK", 96, 128), R("ZK", 64, 96), OP.subtract)
-        tt(R("Pr"), R("won"), R("Df"), OP.mult, R("WL"))
-        tt(R(do, 0, 64), R("Pr"), R("ZK", 32, 96), OP.add)
-        send(R(do, 0, 48), "Din%d" % t, -1 - t, "aD%d" % t, "lD%d" % t)
+        tt(R("won", 0, 16), E("PC", 16), E("PC", 0, 256), OP.is_gt)
+        tt(R("won", 16, 32), E("PC", 16), E("PC", 0, 256), OP.is_le)
+        rnd(R("rN"), E("NS"), R4096)
+        tt(R("ZK", 64, 128), E("NS"), R("rN"), OP.subtract)
+        tt(R(do, 0, 128), R("won"), R("ZK"), OP.mult, R("WL"))
+        send(R(do, 0, 96), R("Din%d" % t), -1 - t, "aD%d" % t, "lD%d" % t)
         if not last:
             part("w")
-            tt(R("wf"), R("won"), R("p_MS", 256, 272), OP.is_gt)
+            tt(R("wf"), R("won", 0, 16), R("p_MS", 256, 272), OP.is_gt)
         part("loc")
-        tt(R(do, 64, 80), R("won"), R("dl"), OP.mult)
-        turned("TP", R(do, 48, 80), "p_H0", 0)
+        tt(R(do, 128, 144), R("won", 0, 16), R("dl"), OP.mult)
+        turned("TP", R(do, 96, 144), "p_H0", 0, cp)
         for h in range(2):
-            mm(H("p_H1", h), H("WZ", h, 0, 32), R("TP", 0, 128, 1, 32))
-        for h in range(2):
-            mm(H("p_H1", 2 + h), R("Ib"), H("bG", h), True, False)
-            mm(H("p_H1", 2 + h), H("WO", h, 0, 32), R("TP", 0, 128, 1, 32), False, True)
+            mm(H("p_H1", h), H("WZ", h, 32), R("TP", 0, 128, 1, 32))
         act(R("zG"), R("p_H1", 0, 256), None, AF.Identity, MID + 4096)
-        act(R("ow"), R("p_H1", 256, 512))
         scat(R(zr), R("WU", 16, 32), R("zG"))
         part("own")
+        for h in range(2):
+            mm(H("p_H0", 2 + h), R("Ib"), H("bG", h))
+            mm(H("p_H0", 2 + h), H("WO", h, 48), R("TP", 0, 128, 1, 48), False)
+        act(R("ow"), R("p_H0", 256, 512))
         scat(R("OWw"), R("WU", 0, 16), R("ow"))
         if last:
-            dma("dyo", [(T.yown[:, :], T.c_OWw[0::16, 0:S])], [R("OWw", 0, S)], [], LOAD + 1.5, "G")
+            dma("dyo", T.yown[:, :], T.c_OWw[0::16, 0:S], [R("OWw", 0, S)], [], LOAD + 1.5, "G")
         for h in range(2):
-            if h not in EARLY:
-                outermost(h)
+            part("dR%d" % h)
+            kb, n = "p_K%d" % h, ON_V["R"][h] if last else 0
+            mm(H(kb, 0), one, R("KR", 0, 128, 1, 1))
+            if n:
+                mm(H("p_MS", 2 + h), R("Ib"), H("CR", h))
+                mm(H(kb, 0), H("CR", h), H("BC%d" % n, 1), False)
+            for k in range(16):
+                col = R("vR", h * 2048 + k, h * 2048 + 2048, 16)
+                if k < n:
+                    mm(R(kb, k, 128, 16), col, R("BV", 8, 16), False)
+                    tt(H("mR", 16 * h + k), col, H("p_MS", 2 + h), OP.max)
+                elif k % 4 == 0:
+                    sizes("R", "vR", "CR", h, k // 4)
+                mm(R(kb, k, 128, 16), H("mR", 16 * h + k), R("BM" if k < n else "BA", 8, 16), False)
+            least(H("FR", h), kb, 0)
         part("pR")
-        places("KK", E("FR"), 16)
-        turned("TR", R("KK"), "p_MS", 0)
-        row = R("one", 0, 256, 1, 1)
-        mm(R("p_H0", 0, 256), R("cq", 0, 128, 1, 1), row, True, False)
-        mm(R("p_H0", 0, 256), R("If"), R(zr, 0, 256), False, False)
+        rnd(R("rR"), E("FR"), RKEY)
+        tt(R("KK", 0, 32, 2), E("FR"), R("rR"), OP.subtract)
+        tt(R("KK", 1, 32, 2), R("KK", 0, 32, 2), R("KK", 0, 32, 2), OP.mult)
+        turned("TR", R("KK"), "p_MS", 0, act)
+        mm(R("p_MS", 256, 512), R("cq", 0, 128, 1, 1), row)
+        mm(R("p_MS", 256, 512), R("If"), R(zr, 0, 256), False)
         for h in range(2):
-            mm(H("p_H0", h), H("WY", h, 0, 32), R("TR", 0, 128, 1, 32), False, h == 1)
+            mm(H("p_MS", 2 + h), H("WY", h, 32), R("TR", 0, 128, 1, 32), False)
+        tt(R("x1"), R("Mi"), R("p_MS", 256, 512), OP.max)
         part("back")
-        turned("TY", R("Din%d" % t), "p_K0", 256)
+        turned("TY", R("Din%d" % t), "p_K0", 256, cp)
         mm(R("p_K0", 0, 256), R("cq", 0, 128, 1, 1), row)
-        mm(R("p_K0", 0, 256), one, R("cc", 0, 256, 1, 1), False)
+        mm(R("p_K0", 0, 256), R("cc", 0, 128, 1, 1), row, False)
         for h in range(2):
-            mm(H("p_K0", h), H("WY", h, 0, 48), R("TY", 0, 128, 1, 48), False)
-        tt(R("x1"), R("Mi"), R("p_K0" if SWAP else "p_H0", 0, 256), OP.max)
-        tt(R("Tm"), R("x1"), R("p_H0" if SWAP else "p_K0", 0, 256), OP.max)
-        ts(R("Mi"), R("Tm"), 4095, OP.bitwise_and)
-        if last:
-            cp(R("Mo"), R("Mi"))
-            dma("dy", [(T.ym[:, :], T.c_Mo[:, :])], [R("Mo")], [], LOAD)
-        else:
-            cp(R("Mu%d" % (t + 1)), R("Mi"))
-            send(R("Mu%d" % (t + 1)), "Lin%d" % (t + 1), 2 + t, "aL%d" % (t + 1), "lL%d" % (t + 1))
+            for w in ("WY", "WX"):
+                mm(H("p_K0", h), H(w, h, 96), R("TY", 0, 128, 1, 96), False)
+        for h in range(2):
+            tt(H("Tm", h), H("x1", h), H("p_K0", h), OP.max)
+            ts(H("Mi", h), H("Tm", h), 4095, OP.bitwise_and)
+            if last:
+                cp(H("Mo", h), H("Mi", h))
+                dma("dy%d" % h, T.ym[:, 128 * h:128 * h + 128], H("Mo", h)[0], [H("Mo", h)], [], LOAD, "YS"[h])
+            else:
+                cp(H("Mu%d" % (t + 1), h), H("Mi", h))
+                send(H("Mu%d" % (t + 1), h), H("Lin%d" % (t + 1), h), 2 + t, "aL%d%d" % (h, t + 1), "lL%d%d" % (h, t + 1), HOP - 0.3)
+        if not last:
             part("w")
-            for c in range(16):
-                mm(R("p_MS", 440, 441), R("one", 0, 128), R("wf", c, c + 1), c == 0, c == 15)
-            cp(R("wI", 0, 1), R("p_MS", 440, 441))
+            mm(R("p_K1", 0, 16), R("one", 0, 128), R("wf"))
+            rsum(R("w16", 8, 9), R("p_K1", 0, 16))
+            cp(R("wI", 0, 1), R("w16", 8, 9))
             ts(R("wI", 8, 9), R("wI", 0, 1), 63, OP.bitwise_and)
-            ts(R("w16"), R("wI", 8, 9), 16.0, OP.mult)
-            ts(R("TH"), R("TH0"), R("w16"), OP.add)
+            ts(R("w16", 0, 1), R("wI", 8, 9), KEY, OP.mult)
+            ts(R("TH"), R("TH0"), R("w16", 0, 1), OP.add)
 
-    op("X", None, [], [], 0.0, ("dy", 16), 0.0, [i for i, o in enumerate(ops) if o["sem"]])
+    op("X", None, [], [], 0.0, ("dy0", 16), 0.0, [i for i, o in enumerate(ops) if o["sem"]])
     n = len(ops)
-    before = [{a: ops[a]["late"] + (SYNC if s else 0.0) for a, s in o["dep"].items()} for o in ops]
+    seq = sorted((o["part"][0], SCALAR.split().index(o["part"][1]), i) for i, o in enumerate(ops)
+                 if o["q"] == "S" and o["part"][1] in SCALAR.split())
+    for a, i in zip(seq, seq[1:]):
+        ops[i[2]]["dep"].setdefault(a[2], False)
+    before = [{a: ops[a]["late"] + ((OWN if ops[a]["q"] == o["q"] else SYNC.get(ops[a]["q"], 0.1)) if s else 0.0)
+               for a, s in o["dep"].items()} for o in ops]
+    for i, o in enumerate(ops):
+        if "first" in o:
+            before[i][o["first"]] = 0.0
     behind = [{} for _ in range(n)]
     for i in range(n):
         for a, x in before[i].items():
@@ -554,15 +586,13 @@ def rank_program(g, core, T, topo):
     if not ORDER:
         plan = PLAN.split()
         end = lay(before, behind, [(o["part"][0], plan.index(o["part"][1]), i) for i, o in enumerate(ops)])
-        for _ in range(TURNS):
-            end = lay(before, behind, [-x for x in lay(behind, before, [-x for x in end])])
+        end = lay(before, behind, [-x for x in lay(behind, before, [-x for x in end])])
         ORDER.extend(sorted(range(n), key=lambda i: (end[i] - ops[i]["us"], end[i], i)))
 
     done = {}
     count = {q: 0 for q in "VSPG"}
     known = {q: {} for q in "VSPGYX"}
-    snap = {}
-    total = {}
+    snap, total = {}, {}
     for i in ORDER:
         o = ops[i]
         q = o["q"]

from concourse.mybir import dt, AluOpType, AxisListType, ActivationFunctionType

S, L, RO = 2176, 256, 3
OP = AluOpType
AF = ActivationFunctionType
MID = 1088.0
BIG = 4096
KEY = 32.0
R1, RKEY, R4096 = 1.5 * 2 ** 23, 1.5 * 2 ** 28, 1.5 * 2 ** 35

ON_V = {"I": (4, 4), "NI": (8, 8), "NR": (8, 12), "R": (8, 8)}
GATHER_V = "R2 I1"
PLAN = "R3 dR0 vT sR0 dI0 I3 own0 sI1 c0 EQ back b1 pI1 I1 dN0 R2 N0 R0 loc b0 pI0 dN1 I2 dI1 pN0 c1 N2 N1 sR2 sI2 R1 w set sR1 sI3 pN1 dR1 fin I0 oI N3 X sI0 pR own lists sR3"
SCALAR = "own0 R0 R1 I0 I2 I3 dI0 R3 dI1 b0 N0 c0 b1 N2 c1 dN0 dN1 vT dR0 dR1"
CUT = {"vR": 64, "vI": 64, "vN": 128}
RUN = 512
SYNC = {"V": 0.22, "S": 0.22, "P": 0.22}
OWN = 0.22
HOP = 2.6
FIRST = 1.5
LOAD = 1.9
ISSUE = 0.3
CY = 0.00083
PE = 0.5
GAT = 1.56
ADDS = 0.0
PADD = 0.0
ORDER = []

SCRATCH = {}
ALIAS = {}


def _d(name, where, shape, dtype):
    SCRATCH[name] = (where, shape, dtype)


for _t, _l in (
        ("bfloat16", "Xw:2432 OWw:2432 ob:136 vR:4096 vI:4096 vN:4096 mxR:4096 mnR:4096 mxI:4096 mnI:4096 CR:256 CI:256 CB:256 "
                     "mI:4096 mR:4096 mNI:4096 mNR:4096 bG:256 EQ:2176 nfG:256 vT:256 fI:256 fR:256 PC:272 ow:256 NE:1024 wf:16 "
                     "one:256 m0:%d a0:%d " % (RUN, RUN) + "AK:128 Ib:128 Nb:128 H1:128 H2:128 BK:128 BK1:128 BC:256 BC4:256 "
                     "BC8:256 BC12:256 sB:80 KR:512 TG:128 DB:128 D1:128 W1:128 W2:128 kw:256 WY:256 WX:256 WZ:256 WO:256 "
                     "cq:128 cq1:128 cc:128 KK:32 TR:128"),
        ("float16", "SF:256 SN:256 ex:256 bs:256 fs:256 TP:128 TY:128"),
        ("float32", "ZR0:2432 ZR1:2432 ZR2:2432 Mo:256 FI:512 FR:256 FN:1024 RS:256 NS:1024 x1:256 zG:256 TH:128 TH0:128 ZK:128 "
                    "sF32:288 wl:8 pf:8 If:128 thr:128 pw:128 pv:128 ii:128 MI:128 ks:16 o6:128 B8:128"),
        ("int32", "NBw:2176 Mi:256 Tm:256 oi:136 pi:8 bi:8 thi:1 wI:16"),
        ("uint16", "nU:256 sU16:64 BL:8 WL:8")):
    for _x in _l.split():
        _d("c_" + _x.split(":")[0], "sbuf", [128, int(_x.split(":")[1])], _t)
for _b, _l in (("c_sF32", "sl:16 sF:16 bL:16 won:32 dl:16 f1:16 w16:16 rR:16 rI:32 rS:16 sb:32 rN:64"),
               ("c_sB", "BM:16 BV:32 BA:16 Sel:16"), ("c_sU16", "sU:16 bU:16 WU:32")):
    _o = 0
    for _x in _l.split():
        ALIAS[_x.split(":")[0]] = (_b, _o, int(_x.split(":")[1]))
        _o += int(_x.split(":")[1])
ALIAS["thf"] = ("c_pf", 7, 1)
for _t in range(RO):
    _d("Mu%d" % _t, "sbuf", [128, 256], "uint16")
    _d("Lin%d" % _t, "sbuf", [128, 256], "uint16")
    _d("Do%d" % _t, "sbuf", [128, 144], "float16")
    _d("Din%d" % _t, "sbuf", [128, 96], "float16")
for _n in ("D0", "D1", "D2", "K0", "K1", "H0", "H1", "MS"):
    _d("p_" + _n, "psum", [128, 512], "float32")

SEMAPHORES = (["qV", "qS", "qP", "qG", "dx", "dm", "dn", "do", "dth", "dy0", "dy1", "dyo"]
              + [n + "%d" % t for n in ("aL0", "aL1", "aD", "lL0", "lL1", "lD") for t in range(RO)])
WIDE = {"float32": 4, "int32": 4, "bfloat16": 2, "float16": 2, "uint16": 2}


def rank_program(g, core, T, topo):
    rank = T.rank_of(core)
    if rank is None:
        return
    N = len(T.cores)
    Q = {"V": g.vector, "S": g.scalar, "P": g.tensor, "G": g, "Y": g.sync}
    ops = []
    acc = {}
    turn = {}
    opened, todo = {}, {}
    now = [0, "set"]

    def R(name, c0=0, c1=None, st=1, p1=128):
        o = 0
        if name in ALIAS:
            name, o, w = ALIAS[name]
        else:
            if not (name in SCRATCH):
                name = "c_" + name
            w = SCRATCH[name][1][1]
        c1 = o + (w if c1 is None else c1)
        c0 = o + c0
        ap = T[name][0:p1, c0:c1] if st == 1 else T[name][0:p1, c0:c1:st]
        return (ap, name, c0, c1, len(range(c0, c1, st)))

    def H(name, h, p1=128):
        return R(name, h * 128, h * 128 + 128, 1, p1)

    def E(name, c0=0, c1=None):
        return R(name, c0 + 15, c1, 16)

    def op(queue, fn, reads, writes, us, sem=None, late=0.0, after=(), sum_=None):
        me = len(ops)
        dep = {a: True for a in after}
        for regs, wr in ((reads, False), (writes, True)):
            for r in regs:
                ps = r[1].startswith("p_")
                if ps:
                    q, cur, prev = turn.get(r[1], (queue, [], []))
                    if q != queue:
                        cur, prev = [], cur
                    for a in prev:
                        dep[a] = True
                    if queue == "P":
                        for a in (cur if sum_ == me else [sum_]):
                            dep.setdefault(a, False)
                    turn[r[1]] = (queue, cur + [me] if me not in cur else cur, prev)
                for (c0, c1, a, w) in acc.get(r[1], []):
                    if c0 >= r[3] or r[2] >= c1 or not (w or wr) or a == me or (ps and ops[a]["q"] == queue == "P"):
                        continue
                    own = ops[a]["q"] == queue and ops[a]["sem"] is None and sem is None
                    if own and (not w or queue == "P" or (ps and wr)):
                        dep.setdefault(a, False)
                    else:
                        dep[a] = True
        ops.append({"q": queue, "fn": fn, "us": us, "sem": sem, "late": late, "dep": dep, "part": tuple(now)})
        for regs, wr in ((reads, False), (writes, True)):
            for r in regs:
                lst = acc.get(r[1], [])
                if wr and r[4] == r[3] - r[2]:
                    lst = [e for e in lst if not (e[0] >= r[2] and e[1] <= r[3])]
                acc[r[1]] = lst + [(r[2], r[3], me, wr)]
        return me

    def part(name):
        now[1] = name

    def narrow(*rs):
        return 0.5 if all(WIDE[SCRATCH[r[1]][2]] == 2 for r in rs) else 1

    def cyc(n):
        return max(64, n) * CY

    def src(a, off):
        return a[0] if off is None else a[0].indirect(off[0])

    def gat(out):
        return 0.06 + GAT * CY * out[4]

    def act(out, in_, off=None, func=AF.Copy, bias=None):
        if off and now[1] in GATHER_V.split():
            return cp(out, in_, off)
        x = src(in_, off)
        fn = (lambda: g.scalar.activation(out[0], x, func)) if bias is None else (lambda: g.scalar.activation(out[0], x, func, bias))
        op("S", fn, [in_] + ([off] if off else []), [out], gat(out) if off else cyc(out[4]) + ADDS)

    def cp(out, in_, off=None):
        x = src(in_, off)
        op("V", lambda: g.vector.tensor_copy(out[0], x), [in_] + ([off] if off else []), [out],
           gat(out) if off else cyc(out[4] * narrow(out, in_)))

    def scat(win, off, in_):
        op("V", lambda: g.vector.tensor_copy(win[0].indirect(off[0]), in_[0]), [in_, off], [win], 0.05 + 3.8 * CY * in_[4])

    def tt(out, a, b, o, off=None):
        x = src(a, off)
        op("V", lambda: g.vector.tensor_tensor(out[0], x, b[0], o), [a, b] + ([off] if off else []), [out],
           gat(out) if off else cyc(out[4] * (1 if "p_" in (a[1][:2], b[1][:2]) else 2)))

    def ts(out, a, s1, o1, s2=None, o2=None):
        rd, x1 = ([a, s1], s1[0]) if isinstance(s1, tuple) else ([a], s1)
        us = cyc(out[4] * narrow(out, a))
        if o2 is None:
            op("V", lambda: g.vector.tensor_scalar(out[0], a[0], x1, None, o1), rd, [out], us)
        else:
            op("V", lambda: g.vector.tensor_scalar(out[0], a[0], x1, s2, o1, o2), rd, [out], us)

    def rnd(out, a, r):
        ts(out, a, r, OP.add, r, OP.subtract)

    def scan(out, a, b, o1, o2):
        op("V", lambda: g.vector.tensor_tensor_scan(out[0], a[0], b[0], 0.0, o1, o2), [a, b], [out], cyc(out[4] * narrow(out, a, b)))

    def fill(out, x):
        op("V", lambda: g.vector.memset(out[0], x), [], [out], cyc(out[4] * narrow(out)))

    def mm(out, l, r, start=True):
        if start:
            opened[out[1]] = len(ops)
        a = opened[out[1]]
        todo[a] = todo.get(a, 0) + 1

        def fn():
            todo[a] -= 1
            return g.tensor.matmul(out[0], l[0], r[0], start, not todo[a])
        op("P", fn, [l, r], [out], max(64, r[4] * (4 if SCRATCH[l[1]][2] == "float32" else 1)) * CY * PE + PADD, sum_=a)

    def rsum(out, in_):
        op("V", lambda: g.vector.tensor_reduce(out[0], in_[0], AxisListType.X, OP.add), [in_], [out], cyc(in_[4]))

    def iota(out, pat, base, mult=0):
        op("G", lambda: g.iota(out[0], pat, base, mult, allow_small_or_imprecise_dtypes=True), [], [out], 0.13 + 2 * CY * out[4])

    def asel(out, in_, pat, cmp_, base, mult=1, other=0.0):
        op("G", lambda: g.affine_select(out[0], in_[0], pat, cmp_, other, base, mult), [in_], [out], 0.17 + 2 * CY * out[4])

    def dma(sem, out, in_, reads, writes, late, queue="Y", behind=None):
        a = op(queue, lambda: Q[queue].dma_start(out, in_).then_inc(T.sem[sem], 16), reads, writes, ISSUE, (sem, 16), late)
        if behind is not None:
            ops[a]["first"] = behind
        return a

    def send(buf, land, step, asem, lsem, late=HOP):
        dst, frm = T.cores[(rank + step) % N], T.cores[(rank - step) % N]
        eng = topo.engines(core, dst)[:8]
        rid, pid = topo.addr(dst, core)
        s = op("G", lambda: g.remote_dma(land[0], buf[0], T.sem[asem], T.sem[lsem], pid, rid, sum(1 << e for e in eng)),
               [buf], [], 0.3, (lsem, len(eng)), late)
        op("X", None, [], [land], 0.0, (asem, len(topo.engines(frm, core)[:8])), 0.0, [s])

    dma("dm", T.c_Mi[:, :], T.m0[:, :], [], [R("Mi")], LOAD + 0.5, "S")
    a = dma("do", T.c_oi[:, :], T.own0[:, :], [], [R("oi")], LOAD + 0.8)
    a = dma("dx", T.c_Xw[:, 0:S], T.x0[:, :], [], [R("Xw", 0, S)], LOAD + 3.3, "Y", a)
    a = dma("dn", T.c_NBw[:, :], T.nb[:, :], [], [R("NBw")], LOAD + 7, "Y", a)
    a = dma("dth", T.c_thi[0:8, :], T.th[:, :], [], [R("thi")], LOAD + 7, "Y", a)
    cp(R("Mu0"), R("Mi"))
    send(R("Mu0"), R("Lin0"), 1, "aL00", "lL00", HOP + FIRST)
    one, row = R("one", 0, 128, 1, 1), R("one", 0, 256, 1, 1)
    fill(R("one"), 1.0)
    asel(R("BK1"), R("one", 0, 128), [[-16, 8], [0, 16]], OP.is_ge, 0)
    asel(R("BK"), R("BK1"), [[16, 8], [0, 16]], OP.is_ge, 15, -1)
    iota(R("ii"), [[0, 8], [1, 16]], 0)
    iota(R("pi", 0, 1), [[0, 1]], 0, 1)
    ts(R("pi", 1, 2), R("pi", 0, 1), 15, OP.bitwise_and)
    cp(R("pf", 0, 1), R("pi", 1, 2))
    ts(R("MI"), R("ii"), R("pf", 0, 1), OP.is_equal)
    part("own0")
    cp(R("ob"), R("oi"))
    for j in range(16):
        ts(H("EQ", j), R("BK"), R("MI", j, j + 1), OP.mult)
    for b in range(6):
        bank = "p_" + ("D0", "D1", "D2", "K0", "K1", "H0")[b]
        n = min(3, 16 - 3 * b)
        for j in range(n):
            mm(R(bank, 136 * j, 136 * j + 136), H("EQ", 3 * b + j), R("ob"))
        (cp if b % 2 else act)(R("OWw", 408 * b, 408 * b + 136 * n), R(bank, 0, 136 * n))
    part("set")
    iota(R("m0"), [[0, RUN // 16], [256, 16]], 0)
    iota(R("a0"), [[0, RUN // 16], [-256, 16]], 256)
    for name, x, first in (("AK", 0.0, 1e7), ("pv", 0.5, 0.0), ("pw", 0.0, 2.0)):
        fill(R(name), x)
        fill(R(name, 0, None, 16), first)
    asel(R("Ib"), R("one", 0, 128), [[-1, 128]], OP.is_equal, 0)
    for name, x in (("Nb", -1.0), ("H1", 255 / 512), ("H2", 0.5), ("If", 1.0)):
        ts(R(name), R("Ib"), x, OP.mult)
    CC = R("BK", 0, 128, 16)
    for name, x in (("BM", 2 * KEY), ("BV", -KEY), ("BA", KEY)):
        ts(R(name, 0, 8), CC, x, OP.mult)
        ts(R(name, 8, 16), CC, -x, OP.mult)
    cp(R("BV", 16, 32), R("BV", 0, 16))
    ts(H("BC", 0), R("BK"), -KEY, OP.mult)
    ts(H("BC", 1), R("BK"), KEY, OP.mult)
    for n in sorted(set(sum(ON_V.values(), ())) - {0, 16}):
        asel(R("BC%d" % n), R("BC"), [[0, 16], [-1, 16]], OP.is_ge, n - 1, 0)
    iota(R("KR", 0, 512, 1, 1), [[0, 32], [2, 16]], -15)
    iota(R("TG", 0, 128, 1, 1), [[0, 8], [4096, 16]], -65536)
    ts(R("pf", 1, 2), R("pf", 0, 1), 1.0, OP.add)
    ts(R("pf", 3, 4), R("pf", 0, 1), 15.0, OP.is_lt, 256.0, OP.mult)
    off = R("pf", 3, 4)
    ts(R("DB"), R("MI"), -1024.0, OP.mult)
    ts(R("D1"), R("ii"), R("pf", 1, 2), OP.is_equal, 256.0, OP.mult)
    tt(R("DB"), R("DB"), R("D1"), OP.add)
    iota(R("bi"), [[1, 8]], 0)
    cp(R("BL"), R("bi"))
    ts(R("pi", 2, 3), R("pi", 1, 2), 1, OP.arith_shift_right)
    cp(R("pf", 4, 5), R("pi", 2, 3))
    iota(R("wl", 0, 4), [[8, 4]], 0)
    iota(R("wl", 4, 8), [[0, 2], [-16, 2]], 16)
    ts(R("WL", 0, 4), R("wl", 0, 4), R("pf", 4, 5), OP.add)
    ts(R("WL", 4, 8), R("wl", 4, 8), R("pf", 0, 1), OP.add)
    iota(R("ks"), [[16, 16]], S, 0)
    ts(R("ks"), R("ks"), R("pf", 0, 1), OP.add)
    scan(R("thr"), R("pv"), R("pw"), OP.mult, OP.add)
    tt(R("pw", 0, 16), R("thr", 0, 16), R("MI", 0, 16), OP.mult)
    rsum(R("pf", 2, 3), R("pw", 0, 16))
    ts(R("W1"), R("BK"), 64.0, OP.mult)
    ts(R("W2"), R("BK"), R("pf", 2, 3), OP.mult, 0.5, OP.mult)
    ts(R("Sel", 0, 8), R("Ib", 0, 128, 16), 4.0, OP.mult)
    ts(R("Sel", 8, 16), R("Ib", 0, 128, 16), -256.0, OP.mult)
    fill(R("PC", 0, 16), 0.0)
    fill(R("o6"), 1.0)
    two, single = [[-16, 2], [-2, 8], [0, 16]], [[-8, 2], [-1, 8], [0, 16]]
    iota(R("kw"), [[0, 16], [4 * BIG, 16]], -30 * BIG)
    for name, o in (("WY", 0), ("WX", 1)):
        asel(R(name), R("kw"), two, OP.is_equal, -32 * o)
        asel(R(name), R(name), two, OP.not_equal, -32 * o - 1, 1, -float(BIG))
        asel(R(name), R(name), single, OP.not_equal, -64 - 16 * o, 1, 1.0)
    asel(R("WZ"), R("one"), single, OP.is_equal, 0)
    asel(R("WZ"), R("WZ"), single, OP.not_equal, -16, 1, 1.0)
    asel(R("WO"), R("one"), single, OP.is_equal, -32)
    ts(R("cq1", 0, 128, 1, 1), R("KR", 0, 128, 1, 1), -float(BIG), OP.mult)
    tt(R("cq", 0, 128, 1, 1), R("cq1", 0, 128, 1, 1), R("KR", 0, 128, 1, 1), OP.mult)
    iota(R("cc", 0, 128, 1, 1), [[0, 128]], int(MID) + 8192)
    for t in range(RO):
        iota(R("ZR%d" % t, 0, 256), [[0, 256]], 0)
    cp(R("thf", 0, 1, 1, 8), R("thi", 0, 1, 1, 8))
    ts(R("thf", 0, 1, 1, 8), R("thf", 0, 1, 1, 8), KEY, OP.mult, -KEY / 2, OP.add)
    asel(R("B8", 0, 128, 1, 8), R("o6", 0, 128, 1, 8), [[-1, 8], [0, 16]], OP.is_equal, 0)
    ts(R("B8", 0, 128, 1, 8), R("B8", 0, 128, 1, 8), R("thf", 0, 1, 1, 8), OP.mult)
    mm(R("p_MS", 0, 128), R("o6", 0, 128, 1, 8), R("B8", 0, 128, 1, 8))
    cp(R("TH0"), R("p_MS", 0, 128))

    def gather(v, lst, h):
        for a in range(128 * h, 128 * h + 128, CUT[v]):
            part(v[1] + str(a // 64))
            act(R(v, a * 16, (a + CUT[v]) * 16), R("Xw", 0, S), R(lst, a, a + CUT[v]))

    def centre(v, C, h):
        mx, mn = "mx" + v[1], "mn" + v[1]
        for c in range(2 * h, 2 * h + 2):
            part("s%s%d" % (v[1], c))
            for a in range(c * 1024, c * 1024 + 1024, RUN):
                scan(R(mx, a, a + RUN), R("m0"), R(v, a, a + RUN), OP.min, OP.max)
                scan(R(mn, a, a + RUN), R("a0"), R(v, a, a + RUN), OP.max, OP.min)
        out = H("p_MS", h) if v == "vR" else H("p_H%d" % h, 3)
        mm(out, R("H1"), E(mx, 2048 * h, 2048 * h + 2048))
        mm(out, R("H2"), E(mn, 2048 * h, 2048 * h + 2048), False)
        rnd(H(C, h), out, R1)

    def sites(sf, h):
        out = H("p_H%d" % h, 2)
        mm(out, one, R("TG", 0, 128, 1, 1))
        mm(out, H(sf, h), R("Ib"), False)

    banks = [0]

    def sizes(name, v, C, h, b):
        d = "p_D%d" % (banks[0] % 3)
        banks[0] += 1
        for k in range(4):
            mm(H(d, k), R("Ib"), H(C, h))
            mm(H(d, k), R("Nb"), R(v, h * 2048 + 4 * b + k, h * 2048 + 2048, 16), False)
        act(R("m" + name, h * 2048 + b * 512, h * 2048 + b * 512 + 512), R(d), None, AF.Abs)

    def keys(v, h, units):
        kb, w = "p_K%d" % h, 256 * len(units)
        col = lambda k: R(v, h * 2048 + k, h * 2048 + 2048, 16)
        part("d%s%d" % (v[1], h))
        mm(R(kb, 0, w), one, R("KR", 0, w, 1, 1))
        for u, (name, C) in enumerate(units):
            n = ON_V[name][h]
            if n and (name != "NI" or not ON_V["I"][h]):
                mm(H("p_H%d" % h, u), R("Ib"), H(C, h))
            if n:
                mm(R(kb, 256 * u, 256 * u + 256), H(C, h), R("BC" if n == 16 else "BC%d" % n), False)
        for k in range(16):
            us = [u for u, (name, C) in enumerate(units) if k < ON_V[name][h]]
            if us:
                mm(R(kb, 256 * us[0] + k, 256 * us[-1] + 256, 16), col(k), R("BV", 0, 16 * len(us)), False)
        for b in range(4):
            for u, (name, C) in enumerate(units):
                vec = 4 * b < ON_V[name][h]
                if vec:
                    for k in range(4 * b, 4 * b + 4):
                        tt(H("m" + name, 16 * h + k), col(k), H("p_H%d" % h, u), OP.max)
                else:
                    sizes(name, v, C, h, b)
                for k in range(4 * b, 4 * b + 4):
                    mm(R(kb, 256 * u + k, 256 * u + 256, 16), H("m" + name, 16 * h + k), R("BM" if vec else "BA"), False)

    def least(out, kb, x):
        scan(out, R("AK"), H(kb, x), OP.add, OP.min)

    def turned(out, in_, bank, c0, copy):
        mm(R(bank, c0, c0 + 128, 1, in_[4]), in_, R("Ib"))
        copy(R(out, 0, 128, 1, in_[4]), R(bank, c0, c0 + 128, 1, in_[4]))

    for t in range(RO):
        last = t == RO - 1
        now[0] = t
        mu, li, do, zr = "Mu%d" % t, "Lin%d" % t, "Do%d" % t, "ZR%d" % t
        th = "TH" if t else "TH0"
        for h in range(2):
            gather("vR", mu, h)
            centre("vR", "CR", h)
        for h in range(2):
            part("sI%d" % (2 * h))
            ts(H("SF", h), H(li, h), -MID, OP.add)
            sites("SF", h)
        for h in range(2):
            gather("vI", li, h)
            centre("vI", "CI", h)
        for h in range(2):
            kb, hb = "p_K%d" % h, "p_H%d" % h
            keys("vI", h, [("I", "CI")])
            part("oI")
            least(H("FI", h), kb, 1)
            part("pI%d" % h)
            least(H("FI", 2 + h), kb, 0)
            tt(H("NE", h), H(kb, 0), H("FI", 2 + h), OP.not_equal)
            scan(H("RS", h), H("NE", h), H(hb, 2), OP.mult, OP.min)
            c = (8 * h, 8 * h + 8)
            ends = E("RS", 128 * h, 128 * h + 128)
            rnd(R("rS", *c), ends, R4096)
            tt(R("sl", *c), ends, R("rS", *c), OP.subtract)
            tt(H("ex", h), R("sl", *c), R("MI"), OP.mult, R("BL"))
            mm(R(hb, 384, 392), H("ex", h), CC)
            ts(R("sU", *c), R(hb, 384, 392), MID, OP.add)
            cp(H("nU", h), R("NBw"), R("sU", *c))
            gather("vN", "nU", h)
            part("b%d" % h)
            act(H("bG", h), R("OWw", 0, S), R("sU", *c))
            ts(H("SN", h), H("nU", h), -MID, OP.add)
            sites("SN", h)
            scan(H("bs", h), R("DB"), H("bG", h), OP.add, OP.max)
            ts(R("bU", *c), E("bs", 128 * h, 128 * h + 128), off, OP.subtract)
            part("c%d" % h)
            act(H("CB", h), R("CR"), R("bU", *c))
        part("oI")
        rnd(R("rI"), E("FI"), RKEY)
        tt(R("ZK", 0, 64, 2), E("FI"), R("rI"), OP.subtract)
        tt(R("ZK", 1, 64, 2), R("ZK", 0, 64, 2), R("ZK", 0, 64, 2), OP.mult)
        part("EQ")
        ts(R("bL"), E("bs"), off, OP.subtract)
        offs = [sum(256 - 16 * x for x in range(c)) for c in range(16)]
        for c in range(16):
            ts(R("EQ", offs[c], offs[c] + 256 - 16 * c), R("bG", 16 * c, 256), R("bL", c, c + 1), OP.is_equal)
        for c in range(16):
            mm(R("p_MS", 16 * c, 16 * c + 16), R("W2"), R("EQ", offs[c], offs[c] + 16), c == 0)
            if c < 15:
                mm(R("p_MS", 16 * c + 16, 256), R("W1"), R("EQ", offs[c] + 16, offs[c] + 256 - 16 * c), c == 0)
        for h in range(2):
            tt(H("nfG", h), H("p_MS", h), R("thr"), OP.is_ge)
        for x in range(2):
            for h in range(2):
                mm(R("p_MS", 256 + 16 * x + 8 * h, 264 + 16 * x + 8 * h), H("nfG", h), R("Sel", 0, 8))
        for h in range(2):
            mm(R("p_MS", 288 + 8 * h, 296 + 8 * h), H("bG", h), R("Sel", 8, 16))
        tt(R("ZK", 1, 64, 2), R("ZK", 1, 64, 2), R("p_MS", 256, 288), OP.add)
        ts(R("dl"), R("p_MS", 288, 304), 65025.0, OP.add, 1.0, OP.min)
        part("lists")
        for h in range(2):
            scan(H("fs", h), R("DB"), H("nfG", h), OP.add, OP.max)
        cp(R("sF"), R("sU"))
        ts(R("f1"), E("fs"), off, OP.subtract)
        tt(R("f1"), R("f1"), R("ks"), OP.mult)
        tt(R("sb", 0, 16), R("f1"), R("sF"), OP.max)
        tt(R("sb", 16, 32), R("f1"), R("bL"), OP.max)
        cp(R("WU"), R("sb"))
        if not last:
            part("vT")
            act(R("vT"), R("Xw", 0, S), R("sU"), AF.Relu, -8.0)
        for h in range(2):
            kb, hb = "p_K%d" % h, "p_H%d" % h
            keys("vN", h, [("NI", "CI"), ("NR", "CB")])
            part("pN%d" % h)
            slots = [2 * s + h for s in (1, 3, 2, 0)]
            for x in range(4):
                least(H("FN", slots[x]), kb, x)
            tt(H("fI", h), H(kb, 0), R(th), OP.is_lt)
            tt(H("fR", h), H(kb, 2), R(th), OP.is_lt)
            for x in range(4):
                tt(H("NE", slots[x]), H(kb, x), H("FN", slots[x]), OP.not_equal)
            for x in range(4):
                scan(H("NS", slots[x]), H("NE", slots[x]), H(hb, 2), OP.mult, OP.min)
        if not last:
            part("X")
            scat(R("Xw"), R("WU", 0, 16), R("vT"))
        part("fin")
        scan(R("PC", 16, 272), R("fI"), R("fR"), OP.add, OP.subtract)
        tt(R("won", 0, 16), E("PC", 16), E("PC", 0, 256), OP.is_gt)
        tt(R("won", 16, 32), E("PC", 16), E("PC", 0, 256), OP.is_le)
        rnd(R("rN"), E("NS"), R4096)
        tt(R("ZK", 64, 128), E("NS"), R("rN"), OP.subtract)
        tt(R(do, 0, 128), R("won"), R("ZK"), OP.mult, R("WL"))
        send(R(do, 0, 96), R("Din%d" % t), -1 - t, "aD%d" % t, "lD%d" % t)
        if not last:
            part("w")
            tt(R("wf"), R("won", 0, 16), R("p_MS", 256, 272), OP.is_gt)
        part("loc")
        tt(R(do, 128, 144), R("won", 0, 16), R("dl"), OP.mult)
        turned("TP", R(do, 96, 144), "p_H0", 0, cp)
        for h in range(2):
            mm(H("p_H1", h), H("WZ", h, 32), R("TP", 0, 128, 1, 32))
        act(R("zG"), R("p_H1", 0, 256), None, AF.Identity, MID + 4096)
        scat(R(zr), R("WU", 16, 32), R("zG"))
        part("own")
        for h in range(2):
            mm(H("p_H0", 2 + h), R("Ib"), H("bG", h))
            mm(H("p_H0", 2 + h), H("WO", h, 48), R("TP", 0, 128, 1, 48), False)
        act(R("ow"), R("p_H0", 256, 512))
        scat(R("OWw"), R("WU", 0, 16), R("ow"))
        if last:
            dma("dyo", T.yown[:, :], T.c_OWw[0::16, 0:S], [R("OWw", 0, S)], [], LOAD + 1.5, "G")
        for h in range(2):
            part("dR%d" % h)
            kb, n = "p_K%d" % h, ON_V["R"][h] if last else 0
            mm(H(kb, 0), one, R("KR", 0, 128, 1, 1))
            if n:
                mm(H("p_MS", 2 + h), R("Ib"), H("CR", h))
                mm(H(kb, 0), H("CR", h), H("BC%d" % n, 1), False)
            for k in range(16):
                col = R("vR", h * 2048 + k, h * 2048 + 2048, 16)
                if k < n:
                    mm(R(kb, k, 128, 16), col, R("BV", 8, 16), False)
                    tt(H("mR", 16 * h + k), col, H("p_MS", 2 + h), OP.max)
                elif k % 4 == 0:
                    sizes("R", "vR", "CR", h, k // 4)
                mm(R(kb, k, 128, 16), H("mR", 16 * h + k), R("BM" if k < n else "BA", 8, 16), False)
            least(H("FR", h), kb, 0)
        part("pR")
        rnd(R("rR"), E("FR"), RKEY)
        tt(R("KK", 0, 32, 2), E("FR"), R("rR"), OP.subtract)
        tt(R("KK", 1, 32, 2), R("KK", 0, 32, 2), R("KK", 0, 32, 2), OP.mult)
        turned("TR", R("KK"), "p_MS", 0, act)
        mm(R("p_MS", 256, 512), R("cq", 0, 128, 1, 1), row)
        mm(R("p_MS", 256, 512), R("If"), R(zr, 0, 256), False)
        for h in range(2):
            mm(H("p_MS", 2 + h), H("WY", h, 32), R("TR", 0, 128, 1, 32), False)
        tt(R("x1"), R("Mi"), R("p_MS", 256, 512), OP.max)
        part("back")
        turned("TY", R("Din%d" % t), "p_K0", 256, cp)
        mm(R("p_K0", 0, 256), R("cq", 0, 128, 1, 1), row)
        mm(R("p_K0", 0, 256), R("cc", 0, 128, 1, 1), row, False)
        for h in range(2):
            for w in ("WY", "WX"):
                mm(H("p_K0", h), H(w, h, 96), R("TY", 0, 128, 1, 96), False)
        for h in range(2):
            tt(H("Tm", h), H("x1", h), H("p_K0", h), OP.max)
            ts(H("Mi", h), H("Tm", h), 4095, OP.bitwise_and)
            if last:
                cp(H("Mo", h), H("Mi", h))
                dma("dy%d" % h, T.ym[:, 128 * h:128 * h + 128], H("Mo", h)[0], [H("Mo", h)], [], LOAD, "YS"[h])
            else:
                cp(H("Mu%d" % (t + 1), h), H("Mi", h))
                send(H("Mu%d" % (t + 1), h), H("Lin%d" % (t + 1), h), 2 + t, "aL%d%d" % (h, t + 1), "lL%d%d" % (h, t + 1), HOP - 0.3)
        if not last:
            part("w")
            mm(R("p_K1", 0, 16), R("one", 0, 128), R("wf"))
            rsum(R("w16", 8, 9), R("p_K1", 0, 16))
            cp(R("wI", 0, 1), R("w16", 8, 9))
            ts(R("wI", 8, 9), R("wI", 0, 1), 63, OP.bitwise_and)
            ts(R("w16", 0, 1), R("wI", 8, 9), KEY, OP.mult)
            ts(R("TH"), R("TH0"), R("w16", 0, 1), OP.add)

    op("X", None, [], [], 0.0, ("dy0", 16), 0.0, [i for i, o in enumerate(ops) if o["sem"]])
    n = len(ops)
    seq = sorted((o["part"][0], SCALAR.split().index(o["part"][1]), i) for i, o in enumerate(ops)
                 if o["q"] == "S" and o["part"][1] in SCALAR.split())
    for a, i in zip(seq, seq[1:]):
        ops[i[2]]["dep"].setdefault(a[2], False)
    before = [{a: ops[a]["late"] + ((OWN if ops[a]["q"] == o["q"] else SYNC.get(ops[a]["q"], 0.1)) if s else 0.0)
               for a, s in o["dep"].items()} for o in ops]
    for i, o in enumerate(ops):
        if "first" in o:
            before[i][o["first"]] = 0.0
    behind = [{} for _ in range(n)]
    for i in range(n):
        for a, x in before[i].items():
            behind[a][i] = x

    def lay(first, then, rank_):
        left = [len(x) for x in first]
        can, end = [0.0] * n, [0.0] * n
        busy = {q: [] for q in "VSPGYX"}
        ready = [i for i in range(n) if not left[i]]
        while ready:
            i = min(ready, key=lambda j: rank_[j])
            ready.remove(i)
            lst, st, us = busy[ops[i]["q"]], can[i], ops[i]["us"]
            k = len(lst)
            while k and lst[k - 1][1] > st:
                k -= 1
            while k < len(lst) and lst[k][0] < st + us - 1e-9:
                st = max(st, lst[k][1])
                k += 1
            lst.insert(k, (st, st + us))
            end[i] = st + us
            for j, x in then[i].items():
                can[j] = max(can[j], end[i] + x)
                left[j] -= 1
                if not left[j]:
                    ready.append(j)
        return end

    if not ORDER:
        plan = PLAN.split()
        end = lay(before, behind, [(o["part"][0], plan.index(o["part"][1]), i) for i, o in enumerate(ops)])
        end = lay(before, behind, [-x for x in lay(behind, before, [-x for x in end])])
        ORDER.extend(sorted(range(n), key=lambda i: (end[i] - ops[i]["us"], end[i], i)))

    done = {}
    count = {q: 0 for q in "VSPG"}
    known = {q: {} for q in "VSPGYX"}
    snap, total = {}, {}
    for i in ORDER:
        o = ops[i]
        q = o["q"]
        if q != "X":
            nd = {}
            for a, s in o["dep"].items():
                if s and done[a][1] > nd.get(done[a][0], (0, 0))[0]:
                    nd[done[a][0]] = (done[a][1], a)
            for s in sorted(nd, key=lambda s: -nd[s][1]):
                if known[q].get(s, 0) < nd[s][0]:
                    Q[q].wait_ge(T.sem[s], nd[s][0])
                    known[q][s] = nd[s][0]
                    for s2, n2 in snap[nd[s][1]].items():
                        known[q][s2] = max(known[q].get(s2, 0), n2)
            inst = o["fn"]()
        snap[i] = dict(known[q]) if q != "X" else {}
        if o["sem"] is None:
            count[q] += 1
            inst.then_inc(T.sem["q" + q], 1)
            done[i] = ("q" + q, count[q])
        else:
            done[i] = o["sem"]
        total[done[i][0]] = done[i][1]
    for s in sorted(total):
        if known["G"].get(s, 0) < total[s]:
            g.wait_ge(T.sem[s], total[s])
